import numpy as np
import ml_dtypes


def mxq(x, axis, fmt="e4m3"):
    dtype, down = {"e4m3": (ml_dtypes.float8_e4m3fn, 7), "e5m2": (ml_dtypes.float8_e5m2, 14)}[fmt]
    v = np.moveaxis(np.asarray(x, np.float32).astype(ml_dtypes.bfloat16).astype(np.float64), axis, -1)
    blocks = v.reshape(v.shape[:-1] + (-1, 32))
    amax = np.abs(blocks).max(-1, keepdims=True)
    byte = np.maximum(np.where(amax > 0, np.frexp(amax)[1] - 1 + 127, 0) - down, 1)
    scale = np.exp2(byte - 127.0)
    codes = (blocks / scale).astype(np.float32).astype(dtype).astype(np.float64)
    return np.moveaxis((codes * scale).reshape(v.shape), -1, axis)


WIDE = False


def mx_kscale(k):
    if not WIDE:
        return np.ones(k)
    levels = np.array([10, -10, 5, -5, 0])
    if k % 512:
        return np.exp2(np.random.permutation(np.resize(levels, k // 32))).repeat(32)
    a = np.empty((k // 512, 16))
    for p in range(k // 512):
        a[p, :8] = np.random.permutation(np.resize(levels, 8))
        for g in range(8):
            far = levels[np.abs(levels - a[p, g]) >= 10]
            a[p, g + 8] = far[np.random.randint(len(far))]
    return np.exp2(a.ravel()).repeat(32)


def f64(x):
    return np.asarray(x).astype(np.float64)


def striped(idx):
    return np.tile(idx.reshape(-1, 16).T, (8, 1)).astype(np.uint16)


def unstriped(offs):
    return offs[:16].T.reshape(-1).astype(np.int64)


E2M1 = np.array([0.0, 0.5, 1.0, 1.5, 2.0, 3.0, 4.0, 6.0, -0.0, -0.5, -1.0, -1.5, -2.0, -3.0, -4.0, -6.0])


def pack_weight(w, fmt):
    k, n = w.shape
    w = f64(np.asarray(w, np.float32).astype(ml_dtypes.bfloat16)).reshape(k // 32, 32, n)
    amax = np.abs(w).max(1)
    if fmt == "e4m3":
        byte = np.frexp(amax)[1] - 1 + 127 - 7
    else:
        mant, ex = np.frexp(amax / 6.0)
        byte = np.where(mant > 0.5, ex, ex - 1) + 127
    byte = np.clip(np.where(amax > 0, byte, 1), 1, 254)
    scaled = (w * np.exp2(127.0 - byte)[:, None, :]).reshape(k, n).astype(np.float32)
    by_word = np.ascontiguousarray(scaled.reshape(k // 512, 128, 4, n).transpose(0, 1, 3, 2))
    if fmt == "e4m3":
        words = by_word.astype(ml_dtypes.float8_e4m3fn).view(np.uint8)
    else:
        c = by_word.astype(ml_dtypes.float4_e2m1fn).view(np.uint8) & 0xF
        words = (c[..., 0::2] | (c[..., 1::2] << 4)).reshape(k // 512, 128, 2 * n)
    return np.ascontiguousarray(words), np.ascontiguousarray(byte.astype(np.uint8).reshape(k // 512, 16, n))


def unpack_weight(words, scales, fmt):
    g, _, n = scales.shape
    words = np.ascontiguousarray(words).reshape(g, 128, n, -1)
    if fmt == "e4m3":
        vals = words.view(ml_dtypes.float8_e4m3fn).astype(np.float64)
    else:
        nib = np.empty((g, 128, n, 4), np.uint8)
        nib[..., 0::2] = words & 0xF
        nib[..., 1::2] = words >> 4
        vals = E2M1[nib]
    vals = vals * np.repeat(np.exp2(scales.astype(np.float64) - 127.0), 8, axis=1)[..., None]
    return vals.transpose(0, 1, 3, 2).reshape(g * 512, n)


def gelu(v):
    return 0.5 * v * (1.0 + np.tanh(np.sqrt(2.0 / np.pi) * (v + 0.044715 * v**3)))


K, H, N, T, S, T2 = 1024, 512, 384, 2048, 1024, 2048

def setup_inputs():
    n = np.random.standard_normal
    s = mx_kscale(K)[:, None]
    u = mx_kscale(H)[:, None]
    tab_words, tab_scales = pack_weight(n((K, T)) * s, "e4m3")
    wm_words, wm_scales = pack_weight(n((K, H)) / np.sqrt(K) * u.T / s, "e2m1")
    wg_words, wg_scales = pack_weight(n((H, H)) / np.sqrt(H) / u, "e4m3")
    return {
        "tab_words": tab_words, "tab_scales": tab_scales,
        "offs": striped(np.random.permutation(T)[:S]),
        "xT": (np.round(16 * n((K, T2))) / 16 * s).astype(np.float32),
        "offs2": striped(np.random.permutation(T2)[:S]),
        "offs3": striped(np.random.permutation(T2)[:S]),
        "wm_words": wm_words, "wm_scales": wm_scales,
        "wp": (n((K, H)) / np.sqrt(2 * K) * u.T / s).astype(np.float32),
        "wg_words": wg_words, "wg_scales": wg_scales,
        "wo": (n((H, N)) / np.sqrt(H) / u).astype(np.float32),
    }

def reference(tab_words, tab_scales, offs, xT, offs2, offs3, wm_words, wm_scales, wp, wg_words, wg_scales, wo):
    v = unpack_weight(tab_words, tab_scales, "e4m3")[:, unstriped(offs)]
    wm = unpack_weight(wm_words, wm_scales, "e2m1")
    wg = unpack_weight(wg_words, wg_scales, "e4m3")
    x = f64(xT)[:, unstriped(offs2)] + f64(xT)[:, unstriped(offs3)]
    a = wm.T @ v
    b = mxq(f64(wp), 0, "e4m3").T @ mxq(x, 0, "e4m3")
    h = a + b
    gate = 1.0 / (1.0 + np.exp(-(wg.T @ mxq(h, 0, "e4m3"))))
    z = b + gate * (a - b)
    return mxq(f64(wo), 0, "e4m3").T @ mxq(z, 0, "e4m3")

@@ -1,0 +1,306 @@
+from contextlib import ExitStack
+
+import concourse.mybir as mybir
+from concourse.masks import make_identity
+
+K, H, N, T, S = 1024, 512, 384, 2048, 1024
+FLOPS = 2 * S * (2 * K * H + H * H + H * N)
+
+F32 = mybir.dt.float32
+BF16 = mybir.dt.bfloat16
+I32 = mybir.dt.int32
+U32 = mybir.dt.uint32
+U16 = mybir.dt.uint16
+U8 = mybir.dt.uint8
+FP8X4 = mybir.dt.float8_e4m3fn_x4
+FP4X4 = mybir.dt.float4_e2m1fn_x4
+ADD = mybir.AluOpType.add
+SUB = mybir.AluOpType.subtract
+MULT = mybir.AluOpType.mult
+SIGMOID = mybir.ActivationFunctionType.Sigmoid
+
+P = 128
+PACK = 4
+K_PASS = P * PACK
+BLOCK = 128
+CHUNK = 256
+CHUNKS = S // CHUNK
+HALF = 512
+
+
+def entries(offsets, first, count):
+    return offsets[:, first // 16 : (first + count) // 16]
+
+
+def tile_list_pivot_irrigation_kernel(
+    tc, tab_words, tab_scales, offs, xT, offs2, offs3, wm_words, wm_scales, wp, wg_words, wg_scales, wo, out
+):
+    nc = tc.nc
+    with ExitStack() as ctx:
+        keep = ctx.enter_context(tc.tile_pool(name="keep", bufs=1))
+        two = ctx.enter_context(tc.tile_pool(name="two", bufs=2))
+        four = ctx.enter_context(tc.tile_pool(name="four", bufs=4))
+        psum1 = ctx.enter_context(tc.psum_pool(name="psum1", bufs=1))
+        psum2 = ctx.enter_context(tc.psum_pool(name="psum2", bufs=2))
+
+        def interleave(copy, dst, src):
+            copy(
+                out=dst.rearrange("p (c i t) -> p c t i", i=4, t=PACK),
+                in_=src.rearrange("p t (c i) -> p c t i", i=4),
+            )
+
+        def quantize(name, src, words, tag=None):
+            codes = keep.tile([P, words], U32, name=name + "_codes", tag=tag or name + "_codes", align_bytes=64)
+            scales = keep.tile([P, words], U8, name=name + "_scales", align_bytes=64)
+            nc.vector.quantize_mx(out=codes[:].bitcast(FP8X4), scales=scales[:], in_=src)
+            return codes, scales
+
+        def load_plane(a, i):
+            slot = (PACK * a + i) % 6
+            plane = keep.tile([P, T], F32, name="plane%d%d" % (a, i), tag="plane%d" % slot)
+            rows = xT[a * K_PASS : (a + 1) * K_PASS, :].rearrange("(p i) t -> p i t", i=PACK)
+            nc.sync.dma_start(out=plane[:], in_=rows[:, i, :])
+            return plane
+
+        def load_rows(name, rows):
+            raw = keep.tile([P, PACK, rows.shape[1]], F32, name=name + "_raw")
+            nc.sync.dma_start(out=raw[:], in_=rows.rearrange("(p j) c -> p j c", j=PACK))
+            return raw
+
+        tab_sc = keep.tile([P, T], U8, align_bytes=64)
+        nc.vector.memset(tab_sc[:].bitcast(I32), 0)
+        for q in range(4):
+            nc.scalar.dma_start(
+                out=tab_sc[32 * q : 32 * q + 8, :].bitcast(I32),
+                in_=tab_scales[:, 4 * q : 4 * q + 4, :].bitcast(I32),
+            )
+        wm_sc = keep.tile([P, 2 * H], U8, align_bytes=64)
+        wg_sc = keep.tile([P, H], U8, align_bytes=64)
+        v_sc1 = keep.tile([P, S], U8, align_bytes=64)
+        for t_ in (wm_sc, wg_sc, v_sc1):
+            nc.vector.memset(t_[:].bitcast(I32), 0)
+        ident = keep.tile([P, P], F32)
+        make_identity(nc, ident[:])
+
+        list1 = keep.tile([P, S // 16], U16)
+        list2 = keep.tile([P, S // 16], U16)
+        list3 = keep.tile([P, S // 16], U16)
+        nc.sync.dma_start(list1[:], offs)
+        planes = {(0, 0): load_plane(0, 0)}
+        nc.sync.dma_start(list2[:], offs2)
+        nc.sync.dma_start(list3[:], offs3)
+
+        v_sc0 = keep.tile([P, S], U8, align_bytes=64)
+        nc.vector.tensor_copy(out=v_sc0[:], in_=tab_sc[:].indirect(list1[:]))
+
+        x0 = keep.tile([P, PACK, S], F32)
+
+        def gather_pass0(i):
+            picks = []
+            for h in range(S // HALF):
+                pick = keep.tile([P, HALF], F32, name="pick0_%d%d" % (i, h), tag="pick0_%d" % h, align_bytes=64)
+                nc.vector.tensor_copy(out=pick[:], in_=planes[0, i][:].indirect(entries(list2, h * HALF, HALF)))
+                picks.append(pick)
+            for h in range(S // HALF):
+                nc.vector.tensor_tensor(
+                    out=x0[:, i, h * HALF : (h + 1) * HALF],
+                    in0=planes[0, i][:].indirect(entries(list3, h * HALF, HALF)),
+                    in1=picks[h][:],
+                    op=ADD,
+                )
+
+        gather_pass0(0)
+
+        v_codes = []
+        for a in range(2):
+            tab = keep.tile([P, T], U32, name="tab%d" % a)
+            nc.sync.dma_start(out=tab[:].bitcast(I32), in_=tab_words[a].rearrange("p t i -> p (t i)").bitcast(I32))
+            picked = keep.tile([P, S], U32, name="v_codes%d" % a, align_bytes=64)
+            nc.vector.tensor_copy(out=picked[:], in_=tab[:].indirect(list1[:]))
+            v_codes.append(picked)
+        v_scales = [v_sc0, v_sc1]
+        nc.sync.dma_start(out=v_sc1[0 : P - 4, :].bitcast(I32), in_=v_sc0[4:P, :].bitcast(I32))
+
+        wm = keep.tile([P, 2, 2 * H], U8, align_bytes=64)
+        nc.sync.dma_start(out=wm[:].bitcast(I32), in_=wm_words.bitcast(I32).rearrange("a p n -> p a n"))
+        for q in range(4):
+            nc.sync.dma_start(
+                out=wm_sc[32 * q : 32 * q + 4, :].bitcast(I32).rearrange("r (a n) -> r a n", a=2),
+                in_=wm_scales[:, 4 * q : 4 * q + 4, :].bitcast(I32).rearrange("a r n -> r a n"),
+            )
+
+        a_sb = []
+        for blk in range(S // BLOCK):
+            cols = slice(blk * BLOCK, (blk + 1) * BLOCK)
+            bank = psum2.tile([P, H], F32, name="ab_bank")
+            for a in range(2):
+                nc.tensor.matmul_mx(
+                    out=bank[:],
+                    lhsT=v_codes[a][:, cols].bitcast(FP8X4),
+                    lhsT_scale=v_scales[a][:, cols],
+                    rhs=wm[:, a, :].bitcast(FP4X4),
+                    rhs_scale=wm_sc[:, a * H : (a + 1) * H],
+                    start=(a == 0),
+                    stop=(a == 1),
+                )
+            a_blk = keep.tile([P, PACK, P], F32, name="a_sb%d" % blk)
+            nc.scalar.copy(out=a_blk[:], in_=bank[:].rearrange("p (m t) -> p t m", t=PACK))
+            a_sb.append(a_blk)
+
+        def round_weight(name, rows):
+            raw = load_rows(name, rows)
+            width = rows.shape[1]
+            grouped = keep.tile([P, PACK * width], BF16, name=name + "_bf", align_bytes=64)
+            interleave(nc.scalar.copy, grouped[:], raw[:])
+            return grouped
+
+        wp_bf = []
+        for i in (1, 2):
+            planes[0, i] = load_plane(0, i)
+            gather_pass0(i)
+            wp_bf.append(round_weight("wp%d" % (i - 1), wp[(i - 1) * K_PASS : i * K_PASS, :]))
+        wo_bf = round_weight("wo", wo)
+        planes[0, 3] = load_plane(0, 3)
+        gather_pass0(3)
+        wp_q = [quantize("wp%d" % a, wp_bf[a][:], H, "pick0_%d" % a) for a in range(2)]
+        wo_q = [quantize("wo%d" % n, wo_bf[:, n * K_PASS : (n + 1) * K_PASS], P) for n in range(N // P)]
+        for i in range(PACK):
+            planes[1, i] = load_plane(1, i)
+        wg = keep.tile([P, H], U32, align_bytes=64)
+        nc.sync.dma_start(out=wg[:].bitcast(I32), in_=wg_words[0].rearrange("p c i -> p (c i)").bitcast(I32))
+        for q in range(4):
+            nc.sync.dma_start(
+                out=wg_sc[32 * q : 32 * q + 4, :].bitcast(I32),
+                in_=wg_scales[0, 4 * q : 4 * q + 4, :].bitcast(I32),
+            )
+
+        x0_bf, x0_q = [], {}
+        for c in range(CHUNKS):
+            grouped = keep.tile([P, PACK * CHUNK], BF16, name="x0_bf%d" % c, align_bytes=64)
+            interleave(nc.scalar.copy, grouped[:], x0[:, :, c * CHUNK : (c + 1) * CHUNK])
+            x0_bf.append(grouped)
+
+        x1, b_sb, diff, gate, term = {}, {}, {}, {}, {}
+
+        def mover(blk):
+            return nc.vector.tensor_copy if blk == S // BLOCK - 1 else nc.scalar.copy
+
+        def gather_pair(c, first, tags):
+            if first == 0:
+                x1[c] = two.tile([P, PACK, CHUNK], F32, name="x1")
+            picks = []
+            for n in range(2):
+                pick = keep.tile([P, CHUNK], F32, name="pick%d%d" % (c, first + n), tag=tags[n], align_bytes=64)
+                nc.vector.tensor_copy(out=pick[:], in_=planes[1, first + n][:].indirect(entries(list2, c * CHUNK, CHUNK)))
+                picks.append(pick)
+            for n in range(2):
+                nc.vector.tensor_tensor(
+                    out=x1[c][:, first + n, :],
+                    in0=planes[1, first + n][:].indirect(entries(list3, c * CHUNK, CHUNK)),
+                    in1=picks[n][:],
+                    op=ADD,
+                )
+
+        def transposed_sum(name, blk, early, late, grouped):
+            bank = psum2.tile([P, PACK, BLOCK], F32, name=name + "_bank")
+            for n, part in enumerate((early, late)):
+                for t in range(PACK):
+                    nc.tensor.matmul(
+                        out=bank[:, t, :],
+                        lhsT=part[:, t, :],
+                        rhs=ident[:],
+                        is_transpose=True,
+                        start=(n == 0 and t == 0),
+                        stop=(n == 1 and t == PACK - 1),
+                    )
+            mover(blk)(out=grouped[:], in_=bank[:].rearrange("p t j -> p j t"))
+            return grouped[:].rearrange("p j t -> p (j t)")
+
+        def project_probes(blk):
+            c, n = divmod(blk, 2)
+            cols = slice(n * BLOCK, (n + 1) * BLOCK)
+            grouped = keep.tile([P, PACK * BLOCK], BF16, name="x1_bf%d" % blk, tag="x_slot%d" % (blk % 4), align_bytes=64)
+            interleave(mover(blk), grouped[:], x1[c][:, :, cols])
+            x1_q = quantize("x1_%d" % blk, grouped[:], BLOCK)
+            bank = psum2.tile([P, H], F32, name="ab_bank")
+            operands = ((x0_q[c][0][:, cols], x0_q[c][1][:, cols]), (x1_q[0][:], x1_q[1][:]))
+            for a in range(2):
+                nc.tensor.matmul_mx(
+                    out=bank[:],
+                    lhsT=operands[a][0].bitcast(FP8X4),
+                    lhsT_scale=operands[a][1],
+                    rhs=wp_q[a][0][:].bitcast(FP8X4),
+                    rhs_scale=wp_q[a][1][:],
+                    start=(a == 0),
+                    stop=(a == 1),
+                )
+            b_sb[blk] = four.tile([P, PACK, P], F32, name="b_sb")
+            mover(blk)(out=b_sb[blk][:], in_=bank[:].rearrange("p (m t) -> p t m", t=PACK))
+
+        def make_gate(blk):
+            grouped = keep.tile([P, BLOCK, PACK], BF16, name="h_bf%d" % blk, tag="h_slot%d" % (blk % 4), align_bytes=64)
+            h_q = quantize("h_%d" % blk, transposed_sum("h", blk, a_sb[blk], b_sb[blk], grouped), BLOCK)
+            bank = psum1.tile([P, H], F32, name="gate_bank")
+            nc.tensor.matmul_mx(
+                out=bank[:],
+                lhsT=h_q[0][:].bitcast(FP8X4),
+                lhsT_scale=h_q[1][:],
+                rhs=wg[:].bitcast(FP8X4),
+                rhs_scale=wg_sc[:],
+                start=True,
+                stop=True,
+            )
+            gate[blk] = four.tile([P, PACK, P], F32, name="gate")
+            nc.scalar.activation(out=gate[blk][:], in_=bank[:].rearrange("p (m t) -> p t m", t=PACK), func=SIGMOID)
+
+        def difference(blk):
+            diff[blk] = keep.tile([P, PACK, P], F32, name="diff%d" % blk, tag="x_slot%d" % (blk % 4), align_bytes=64)
+            nc.vector.tensor_tensor(out=diff[blk][:], in0=a_sb[blk][:], in1=b_sb[blk][:], op=SUB)
+
+        def interpolate(blk):
+            term[blk] = keep.tile([P, PACK, P], F32, name="term%d" % blk, tag="h_slot%d" % (blk % 4), align_bytes=64)
+            nc.vector.tensor_tensor(out=term[blk][:], in0=gate[blk][:], in1=diff[blk][:], op=MULT)
+
+        def finish(blk):
+            grouped = two.tile([P, BLOCK, PACK], BF16, name="z_bf", align_bytes=64)
+            z_q = quantize("z_%d" % blk, transposed_sum("z", blk, b_sb[blk], term[blk], grouped), BLOCK)
+            bank = psum1.tile([P, N // P, BLOCK], F32, name="out_bank")
+            for n in range(N // P):
+                nc.tensor.matmul_mx(
+                    out=bank[:, n, :],
+                    lhsT=wo_q[n][0][:].bitcast(FP8X4),
+                    lhsT_scale=wo_q[n][1][:],
+                    rhs=z_q[0][:].bitcast(FP8X4),
+                    rhs_scale=z_q[1][:],
+                    start=True,
+                    stop=True,
+                )
+            staged = two.tile([P, N // P, BLOCK], F32, name="staged")
+            mover(blk)(out=staged[:], in_=bank[:])
+            nc.sync.dma_start(
+                out=out.rearrange("(n p) j -> p n j", p=P)[:, :, blk * BLOCK : (blk + 1) * BLOCK], in_=staged[:]
+            )
+
+        def both(step, c):
+            for n in range(2):
+                step(2 * c + n)
+
+        def slots(kind, c):
+            return ["%s_slot%d" % (kind, (2 * c + n) % 4) for n in range(2)]
+
+        for first in (0, 2):
+            gather_pair(0, first, ["first%d" % first, "first%d" % (first + 1)])
+            for n in (first, first + 1):
+                x0_q[n] = quantize("x0_%d" % n, x0_bf[n][:], CHUNK, "first%d" % n)
+        for c in range(CHUNKS):
+            both(project_probes, c)
+            if c + 1 < CHUNKS:
+                gather_pair(c + 1, 0, slots("x", c))
+            if c >= 1:
+                both(finish, c - 1)
+            both(make_gate, c)
+            both(difference, c)
+            if c + 1 < CHUNKS:
+                gather_pair(c + 1, 2, slots("h", c))
+            both(interpolate, c)
+        both(finish, CHUNKS - 1)

@@ -49,9 +49,9 @@ def tile_list_pivot_irrigation_kernel(
                 in_=src.rearrange("p t (c i) -> p c t i", i=4),
             )
 
-        def quantize(name, src, words, tag=None):
-            codes = keep.tile([P, words], U32, name=name + "_codes", tag=tag or name + "_codes", align_bytes=64)
-            scales = keep.tile([P, words], U8, name=name + "_scales", align_bytes=64)
+        def quantize(pool, name, src, words, tag=None):
+            codes = pool.tile([P, words], U32, name=name + "_codes", tag=tag or name + "_codes", align_bytes=64)
+            scales = pool.tile([P, words], U8, name=name + "_scales", align_bytes=64)
             nc.vector.quantize_mx(out=codes[:].bitcast(FP8X4), scales=scales[:], in_=src)
             return codes, scales
 
@@ -96,20 +96,22 @@ def tile_list_pivot_irrigation_kernel(
         x0 = keep.tile([P, PACK, S], F32)
 
         def gather_pass0(i):
-            picks = []
             for h in range(S // HALF):
+                total = x0[:, i, h * HALF : (h + 1) * HALF]
                 pick = keep.tile([P, HALF], F32, name="pick0_%d%d" % (i, h), tag="pick0_%d" % h, align_bytes=64)
-                nc.vector.tensor_copy(out=pick[:], in_=planes[0, i][:].indirect(entries(list2, h * HALF, HALF)))
-                picks.append(pick)
-            for h in range(S // HALF):
-                nc.vector.tensor_tensor(
-                    out=x0[:, i, h * HALF : (h + 1) * HALF],
-                    in0=planes[0, i][:].indirect(entries(list3, h * HALF, HALF)),
-                    in1=picks[h][:],
-                    op=ADD,
-                )
+                nc.vector.tensor_copy(out=total, in_=planes[0, i][:].indirect(entries(list2, h * HALF, HALF)))
+                nc.vector.tensor_copy(out=pick[:], in_=planes[0, i][:].indirect(entries(list3, h * HALF, HALF)))
+                nc.gpsimd.tensor_tensor(out=total, in0=total, in1=pick[:], op=ADD)
+
+        def round_weight(name, rows):
+            raw = load_rows(name, rows)
+            width = rows.shape[1]
+            grouped = keep.tile([P, PACK * width], BF16, name=name + "_bf", align_bytes=64)
+            interleave(nc.scalar.copy, grouped[:], raw[:])
+            return grouped
 
         gather_pass0(0)
+        wo_bf = round_weight("wo", wo)
 
         v_codes = []
         for a in range(2):
@@ -143,27 +145,18 @@ def tile_list_pivot_irrigation_kernel(
                     start=(a == 0),
                     stop=(a == 1),
                 )
-            a_blk = keep.tile([P, PACK, P], F32, name="a_sb%d" % blk)
+            a_blk = keep.tile([P, PACK, P], F32, name="a_sb%d" % blk, tag="a_slot%d" % blk, align_bytes=64)
             nc.scalar.copy(out=a_blk[:], in_=bank[:].rearrange("p (m t) -> p t m", t=PACK))
             a_sb.append(a_blk)
-
-        def round_weight(name, rows):
-            raw = load_rows(name, rows)
-            width = rows.shape[1]
-            grouped = keep.tile([P, PACK * width], BF16, name=name + "_bf", align_bytes=64)
-            interleave(nc.scalar.copy, grouped[:], raw[:])
-            return grouped
 
         wp_bf = []
         for i in (1, 2):
             planes[0, i] = load_plane(0, i)
             gather_pass0(i)
             wp_bf.append(round_weight("wp%d" % (i - 1), wp[(i - 1) * K_PASS : i * K_PASS, :]))
-        wo_bf = round_weight("wo", wo)
         planes[0, 3] = load_plane(0, 3)
         gather_pass0(3)
-        wp_q = [quantize("wp%d" % a, wp_bf[a][:], H, "pick0_%d" % a) for a in range(2)]
-        wo_q = [quantize("wo%d" % n, wo_bf[:, n * K_PASS : (n + 1) * K_PASS], P) for n in range(N // P)]
+        wp_q = [quantize(keep, "wp0", wp_bf[0][:], H, "pick0_0")]
         for i in range(PACK):
             planes[1, i] = load_plane(1, i)
         wg = keep.tile([P, H], U32, align_bytes=64)
@@ -185,21 +178,15 @@ def tile_list_pivot_irrigation_kernel(
         def mover(blk):
             return nc.vector.tensor_copy if blk == S // BLOCK - 1 else nc.scalar.copy
 
-        def gather_pair(c, first, tags):
-            if first == 0:
+        def gather_plane(c, i, tags):
+            if i == 0:
                 x1[c] = two.tile([P, PACK, CHUNK], F32, name="x1")
             picks = []
-            for n in range(2):
-                pick = keep.tile([P, CHUNK], F32, name="pick%d%d" % (c, first + n), tag=tags[n], align_bytes=64)
-                nc.vector.tensor_copy(out=pick[:], in_=planes[1, first + n][:].indirect(entries(list2, c * CHUNK, CHUNK)))
+            for n, offsets in enumerate((list2, list3)):
+                pick = keep.tile([P, CHUNK], F32, name="pick%d%d%d" % (c, i, n), tag=tags[n], align_bytes=64)
+                nc.vector.tensor_copy(out=pick[:], in_=planes[1, i][:].indirect(entries(offsets, c * CHUNK, CHUNK)))
                 picks.append(pick)
-            for n in range(2):
-                nc.vector.tensor_tensor(
-                    out=x1[c][:, first + n, :],
-                    in0=planes[1, first + n][:].indirect(entries(list3, c * CHUNK, CHUNK)),
-                    in1=picks[n][:],
-                    op=ADD,
-                )
+            nc.gpsimd.tensor_tensor(out=x1[c][:, i, :], in0=picks[0][:], in1=picks[1][:], op=ADD)
 
         def transposed_sum(name, blk, early, late, grouped):
             bank = psum2.tile([P, PACK, BLOCK], F32, name=name + "_bank")
@@ -221,7 +208,7 @@ def tile_list_pivot_irrigation_kernel(
             cols = slice(n * BLOCK, (n + 1) * BLOCK)
             grouped = keep.tile([P, PACK * BLOCK], BF16, name="x1_bf%d" % blk, tag="x_slot%d" % (blk % 4), align_bytes=64)
             interleave(mover(blk), grouped[:], x1[c][:, :, cols])
-            x1_q = quantize("x1_%d" % blk, grouped[:], BLOCK)
+            x1_q = quantize(four, "x1", grouped[:], BLOCK)
             bank = psum2.tile([P, H], F32, name="ab_bank")
             operands = ((x0_q[c][0][:, cols], x0_q[c][1][:, cols]), (x1_q[0][:], x1_q[1][:]))
             for a in range(2):
@@ -238,8 +225,8 @@ def tile_list_pivot_irrigation_kernel(
             mover(blk)(out=b_sb[blk][:], in_=bank[:].rearrange("p (m t) -> p t m", t=PACK))
 
         def make_gate(blk):
-            grouped = keep.tile([P, BLOCK, PACK], BF16, name="h_bf%d" % blk, tag="h_slot%d" % (blk % 4), align_bytes=64)
-            h_q = quantize("h_%d" % blk, transposed_sum("h", blk, a_sb[blk], b_sb[blk], grouped), BLOCK)
+            grouped = keep.tile([P, BLOCK, PACK], BF16, name="h_bf%d" % blk, tag="h_slot%d" % blk, align_bytes=64)
+            h_q = quantize(four, "h", transposed_sum("h", blk, a_sb[blk], b_sb[blk], grouped), BLOCK)
             bank = psum1.tile([P, H], F32, name="gate_bank")
             nc.tensor.matmul_mx(
                 out=bank[:],
@@ -254,22 +241,22 @@ def tile_list_pivot_irrigation_kernel(
             nc.scalar.activation(out=gate[blk][:], in_=bank[:].rearrange("p (m t) -> p t m", t=PACK), func=SIGMOID)
 
         def difference(blk):
-            diff[blk] = keep.tile([P, PACK, P], F32, name="diff%d" % blk, tag="x_slot%d" % (blk % 4), align_bytes=64)
-            nc.vector.tensor_tensor(out=diff[blk][:], in0=a_sb[blk][:], in1=b_sb[blk][:], op=SUB)
+            diff[blk] = four.tile([P, PACK, P], F32, name="diff")
+            (nc.vector if blk >= S // BLOCK - 2 else nc.gpsimd).tensor_tensor(out=diff[blk][:], in0=a_sb[blk][:], in1=b_sb[blk][:], op=SUB)
 
         def interpolate(blk):
-            term[blk] = keep.tile([P, PACK, P], F32, name="term%d" % blk, tag="h_slot%d" % (blk % 4), align_bytes=64)
+            term[blk] = keep.tile([P, PACK, P], F32, name="term%d" % blk, tag="a_slot%d" % blk, align_bytes=64)
             nc.vector.tensor_tensor(out=term[blk][:], in0=gate[blk][:], in1=diff[blk][:], op=MULT)
 
         def finish(blk):
             grouped = two.tile([P, BLOCK, PACK], BF16, name="z_bf", align_bytes=64)
-            z_q = quantize("z_%d" % blk, transposed_sum("z", blk, b_sb[blk], term[blk], grouped), BLOCK)
+            z_q = quantize(four, "z", transposed_sum("z", blk, b_sb[blk], term[blk], grouped), BLOCK)
             bank = psum1.tile([P, N // P, BLOCK], F32, name="out_bank")
             for n in range(N // P):
                 nc.tensor.matmul_mx(
                     out=bank[:, n, :],
-                    lhsT=wo_q[n][0][:].bitcast(FP8X4),
-                    lhsT_scale=wo_q[n][1][:],
+                    lhsT=wo_codes[:, n * P : (n + 1) * P].bitcast(FP8X4),
+                    lhsT_scale=wo_scales[:, n * P : (n + 1) * P],
                     rhs=z_q[0][:].bitcast(FP8X4),
                     rhs_scale=z_q[1][:],
                     start=True,
@@ -285,22 +272,41 @@ def tile_list_pivot_irrigation_kernel(
             for n in range(2):
                 step(2 * c + n)
 
-        def slots(kind, c):
-            return ["%s_slot%d" % (kind, (2 * c + n) % 4) for n in range(2)]
+        def quantize_x0(c, tag):
+            x0_q[c] = quantize(keep, "x0_%d" % c, x0_bf[c][:], CHUNK, tag)
 
-        for first in (0, 2):
-            gather_pair(0, first, ["first%d" % first, "first%d" % (first + 1)])
-            for n in (first, first + 1):
-                x0_q[n] = quantize("x0_%d" % n, x0_bf[n][:], CHUNK, "first%d" % n)
+        for i in range(PACK):
+            gather_plane(0, i, ["first%d0" % i, "first%d1" % i])
+            if i == 1:
+                wp_q.append(quantize(keep, "wp1", wp_bf[1][:], H, "first00"))
+                quantize_x0(0, "first01")
+        quantize_x0(1, "first20")
+        last_picks = ["first30", "first31"]
         for c in range(CHUNKS):
+            more = c + 1 < CHUNKS
             both(project_probes, c)
-            if c + 1 < CHUNKS:
-                gather_pair(c + 1, 0, slots("x", c))
+            if more:
+                for n in range(2):
+                    gather_plane(c + 1, n, ["x_slot%d" % ((2 * c + n) % 4), last_picks[n]])
+                if c + 2 < CHUNKS:
+                    quantize_x0(c + 2, last_picks[0])
+            if c == 0:
+                wo_codes = keep.tile([P, N], U32, tag=last_picks[1], align_bytes=64)
+                wo_scales = keep.tile([P, N], U8, align_bytes=64)
+                for n in range(N // P):
+                    cols = slice(n * P, (n + 1) * P)
+                    nc.vector.quantize_mx(
+                        out=wo_codes[:, cols].bitcast(FP8X4),
+                        scales=wo_scales[:, cols],
+                        in_=wo_bf[:, n * K_PASS : (n + 1) * K_PASS],
+                    )
             if c >= 1:
                 both(finish, c - 1)
             both(make_gate, c)
             both(difference, c)
-            if c + 1 < CHUNKS:
-                gather_pair(c + 1, 2, slots("h", c))
+            if more:
+                last_picks = ["h_slot%d" % (2 * c + n) for n in range(2)]
+                gather_plane(c + 1, 2, ["a_slot%d" % (2 * c + n) for n in range(2)])
+                gather_plane(c + 1, 3, last_picks)
             both(interpolate, c)
         both(finish, CHUNKS - 1)

@@ -40,7 +40,6 @@ def tile_list_pivot_irrigation_kernel(
         keep = ctx.enter_context(tc.tile_pool(name="keep", bufs=1))
         two = ctx.enter_context(tc.tile_pool(name="two", bufs=2))
         four = ctx.enter_context(tc.tile_pool(name="four", bufs=4))
-        psum1 = ctx.enter_context(tc.psum_pool(name="psum1", bufs=1))
         psum2 = ctx.enter_context(tc.psum_pool(name="psum2", bufs=2))
 
         def interleave(copy, dst, src):
@@ -68,7 +67,7 @@ def tile_list_pivot_irrigation_kernel(
             return raw
 
         tab_sc = keep.tile([P, T], U8, align_bytes=64)
-        nc.vector.memset(tab_sc[:].bitcast(I32), 0)
+        nc.gpsimd.memset(tab_sc[:].bitcast(I32), 0)
         for q in range(4):
             nc.scalar.dma_start(
                 out=tab_sc[32 * q : 32 * q + 8, :].bitcast(I32),
@@ -89,19 +88,24 @@ def tile_list_pivot_irrigation_kernel(
         planes = {(0, 0): load_plane(0, 0)}
         nc.sync.dma_start(list2[:], offs2)
         nc.sync.dma_start(list3[:], offs3)
-
         v_sc0 = keep.tile([P, S], U8, align_bytes=64)
         nc.vector.tensor_copy(out=v_sc0[:], in_=tab_sc[:].indirect(list1[:]))
 
         x0 = keep.tile([P, PACK, S], F32)
 
         def gather_pass0(i):
+            picks = []
             for h in range(S // HALF):
-                total = x0[:, i, h * HALF : (h + 1) * HALF]
                 pick = keep.tile([P, HALF], F32, name="pick0_%d%d" % (i, h), tag="pick0_%d" % h, align_bytes=64)
-                nc.vector.tensor_copy(out=total, in_=planes[0, i][:].indirect(entries(list2, h * HALF, HALF)))
-                nc.vector.tensor_copy(out=pick[:], in_=planes[0, i][:].indirect(entries(list3, h * HALF, HALF)))
-                nc.gpsimd.tensor_tensor(out=total, in0=total, in1=pick[:], op=ADD)
+                nc.vector.tensor_copy(out=pick[:], in_=planes[0, i][:].indirect(entries(list2, h * HALF, HALF)))
+                picks.append(pick)
+            for h in range(S // HALF):
+                nc.vector.tensor_tensor(
+                    out=x0[:, i, h * HALF : (h + 1) * HALF],
+                    in0=planes[0, i][:].indirect(entries(list3, h * HALF, HALF)),
+                    in1=picks[h][:],
+                    op=ADD,
+                )
 
         def round_weight(name, rows):
             raw = load_rows(name, rows)
@@ -112,6 +116,7 @@ def tile_list_pivot_irrigation_kernel(
 
         gather_pass0(0)
         wo_bf = round_weight("wo", wo)
+        wo_q = [quantize(keep, "wo%d" % n, wo_bf[:, n * K_PASS : (n + 1) * K_PASS], P) for n in range(N // P)]
 
         v_codes = []
         for a in range(2):
@@ -121,7 +126,7 @@ def tile_list_pivot_irrigation_kernel(
             nc.vector.tensor_copy(out=picked[:], in_=tab[:].indirect(list1[:]))
             v_codes.append(picked)
         v_scales = [v_sc0, v_sc1]
-        nc.sync.dma_start(out=v_sc1[0 : P - 4, :].bitcast(I32), in_=v_sc0[4:P, :].bitcast(I32))
+        nc.scalar.dma_start(out=v_sc1[0 : P - 4, :].bitcast(I32), in_=v_sc0[4:P, :].bitcast(I32))
 
         wm = keep.tile([P, 2, 2 * H], U8, align_bytes=64)
         nc.sync.dma_start(out=wm[:].bitcast(I32), in_=wm_words.bitcast(I32).rearrange("a p n -> p a n"))
@@ -145,7 +150,7 @@ def tile_list_pivot_irrigation_kernel(
                     start=(a == 0),
                     stop=(a == 1),
                 )
-            a_blk = keep.tile([P, PACK, P], F32, name="a_sb%d" % blk, tag="a_slot%d" % blk, align_bytes=64)
+            a_blk = keep.tile([P, PACK, P], F32, name="a_sb%d" % blk)
             nc.scalar.copy(out=a_blk[:], in_=bank[:].rearrange("p (m t) -> p t m", t=PACK))
             a_sb.append(a_blk)
 
@@ -156,7 +161,7 @@ def tile_list_pivot_irrigation_kernel(
             wp_bf.append(round_weight("wp%d" % (i - 1), wp[(i - 1) * K_PASS : i * K_PASS, :]))
         planes[0, 3] = load_plane(0, 3)
         gather_pass0(3)
-        wp_q = [quantize(keep, "wp0", wp_bf[0][:], H, "pick0_0")]
+        wp_q = [quantize(keep, "wp%d" % a, wp_bf[a][:], H, "pick0_%d" % a) for a in range(2)]
         for i in range(PACK):
             planes[1, i] = load_plane(1, i)
         wg = keep.tile([P, H], U32, align_bytes=64)
@@ -167,26 +172,48 @@ def tile_list_pivot_irrigation_kernel(
                 in_=wg_scales[0, 4 * q : 4 * q + 4, :].bitcast(I32),
             )
 
-        x0_bf, x0_q = [], {}
+        x0_bf = keep.tile([P, PACK * S], BF16, align_bytes=64)
         for c in range(CHUNKS):
-            grouped = keep.tile([P, PACK * CHUNK], BF16, name="x0_bf%d" % c, align_bytes=64)
-            interleave(nc.scalar.copy, grouped[:], x0[:, :, c * CHUNK : (c + 1) * CHUNK])
-            x0_bf.append(grouped)
+            interleave(
+                nc.scalar.copy, x0_bf[:, PACK * c * CHUNK : PACK * (c + 1) * CHUNK], x0[:, :, c * CHUNK : (c + 1) * CHUNK]
+            )
 
-        x1, b_sb, diff, gate, term = {}, {}, {}, {}, {}
+        x1, b_sb, diff, gate, term, z_bf = {}, {}, {}, {}, {}, {}
 
         def mover(blk):
             return nc.vector.tensor_copy if blk == S // BLOCK - 1 else nc.scalar.copy
 
-        def gather_plane(c, i, tags):
-            if i == 0:
-                x1[c] = two.tile([P, PACK, CHUNK], F32, name="x1")
+        def early_tags(c):
+            return ["early%d_0" % (c % 3), "early%d_1" % (c % 3)]
+
+        def late_tags(c):
+            return early_tags(1) if c == 1 else ["late%d_0" % (c % 2), "late%d_1" % (c % 2)]
+
+        def x_tag(blk):
+            c, n = divmod(blk, 2)
+            return early_tags(c + 1)[n] if n == 1 or c == 0 else "x_first"
+
+        def h_tag(blk):
+            c, n = divmod(blk, 2)
+            return early_tags(c + 2)[0] if n == 1 else "h_first"
+
+        def gather_pair(c, first, tags):
+            if first == 0:
+                x1[c] = keep.tile([P, PACK, CHUNK], F32, name="x1_%d" % c, tag="x1_slot%d" % (c % 2), align_bytes=64)
             picks = []
-            for n, offsets in enumerate((list2, list3)):
-                pick = keep.tile([P, CHUNK], F32, name="pick%d%d%d" % (c, i, n), tag=tags[n], align_bytes=64)
-                nc.vector.tensor_copy(out=pick[:], in_=planes[1, i][:].indirect(entries(offsets, c * CHUNK, CHUNK)))
+            for n in range(2):
+                pick = keep.tile([P, CHUNK], F32, name="pick%d%d" % (c, first + n), tag=tags[n], align_bytes=64)
+                nc.vector.tensor_copy(out=pick[:], in_=planes[1, first + n][:].indirect(entries(list2, c * CHUNK, CHUNK)))
                 picks.append(pick)
-            nc.gpsimd.tensor_tensor(out=x1[c][:, i, :], in0=picks[0][:], in1=picks[1][:], op=ADD)
+            width = BLOCK if (c, first) == (CHUNKS - 1, 2) else CHUNK
+            for start in range(0, CHUNK, width):
+                for n in range(2):
+                    nc.vector.tensor_tensor(
+                        out=x1[c][:, first + n, start : start + width],
+                        in0=planes[1, first + n][:].indirect(entries(list3, c * CHUNK + start, width)),
+                        in1=picks[n][:, start : start + width],
+                        op=ADD,
+                    )
 
         def transposed_sum(name, blk, early, late, grouped):
             bank = psum2.tile([P, PACK, BLOCK], F32, name=name + "_bank")
@@ -200,17 +227,18 @@ def tile_list_pivot_irrigation_kernel(
                         start=(n == 0 and t == 0),
                         stop=(n == 1 and t == PACK - 1),
                     )
-            mover(blk)(out=grouped[:], in_=bank[:].rearrange("p t j -> p j t"))
-            return grouped[:].rearrange("p j t -> p (j t)")
+            nc.scalar.copy(out=grouped, in_=bank[:].rearrange("p t j -> p j t"))
+            return grouped.rearrange("p j t -> p (j t)")
 
         def project_probes(blk):
             c, n = divmod(blk, 2)
             cols = slice(n * BLOCK, (n + 1) * BLOCK)
-            grouped = keep.tile([P, PACK * BLOCK], BF16, name="x1_bf%d" % blk, tag="x_slot%d" % (blk % 4), align_bytes=64)
+            grouped = keep.tile([P, PACK * BLOCK], BF16, name="x1_bf%d" % blk, tag=x_tag(blk), align_bytes=64)
             interleave(mover(blk), grouped[:], x1[c][:, :, cols])
             x1_q = quantize(four, "x1", grouped[:], BLOCK)
             bank = psum2.tile([P, H], F32, name="ab_bank")
-            operands = ((x0_q[c][0][:, cols], x0_q[c][1][:, cols]), (x1_q[0][:], x1_q[1][:]))
+            tokens = slice(blk * BLOCK, (blk + 1) * BLOCK)
+            operands = ((x0_q[0][:, tokens], x0_q[1][:, tokens]), (x1_q[0][:], x1_q[1][:]))
             for a in range(2):
                 nc.tensor.matmul_mx(
                     out=bank[:],
@@ -222,12 +250,12 @@ def tile_list_pivot_irrigation_kernel(
                     stop=(a == 1),
                 )
             b_sb[blk] = four.tile([P, PACK, P], F32, name="b_sb")
-            mover(blk)(out=b_sb[blk][:], in_=bank[:].rearrange("p (m t) -> p t m", t=PACK))
+            nc.scalar.copy(out=b_sb[blk][:], in_=bank[:].rearrange("p (m t) -> p t m", t=PACK))
 
         def make_gate(blk):
-            grouped = keep.tile([P, BLOCK, PACK], BF16, name="h_bf%d" % blk, tag="h_slot%d" % blk, align_bytes=64)
-            h_q = quantize(four, "h", transposed_sum("h", blk, a_sb[blk], b_sb[blk], grouped), BLOCK)
-            bank = psum1.tile([P, H], F32, name="gate_bank")
+            grouped = keep.tile([P, BLOCK, PACK], BF16, name="h_bf%d" % blk, tag=h_tag(blk), align_bytes=64)
+            h_q = quantize(four, "h", transposed_sum("h", blk, a_sb[blk], b_sb[blk], grouped[:]), BLOCK)
+            bank = psum2.tile([P, H], F32, name="gate_bank", tag="lone_pass")
             nc.tensor.matmul_mx(
                 out=bank[:],
                 lhsT=h_q[0][:].bitcast(FP8X4),
@@ -237,26 +265,28 @@ def tile_list_pivot_irrigation_kernel(
                 start=True,
                 stop=True,
             )
-            gate[blk] = four.tile([P, PACK, P], F32, name="gate")
+            gate[blk] = keep.tile([P, PACK, P], F32, name="gate%d" % blk, tag=late_tags(blk // 2 + 2)[blk % 2], align_bytes=64)
             nc.scalar.activation(out=gate[blk][:], in_=bank[:].rearrange("p (m t) -> p t m", t=PACK), func=SIGMOID)
 
         def difference(blk):
-            diff[blk] = four.tile([P, PACK, P], F32, name="diff")
-            (nc.vector if blk >= S // BLOCK - 2 else nc.gpsimd).tensor_tensor(out=diff[blk][:], in0=a_sb[blk][:], in1=b_sb[blk][:], op=SUB)
+            diff[blk] = keep.tile([P, PACK, P], F32, name="diff%d" % blk, tag=late_tags(blk // 2 + 1)[blk % 2], align_bytes=64)
+            nc.vector.tensor_tensor(out=diff[blk][:], in0=a_sb[blk][:], in1=b_sb[blk][:], op=SUB)
 
         def interpolate(blk):
-            term[blk] = keep.tile([P, PACK, P], F32, name="term%d" % blk, tag="a_slot%d" % blk, align_bytes=64)
+            term[blk] = keep.tile([P, PACK, P], F32, name="term%d" % blk, tag=early_tags(blk // 2 + 2)[blk % 2], align_bytes=64)
             nc.vector.tensor_tensor(out=term[blk][:], in0=gate[blk][:], in1=diff[blk][:], op=MULT)
 
         def finish(blk):
-            grouped = two.tile([P, BLOCK, PACK], BF16, name="z_bf", align_bytes=64)
-            z_q = quantize(four, "z", transposed_sum("z", blk, b_sb[blk], term[blk], grouped), BLOCK)
-            bank = psum1.tile([P, N // P, BLOCK], F32, name="out_bank")
+            c, n = divmod(blk, 2)
+            if n == 0:
+                z_bf[c] = keep.tile([P, 2, BLOCK, PACK], BF16, name="z_bf%d" % c, tag="x1_slot%d" % ((c + 1) % 2), align_bytes=64)
+            z_q = quantize(four, "z", transposed_sum("z", blk, b_sb[blk], term[blk], z_bf[c][:, n]), BLOCK)
+            bank = psum2.tile([P, N // P, BLOCK], F32, name="out_bank", tag="lone_pass")
             for n in range(N // P):
                 nc.tensor.matmul_mx(
                     out=bank[:, n, :],
-                    lhsT=wo_codes[:, n * P : (n + 1) * P].bitcast(FP8X4),
-                    lhsT_scale=wo_scales[:, n * P : (n + 1) * P],
+                    lhsT=wo_q[n][0][:].bitcast(FP8X4),
+                    lhsT_scale=wo_q[n][1][:],
                     rhs=z_q[0][:].bitcast(FP8X4),
                     rhs_scale=z_q[1][:],
                     start=True,
@@ -272,41 +302,23 @@ def tile_list_pivot_irrigation_kernel(
             for n in range(2):
                 step(2 * c + n)
 
-        def quantize_x0(c, tag):
-            x0_q[c] = quantize(keep, "x0_%d" % c, x0_bf[c][:], CHUNK, tag)
-
-        for i in range(PACK):
-            gather_plane(0, i, ["first%d0" % i, "first%d1" % i])
-            if i == 1:
-                wp_q.append(quantize(keep, "wp1", wp_bf[1][:], H, "first00"))
-                quantize_x0(0, "first01")
-        quantize_x0(1, "first20")
-        last_picks = ["first30", "first31"]
+        gather_pair(0, 0, ["first0", "first1"])
+        gather_pair(0, 2, ["first0", "first1"])
+        x0_q = quantize(keep, "x0", x0_bf[:], S, "first1")
         for c in range(CHUNKS):
-            more = c + 1 < CHUNKS
             both(project_probes, c)
-            if more:
-                for n in range(2):
-                    gather_plane(c + 1, n, ["x_slot%d" % ((2 * c + n) % 4), last_picks[n]])
-                if c + 2 < CHUNKS:
-                    quantize_x0(c + 2, last_picks[0])
-            if c == 0:
-                wo_codes = keep.tile([P, N], U32, tag=last_picks[1], align_bytes=64)
-                wo_scales = keep.tile([P, N], U8, align_bytes=64)
-                for n in range(N // P):
-                    cols = slice(n * P, (n + 1) * P)
-                    nc.vector.quantize_mx(
-                        out=wo_codes[:, cols].bitcast(FP8X4),
-                        scales=wo_scales[:, cols],
-                        in_=wo_bf[:, n * K_PASS : (n + 1) * K_PASS],
-                    )
             if c >= 1:
-                both(finish, c - 1)
+                both(difference, c - 1)
             both(make_gate, c)
-            both(difference, c)
-            if more:
-                last_picks = ["h_slot%d" % (2 * c + n) for n in range(2)]
-                gather_plane(c + 1, 2, ["a_slot%d" % (2 * c + n) for n in range(2)])
-                gather_plane(c + 1, 3, last_picks)
-            both(interpolate, c)
+            if c >= 2:
+                both(finish, c - 2)
+            if c + 1 < CHUNKS:
+                gather_pair(c + 1, 0, early_tags(c + 1))
+            if c >= 1:
+                both(interpolate, c - 1)
+            if c + 1 < CHUNKS:
+                gather_pair(c + 1, 2, late_tags(c + 1))
+        both(difference, CHUNKS - 1)
+        both(interpolate, CHUNKS - 1)
+        both(finish, CHUNKS - 2)
         both(finish, CHUNKS - 1)

@@ -25,7 +25,6 @@ K_PASS = P * PACK
 BLOCK = 128
 CHUNK = 256
 CHUNKS = S // CHUNK
-HALF = 512
 
 
 def entries(offsets, first, count):
@@ -40,6 +39,7 @@ def tile_list_pivot_irrigation_kernel(
         keep = ctx.enter_context(tc.tile_pool(name="keep", bufs=1))
         two = ctx.enter_context(tc.tile_pool(name="two", bufs=2))
         four = ctx.enter_context(tc.tile_pool(name="four", bufs=4))
+        psum1 = ctx.enter_context(tc.psum_pool(name="psum1", bufs=1))
         psum2 = ctx.enter_context(tc.psum_pool(name="psum2", bufs=2))
 
         def interleave(copy, dst, src):
@@ -91,21 +91,31 @@ def tile_list_pivot_irrigation_kernel(
         v_sc0 = keep.tile([P, S], U8, align_bytes=64)
         nc.vector.tensor_copy(out=v_sc0[:], in_=tab_sc[:].indirect(list1[:]))
 
-        x0 = keep.tile([P, PACK, S], F32)
+        x0_turned = [keep.tile([P, 2, 2, P, 2], BF16, name="x0_turned%d" % c) for c in range(CHUNKS)]
+        sum_banks = {}
 
         def gather_pass0(i):
-            picks = []
-            for h in range(S // HALF):
-                pick = keep.tile([P, HALF], F32, name="pick0_%d%d" % (i, h), tag="pick0_%d" % h, align_bytes=64)
-                nc.vector.tensor_copy(out=pick[:], in_=planes[0, i][:].indirect(entries(list2, h * HALF, HALF)))
-                picks.append(pick)
-            for h in range(S // HALF):
-                nc.vector.tensor_tensor(
-                    out=x0[:, i, h * HALF : (h + 1) * HALF],
-                    in0=planes[0, i][:].indirect(entries(list3, h * HALF, HALF)),
-                    in1=picks[h][:],
-                    op=ADD,
-                )
+            u, e = divmod(i, 2)
+            for n, offsets in enumerate((list2, list3)):
+                pick = keep.tile([P, S], F32, name="pick0_%d%d" % (i, n), tag="pick0_%d%d" % (e, n), align_bytes=64)
+                nc.vector.tensor_copy(out=pick[:], in_=planes[0, i][:].indirect(offsets[:]))
+                for c in range(CHUNKS):
+                    if (e, n) == (0, 0):
+                        sum_banks[c] = psum2.tile([P, 2, 2, P], F32, name="sum_bank", tag="hz"[c % 2] + "_bank")
+                    for b in range(2):
+                        blk = 2 * c + b
+                        nc.tensor.matmul(
+                            out=sum_banks[c][:, b, e, :],
+                            lhsT=pick[:, blk * BLOCK : (blk + 1) * BLOCK],
+                            rhs=ident[:],
+                            is_transpose=True,
+                            start=(e, n, b) == (0, 0, 0),
+                            stop=(e, n, b) == (1, 1, 1),
+                        )
+                    if (e, n) == (1, 1):
+                        nc.scalar.copy(
+                            out=x0_turned[c][:, :, u], in_=sum_banks[c][:].rearrange("j b e p -> j b p e")
+                        )
 
         def round_weight(name, rows):
             raw = load_rows(name, rows)
@@ -161,7 +171,7 @@ def tile_list_pivot_irrigation_kernel(
             wp_bf.append(round_weight("wp%d" % (i - 1), wp[(i - 1) * K_PASS : i * K_PASS, :]))
         planes[0, 3] = load_plane(0, 3)
         gather_pass0(3)
-        wp_q = [quantize(keep, "wp%d" % a, wp_bf[a][:], H, "pick0_%d" % a) for a in range(2)]
+        wp_q = [quantize(keep, "wp%d" % a, wp_bf[a][:], H, "pick0_1%d" % a) for a in range(2)]
         for i in range(PACK):
             planes[1, i] = load_plane(1, i)
         wg = keep.tile([P, H], U32, align_bytes=64)
@@ -174,9 +184,13 @@ def tile_list_pivot_irrigation_kernel(
 
         x0_bf = keep.tile([P, PACK * S], BF16, align_bytes=64)
         for c in range(CHUNKS):
-            interleave(
-                nc.scalar.copy, x0_bf[:, PACK * c * CHUNK : PACK * (c + 1) * CHUNK], x0[:, :, c * CHUNK : (c + 1) * CHUNK]
-            )
+            bank = psum2.tile([P, 2, 2, BLOCK], F32, name="back_bank", tag="ab_bank")
+            for b in range(2):
+                for u in range(2):
+                    pairs = x0_turned[c][:, b, u].rearrange("j p e -> j (p e)").bitcast(F32)
+                    nc.tensor.transpose(out=bank[:, b, u, :], in_=pairs, identity=ident[:])
+            words = x0_bf[:, PACK * c * CHUNK : PACK * (c + 1) * CHUNK].bitcast(F32)
+            nc.scalar.copy(out=words.rearrange("p (b j u) -> p b j u", b=2, u=2), in_=bank[:].rearrange("p b u j -> p b j u"))
 
         x1, b_sb, diff, gate, term, z_bf = {}, {}, {}, {}, {}, {}
 
@@ -216,7 +230,7 @@ def tile_list_pivot_irrigation_kernel(
                     )
 
         def transposed_sum(name, blk, early, late, grouped):
-            bank = psum2.tile([P, PACK, BLOCK], F32, name=name + "_bank")
+            bank = psum2.tile([P, PACK, BLOCK], F32, name=name + "_bank", tag=name + "_bank")
             for n, part in enumerate((early, late)):
                 for t in range(PACK):
                     nc.tensor.matmul(
@@ -255,7 +269,7 @@ def tile_list_pivot_irrigation_kernel(
         def make_gate(blk):
             grouped = keep.tile([P, BLOCK, PACK], BF16, name="h_bf%d" % blk, tag=h_tag(blk), align_bytes=64)
             h_q = quantize(four, "h", transposed_sum("h", blk, a_sb[blk], b_sb[blk], grouped[:]), BLOCK)
-            bank = psum2.tile([P, H], F32, name="gate_bank", tag="lone_pass")
+            bank = psum1.tile([P, H], F32, name="gate_bank")
             nc.tensor.matmul_mx(
                 out=bank[:],
                 lhsT=h_q[0][:].bitcast(FP8X4),
@@ -281,7 +295,7 @@ def tile_list_pivot_irrigation_kernel(
             if n == 0:
                 z_bf[c] = keep.tile([P, 2, BLOCK, PACK], BF16, name="z_bf%d" % c, tag="x1_slot%d" % ((c + 1) % 2), align_bytes=64)
             z_q = quantize(four, "z", transposed_sum("z", blk, b_sb[blk], term[blk], z_bf[c][:, n]), BLOCK)
-            bank = psum2.tile([P, N // P, BLOCK], F32, name="out_bank", tag="lone_pass")
+            bank = psum1.tile([P, N // P, BLOCK], F32, name="out_bank")
             for n in range(N // P):
                 nc.tensor.matmul_mx(
                     out=bank[:, n, :],

@@ -22,13 +22,23 @@ SIGMOID = mybir.ActivationFunctionType.Sigmoid
 P = 128
 PACK = 4
 K_PASS = P * PACK
+PASSES = K // K_PASS
+QUADRANTS = 4
+GROUP = 16
 BLOCK = 128
-CHUNK = 256
+BLOCKS = S // BLOCK
+CHUNK = 2 * BLOCK
 CHUNKS = S // CHUNK
+PLANE_BUFFERS = 6
+SLOT_RING = 3
 
 
 def entries(offsets, first, count):
-    return offsets[:, first // 16 : (first + count) // 16]
+    return offsets[:, first // GROUP : (first + count) // GROUP]
+
+
+def by_word_slot(bank):
+    return bank[:].rearrange("j (p t) -> j t p", t=PACK)
 
 
 def tile_list_pivot_irrigation_kernel(
@@ -44,8 +54,8 @@ def tile_list_pivot_irrigation_kernel(
 
         def interleave(copy, dst, src):
             copy(
-                out=dst.rearrange("p (c i t) -> p c t i", i=4, t=PACK),
-                in_=src.rearrange("p t (c i) -> p c t i", i=4),
+                out=dst.rearrange("p (c i t) -> p c t i", i=2, t=PACK),
+                in_=src.rearrange("p t (c i) -> p c t i", i=2),
             )
 
         def quantize(pool, name, src, words, tag=None):
@@ -54,36 +64,39 @@ def tile_list_pivot_irrigation_kernel(
             nc.vector.quantize_mx(out=codes[:].bitcast(FP8X4), scales=scales[:], in_=src)
             return codes, scales
 
-        def load_plane(a, i):
-            slot = (PACK * a + i) % 6
-            plane = keep.tile([P, T], F32, name="plane%d%d" % (a, i), tag="plane%d" % slot)
-            rows = xT[a * K_PASS : (a + 1) * K_PASS, :].rearrange("(p i) t -> p i t", i=PACK)
-            nc.sync.dma_start(out=plane[:], in_=rows[:, i, :])
+        def load_plane(a, t):
+            tag = "plane%d" % ((PACK * a + t) % PLANE_BUFFERS)
+            plane = keep.tile([P, T], F32, name="plane%d%d" % (a, t), tag=tag)
+            rows = xT[a * K_PASS : (a + 1) * K_PASS, :].rearrange("(p t) c -> p t c", t=PACK)
+            nc.sync.dma_start(out=plane[:], in_=rows[:, t, :])
             return plane
 
-        def load_rows(name, rows):
-            raw = keep.tile([P, PACK, rows.shape[1]], F32, name=name + "_raw")
-            nc.sync.dma_start(out=raw[:], in_=rows.rearrange("(p j) c -> p j c", j=PACK))
-            return raw
+        def round_weight(name, rows):
+            width = rows.shape[1]
+            raw = keep.tile([P, PACK, width], F32, name=name + "_raw")
+            nc.sync.dma_start(out=raw[:], in_=rows.rearrange("(p t) c -> p t c", t=PACK))
+            grouped = keep.tile([P, PACK * width], BF16, name=name + "_bf", align_bytes=64)
+            interleave(nc.scalar.copy, grouped[:], raw[:])
+            return grouped
 
         tab_sc = keep.tile([P, T], U8, align_bytes=64)
         nc.gpsimd.memset(tab_sc[:].bitcast(I32), 0)
-        for q in range(4):
+        for q in range(QUADRANTS):
             nc.scalar.dma_start(
-                out=tab_sc[32 * q : 32 * q + 8, :].bitcast(I32),
+                out=tab_sc[32 * q : 32 * q + 4 * PASSES, :].bitcast(I32),
                 in_=tab_scales[:, 4 * q : 4 * q + 4, :].bitcast(I32),
             )
-        wm_sc = keep.tile([P, 2 * H], U8, align_bytes=64)
+        wm_sc = keep.tile([P, PASSES * H], U8, align_bytes=64)
         wg_sc = keep.tile([P, H], U8, align_bytes=64)
         v_sc1 = keep.tile([P, S], U8, align_bytes=64)
-        for t_ in (wm_sc, wg_sc, v_sc1):
-            nc.vector.memset(t_[:].bitcast(I32), 0)
+        for scale_tile in (wm_sc, wg_sc, v_sc1):
+            nc.vector.memset(scale_tile[:].bitcast(I32), 0)
         ident = keep.tile([P, P], F32)
         make_identity(nc, ident[:])
 
-        list1 = keep.tile([P, S // 16], U16)
-        list2 = keep.tile([P, S // 16], U16)
-        list3 = keep.tile([P, S // 16], U16)
+        list1 = keep.tile([P, S // GROUP], U16)
+        list2 = keep.tile([P, S // GROUP], U16)
+        list3 = keep.tile([P, S // GROUP], U16)
         nc.sync.dma_start(list1[:], offs)
         planes = {(0, 0): load_plane(0, 0)}
         nc.sync.dma_start(list2[:], offs2)
@@ -94,14 +107,14 @@ def tile_list_pivot_irrigation_kernel(
         x0_turned = [keep.tile([P, 2, 2, P, 2], BF16, name="x0_turned%d" % c) for c in range(CHUNKS)]
         sum_banks = {}
 
-        def gather_pass0(i):
-            u, e = divmod(i, 2)
-            for n, offsets in enumerate((list2, list3)):
-                pick = keep.tile([P, S], F32, name="pick0_%d%d" % (i, n), tag="pick0_%d%d" % (e, n), align_bytes=64)
-                nc.vector.tensor_copy(out=pick[:], in_=planes[0, i][:].indirect(offsets[:]))
+        def gather_pass0(t):
+            u, e = divmod(t, 2)
+            for probe, offsets in enumerate((list2, list3)):
+                pick = keep.tile([P, S], F32, name="pick0_%d%d" % (t, probe), tag="pick0_%d%d" % (e, probe), align_bytes=64)
+                nc.vector.tensor_copy(out=pick[:], in_=planes[0, t][:].indirect(offsets[:]))
                 for c in range(CHUNKS):
-                    if (e, n) == (0, 0):
-                        sum_banks[c] = psum2.tile([P, 2, 2, P], F32, name="sum_bank", tag="hz"[c % 2] + "_bank")
+                    if (e, probe) == (0, 0):
+                        sum_banks[c] = psum2.tile([P, 2, 2, P], F32, name="sum_bank", tag=("h_bank", "z_bank")[c % 2])
                     for b in range(2):
                         blk = 2 * c + b
                         nc.tensor.matmul(
@@ -109,48 +122,39 @@ def tile_list_pivot_irrigation_kernel(
                             lhsT=pick[:, blk * BLOCK : (blk + 1) * BLOCK],
                             rhs=ident[:],
                             is_transpose=True,
-                            start=(e, n, b) == (0, 0, 0),
-                            stop=(e, n, b) == (1, 1, 1),
+                            start=(e, probe, b) == (0, 0, 0),
+                            stop=(e, probe, b) == (1, 1, 1),
                         )
-                    if (e, n) == (1, 1):
-                        nc.scalar.copy(
-                            out=x0_turned[c][:, :, u], in_=sum_banks[c][:].rearrange("j b e p -> j b p e")
-                        )
-
-        def round_weight(name, rows):
-            raw = load_rows(name, rows)
-            width = rows.shape[1]
-            grouped = keep.tile([P, PACK * width], BF16, name=name + "_bf", align_bytes=64)
-            interleave(nc.scalar.copy, grouped[:], raw[:])
-            return grouped
+                    if (e, probe) == (1, 1):
+                        nc.scalar.copy(out=x0_turned[c][:, :, u], in_=sum_banks[c][:].rearrange("j b e p -> j b p e"))
 
         gather_pass0(0)
         wo_bf = round_weight("wo", wo)
         wo_q = [quantize(keep, "wo%d" % n, wo_bf[:, n * K_PASS : (n + 1) * K_PASS], P) for n in range(N // P)]
 
         v_codes = []
-        for a in range(2):
+        for a in range(PASSES):
             tab = keep.tile([P, T], U32, name="tab%d" % a)
-            nc.sync.dma_start(out=tab[:].bitcast(I32), in_=tab_words[a].rearrange("p t i -> p (t i)").bitcast(I32))
+            nc.sync.dma_start(out=tab[:].bitcast(I32), in_=tab_words[a].rearrange("p c t -> p (c t)").bitcast(I32))
             picked = keep.tile([P, S], U32, name="v_codes%d" % a, align_bytes=64)
             nc.vector.tensor_copy(out=picked[:], in_=tab[:].indirect(list1[:]))
             v_codes.append(picked)
         v_scales = [v_sc0, v_sc1]
         nc.scalar.dma_start(out=v_sc1[0 : P - 4, :].bitcast(I32), in_=v_sc0[4:P, :].bitcast(I32))
 
-        wm = keep.tile([P, 2, 2 * H], U8, align_bytes=64)
-        nc.sync.dma_start(out=wm[:].bitcast(I32), in_=wm_words.bitcast(I32).rearrange("a p n -> p a n"))
-        for q in range(4):
+        wm = keep.tile([P, PASSES, 2 * H], U8, align_bytes=64)
+        nc.sync.dma_start(out=wm[:].bitcast(I32), in_=wm_words.bitcast(I32).rearrange("a p c -> p a c"))
+        for q in range(QUADRANTS):
             nc.sync.dma_start(
-                out=wm_sc[32 * q : 32 * q + 4, :].bitcast(I32).rearrange("r (a n) -> r a n", a=2),
-                in_=wm_scales[:, 4 * q : 4 * q + 4, :].bitcast(I32).rearrange("a r n -> r a n"),
+                out=wm_sc[32 * q : 32 * q + 4, :].bitcast(I32).rearrange("r (a c) -> r a c", a=PASSES),
+                in_=wm_scales[:, 4 * q : 4 * q + 4, :].bitcast(I32).rearrange("a r c -> r a c"),
             )
 
         a_sb = []
-        for blk in range(S // BLOCK):
+        for blk in range(BLOCKS):
             cols = slice(blk * BLOCK, (blk + 1) * BLOCK)
             bank = psum2.tile([P, H], F32, name="ab_bank")
-            for a in range(2):
+            for a in range(PASSES):
                 nc.tensor.matmul_mx(
                     out=bank[:],
                     lhsT=v_codes[a][:, cols].bitcast(FP8X4),
@@ -158,25 +162,25 @@ def tile_list_pivot_irrigation_kernel(
                     rhs=wm[:, a, :].bitcast(FP4X4),
                     rhs_scale=wm_sc[:, a * H : (a + 1) * H],
                     start=(a == 0),
-                    stop=(a == 1),
+                    stop=(a == PASSES - 1),
                 )
             a_blk = keep.tile([P, PACK, P], F32, name="a_sb%d" % blk)
-            nc.scalar.copy(out=a_blk[:], in_=bank[:].rearrange("p (m t) -> p t m", t=PACK))
+            nc.scalar.copy(out=a_blk[:], in_=by_word_slot(bank))
             a_sb.append(a_blk)
 
         wp_bf = []
-        for i in (1, 2):
-            planes[0, i] = load_plane(0, i)
-            gather_pass0(i)
-            wp_bf.append(round_weight("wp%d" % (i - 1), wp[(i - 1) * K_PASS : i * K_PASS, :]))
+        for a in range(PASSES):
+            planes[0, a + 1] = load_plane(0, a + 1)
+            gather_pass0(a + 1)
+            wp_bf.append(round_weight("wp%d" % a, wp[a * K_PASS : (a + 1) * K_PASS, :]))
         planes[0, 3] = load_plane(0, 3)
         gather_pass0(3)
-        wp_q = [quantize(keep, "wp%d" % a, wp_bf[a][:], H, "pick0_1%d" % a) for a in range(2)]
-        for i in range(PACK):
-            planes[1, i] = load_plane(1, i)
+        wp_q = [quantize(keep, "wp%d" % a, wp_bf[a][:], H, "pick0_1%d" % a) for a in range(PASSES)]
+        for t in range(PACK):
+            planes[1, t] = load_plane(1, t)
         wg = keep.tile([P, H], U32, align_bytes=64)
-        nc.sync.dma_start(out=wg[:].bitcast(I32), in_=wg_words[0].rearrange("p c i -> p (c i)").bitcast(I32))
-        for q in range(4):
+        nc.sync.dma_start(out=wg[:].bitcast(I32), in_=wg_words[0].rearrange("p c t -> p (c t)").bitcast(I32))
+        for q in range(QUADRANTS):
             nc.sync.dma_start(
                 out=wg_sc[32 * q : 32 * q + 4, :].bitcast(I32),
                 in_=wg_scales[0, 4 * q : 4 * q + 4, :].bitcast(I32),
@@ -190,85 +194,72 @@ def tile_list_pivot_irrigation_kernel(
                     pairs = x0_turned[c][:, b, u].rearrange("j p e -> j (p e)").bitcast(F32)
                     nc.tensor.transpose(out=bank[:, b, u, :], in_=pairs, identity=ident[:])
             words = x0_bf[:, PACK * c * CHUNK : PACK * (c + 1) * CHUNK].bitcast(F32)
-            nc.scalar.copy(out=words.rearrange("p (b j u) -> p b j u", b=2, u=2), in_=bank[:].rearrange("p b u j -> p b j u"))
+            nc.scalar.copy(
+                out=words.rearrange("p (b j u) -> p b j u", b=2, u=2), in_=bank[:].rearrange("p b u j -> p b j u")
+            )
 
-        x1, b_sb, diff, gate, term, z_bf = {}, {}, {}, {}, {}, {}
+        x1, picks, b_sb, diff, gate, term, z_bf = {}, {}, {}, {}, {}, {}, {}
 
-        def mover(blk):
-            return nc.vector.tensor_copy if blk == S // BLOCK - 1 else nc.scalar.copy
+        def copier(blk):
+            return nc.vector.tensor_copy if blk == BLOCKS - 1 else nc.scalar.copy
 
-        def early_tags(c):
-            return ["early%d_0" % (c % 3), "early%d_1" % (c % 3)]
+        def slot(kind, c):
+            return "%s_slot%d" % (kind, c % SLOT_RING)
 
-        def late_tags(c):
-            return early_tags(1) if c == 1 else ["late%d_0" % (c % 2), "late%d_1" % (c % 2)]
+        def pick_first(c, t, tag):
+            if t == 0:
+                x1[c] = two.tile([P, PACK, CHUNK], F32, name="x1")
+            picks[t] = keep.tile([P, CHUNK], F32, name="pick%d%d" % (c, t), tag=tag, align_bytes=64)
+            nc.vector.tensor_copy(out=picks[t][:], in_=planes[1, t][:].indirect(entries(list2, c * CHUNK, CHUNK)))
 
-        def x_tag(blk):
-            c, n = divmod(blk, 2)
-            return early_tags(c + 1)[n] if n == 1 or c == 0 else "x_first"
+        def add_second(c, t):
+            nc.vector.tensor_tensor(
+                out=x1[c][:, t, :],
+                in0=planes[1, t][:].indirect(entries(list3, c * CHUNK, CHUNK)),
+                in1=picks[t][:],
+                op=ADD,
+            )
 
-        def h_tag(blk):
-            c, n = divmod(blk, 2)
-            return early_tags(c + 2)[0] if n == 1 else "h_first"
-
-        def gather_pair(c, first, tags):
-            if first == 0:
-                x1[c] = keep.tile([P, PACK, CHUNK], F32, name="x1_%d" % c, tag="x1_slot%d" % (c % 2), align_bytes=64)
-            picks = []
-            for n in range(2):
-                pick = keep.tile([P, CHUNK], F32, name="pick%d%d" % (c, first + n), tag=tags[n], align_bytes=64)
-                nc.vector.tensor_copy(out=pick[:], in_=planes[1, first + n][:].indirect(entries(list2, c * CHUNK, CHUNK)))
-                picks.append(pick)
-            width = BLOCK if (c, first) == (CHUNKS - 1, 2) else CHUNK
-            for start in range(0, CHUNK, width):
-                for n in range(2):
-                    nc.vector.tensor_tensor(
-                        out=x1[c][:, first + n, start : start + width],
-                        in0=planes[1, first + n][:].indirect(entries(list3, c * CHUNK + start, width)),
-                        in1=picks[n][:, start : start + width],
-                        op=ADD,
-                    )
-
-        def transposed_sum(name, blk, early, late, grouped):
+        def transposed_sum(name, early, late, grouped):
             bank = psum2.tile([P, PACK, BLOCK], F32, name=name + "_bank", tag=name + "_bank")
-            for n, part in enumerate((early, late)):
+            for order, part in enumerate((early, late)):
                 for t in range(PACK):
                     nc.tensor.matmul(
                         out=bank[:, t, :],
                         lhsT=part[:, t, :],
                         rhs=ident[:],
                         is_transpose=True,
-                        start=(n == 0 and t == 0),
-                        stop=(n == 1 and t == PACK - 1),
+                        start=(order == 0 and t == 0),
+                        stop=(order == 1 and t == PACK - 1),
                     )
             nc.scalar.copy(out=grouped, in_=bank[:].rearrange("p t j -> p j t"))
             return grouped.rearrange("p j t -> p (j t)")
 
-        def project_probes(blk):
-            c, n = divmod(blk, 2)
-            cols = slice(n * BLOCK, (n + 1) * BLOCK)
-            grouped = keep.tile([P, PACK * BLOCK], BF16, name="x1_bf%d" % blk, tag=x_tag(blk), align_bytes=64)
-            interleave(mover(blk), grouped[:], x1[c][:, :, cols])
+        def project_probes(c, b, tag):
+            blk = 2 * c + b
+            grouped = keep.tile([P, PACK * BLOCK], BF16, name="x1_bf%d" % blk, tag=tag, align_bytes=64)
+            interleave(copier(blk), grouped[:], x1[c][:, :, b * BLOCK : (b + 1) * BLOCK])
             x1_q = quantize(four, "x1", grouped[:], BLOCK)
             bank = psum2.tile([P, H], F32, name="ab_bank")
             tokens = slice(blk * BLOCK, (blk + 1) * BLOCK)
-            operands = ((x0_q[0][:, tokens], x0_q[1][:, tokens]), (x1_q[0][:], x1_q[1][:]))
-            for a in range(2):
+            x_q = ((x0_q[0][:, tokens], x0_q[1][:, tokens]), (x1_q[0][:], x1_q[1][:]))
+            for a in range(PASSES):
                 nc.tensor.matmul_mx(
                     out=bank[:],
-                    lhsT=operands[a][0].bitcast(FP8X4),
-                    lhsT_scale=operands[a][1],
+                    lhsT=x_q[a][0].bitcast(FP8X4),
+                    lhsT_scale=x_q[a][1],
                     rhs=wp_q[a][0][:].bitcast(FP8X4),
                     rhs_scale=wp_q[a][1][:],
                     start=(a == 0),
-                    stop=(a == 1),
+                    stop=(a == PASSES - 1),
                 )
             b_sb[blk] = four.tile([P, PACK, P], F32, name="b_sb")
-            nc.scalar.copy(out=b_sb[blk][:], in_=bank[:].rearrange("p (m t) -> p t m", t=PACK))
+            nc.scalar.copy(out=b_sb[blk][:], in_=by_word_slot(bank))
 
-        def make_gate(blk):
-            grouped = keep.tile([P, BLOCK, PACK], BF16, name="h_bf%d" % blk, tag=h_tag(blk), align_bytes=64)
-            h_q = quantize(four, "h", transposed_sum("h", blk, a_sb[blk], b_sb[blk], grouped[:]), BLOCK)
+        def make_gate(c, b, h_tag, gate_tag):
+            blk = 2 * c + b
+            grouped = keep.tile([P, BLOCK, PACK], BF16, name="h_bf%d" % blk, tag=h_tag, align_bytes=64)
+            h_q = quantize(four, "h", transposed_sum("h", a_sb[blk], b_sb[blk], grouped[:]), BLOCK)
             bank = psum1.tile([P, H], F32, name="gate_bank")
             nc.tensor.matmul_mx(
                 out=bank[:],
@@ -279,60 +270,77 @@ def tile_list_pivot_irrigation_kernel(
                 start=True,
                 stop=True,
             )
-            gate[blk] = keep.tile([P, PACK, P], F32, name="gate%d" % blk, tag=late_tags(blk // 2 + 2)[blk % 2], align_bytes=64)
-            nc.scalar.activation(out=gate[blk][:], in_=bank[:].rearrange("p (m t) -> p t m", t=PACK), func=SIGMOID)
+            gate[blk] = keep.tile([P, PACK, P], F32, name="gate%d" % blk, tag=gate_tag, align_bytes=64)
+            nc.scalar.activation(out=gate[blk][:], in_=by_word_slot(bank), func=SIGMOID)
 
-        def difference(blk):
-            diff[blk] = keep.tile([P, PACK, P], F32, name="diff%d" % blk, tag=late_tags(blk // 2 + 1)[blk % 2], align_bytes=64)
-            nc.vector.tensor_tensor(out=diff[blk][:], in0=a_sb[blk][:], in1=b_sb[blk][:], op=SUB)
+        def difference(c):
+            kinds = ("gb", "ga") if c >= 1 else ("h", "x")
+            for b in range(2):
+                blk = 2 * c + b
+                diff[blk] = keep.tile([P, PACK, P], F32, name="diff%d" % blk, tag=slot(kinds[b], c), align_bytes=64)
+                nc.vector.tensor_tensor(out=diff[blk][:], in0=a_sb[blk][:], in1=b_sb[blk][:], op=SUB)
 
-        def interpolate(blk):
-            term[blk] = keep.tile([P, PACK, P], F32, name="term%d" % blk, tag=early_tags(blk // 2 + 2)[blk % 2], align_bytes=64)
+        def interpolate(c, b):
+            kinds = ("x", "z") if c >= 1 else ("x", "h")
+            blk = 2 * c + b
+            term[blk] = keep.tile([P, PACK, P], F32, name="term%d" % blk, tag=slot(kinds[b], c + 1), align_bytes=64)
             nc.vector.tensor_tensor(out=term[blk][:], in0=gate[blk][:], in1=diff[blk][:], op=MULT)
 
-        def finish(blk):
-            c, n = divmod(blk, 2)
-            if n == 0:
-                z_bf[c] = keep.tile([P, 2, BLOCK, PACK], BF16, name="z_bf%d" % c, tag="x1_slot%d" % ((c + 1) % 2), align_bytes=64)
-            z_q = quantize(four, "z", transposed_sum("z", blk, b_sb[blk], term[blk], z_bf[c][:, n]), BLOCK)
-            bank = psum1.tile([P, N // P, BLOCK], F32, name="out_bank")
-            for n in range(N // P):
-                nc.tensor.matmul_mx(
-                    out=bank[:, n, :],
-                    lhsT=wo_q[n][0][:].bitcast(FP8X4),
-                    lhsT_scale=wo_q[n][1][:],
-                    rhs=z_q[0][:].bitcast(FP8X4),
-                    rhs_scale=z_q[1][:],
-                    start=True,
-                    stop=True,
+        def finish(c):
+            z_bf[c] = keep.tile([P, 2, BLOCK, PACK], BF16, name="z_bf%d" % c, tag=slot("z", c + 2), align_bytes=64)
+            for b in range(2):
+                blk = 2 * c + b
+                z_q = quantize(four, "z", transposed_sum("z", b_sb[blk], term[blk], z_bf[c][:, b]), BLOCK)
+                bank = psum1.tile([P, N // P, BLOCK], F32, name="out_bank")
+                for n in range(N // P):
+                    nc.tensor.matmul_mx(
+                        out=bank[:, n, :],
+                        lhsT=wo_q[n][0][:].bitcast(FP8X4),
+                        lhsT_scale=wo_q[n][1][:],
+                        rhs=z_q[0][:].bitcast(FP8X4),
+                        rhs_scale=z_q[1][:],
+                        start=True,
+                        stop=True,
+                    )
+                staged = two.tile([P, N // P, BLOCK], F32, name="staged")
+                copier(blk)(out=staged[:], in_=bank[:])
+                nc.sync.dma_start(
+                    out=out.rearrange("(n p) j -> p n j", p=P)[:, :, blk * BLOCK : (blk + 1) * BLOCK], in_=staged[:]
                 )
-            staged = two.tile([P, N // P, BLOCK], F32, name="staged")
-            mover(blk)(out=staged[:], in_=bank[:])
-            nc.sync.dma_start(
-                out=out.rearrange("(n p) j -> p n j", p=P)[:, :, blk * BLOCK : (blk + 1) * BLOCK], in_=staged[:]
-            )
 
-        def both(step, c):
-            for n in range(2):
-                step(2 * c + n)
-
-        gather_pair(0, 0, ["first0", "first1"])
-        gather_pair(0, 2, ["first0", "first1"])
+        for t in range(PACK):
+            pick_first(0, t, "first%d" % (t % 2))
+            add_second(0, t)
         x0_q = quantize(keep, "x0", x0_bf[:], S, "first1")
+
         for c in range(CHUNKS):
-            both(project_probes, c)
+            gathers = c + 1 < CHUNKS
+            project_probes(c, 0, slot("h", 0) if c == 0 else "x_first")
+            project_probes(c, 1, slot("x", c))
             if c >= 1:
-                both(difference, c - 1)
-            both(make_gate, c)
+                difference(c - 1)
+            make_gate(c, 0, "h_first", slot("ga", c + 1))
+            make_gate(c, 1, slot("h", c + 1), slot("gb", c + 1))
             if c >= 2:
-                both(finish, c - 2)
-            if c + 1 < CHUNKS:
-                gather_pair(c + 1, 0, early_tags(c + 1))
+                finish(c - 2)
+            if gathers:
+                pick_first(c + 1, 0, slot("h", c))
+                pick_first(c + 1, 1, slot("x", c))
+                add_second(c + 1, 0)
+                pick_first(c + 1, 2, slot("z" if c >= 2 else "h", c))
+                add_second(c + 1, 1)
+                if c == 0:
+                    pick_first(c + 1, 3, slot("x", c))
+                add_second(c + 1, 2)
             if c >= 1:
-                both(interpolate, c - 1)
-            if c + 1 < CHUNKS:
-                gather_pair(c + 1, 2, late_tags(c + 1))
-        both(difference, CHUNKS - 1)
-        both(interpolate, CHUNKS - 1)
-        both(finish, CHUNKS - 2)
-        both(finish, CHUNKS - 1)
+                interpolate(c - 1, 0)
+                if gathers:
+                    pick_first(c + 1, 3, slot("ga", c))
+                interpolate(c - 1, 1)
+            if gathers:
+                add_second(c + 1, 3)
+        difference(CHUNKS - 1)
+        finish(CHUNKS - 2)
+        for b in range(2):
+            interpolate(CHUNKS - 1, b)
+        finish(CHUNKS - 1)

@@ -26,15 +26,13 @@ PASSES = K // K_PASS
 QUADRANTS = 4
 GROUP = 16
 BLOCK = 128
-BLOCKS = S // BLOCK
 CHUNK = 2 * BLOCK
 CHUNKS = S // CHUNK
-PLANE_BUFFERS = 6
-SLOT_RING = 3
+LAST = CHUNKS - 1
 
 
-def entries(offsets, first, count):
-    return offsets[:, first // GROUP : (first + count) // GROUP]
+def entries(offsets, c):
+    return offsets[:, c * CHUNK // GROUP : (c + 1) * CHUNK // GROUP]
 
 
 def by_word_slot(bank):
@@ -49,24 +47,28 @@ def tile_list_pivot_irrigation_kernel(
         keep = ctx.enter_context(tc.tile_pool(name="keep", bufs=1))
         two = ctx.enter_context(tc.tile_pool(name="two", bufs=2))
         four = ctx.enter_context(tc.tile_pool(name="four", bufs=4))
-        psum1 = ctx.enter_context(tc.psum_pool(name="psum1", bufs=1))
-        psum2 = ctx.enter_context(tc.psum_pool(name="psum2", bufs=2))
+        psum = ctx.enter_context(tc.psum_pool(name="psum", bufs=2))
 
-        def interleave(copy, dst, src):
-            copy(
+        def shared(shape, dtype, name, tag):
+            return keep.tile(shape, dtype, name=name, tag=tag, align_bytes=64)
+
+        def interleave(dst, src):
+            nc.scalar.copy(
                 out=dst.rearrange("p (c i t) -> p c t i", i=2, t=PACK),
                 in_=src.rearrange("p t (c i) -> p c t i", i=2),
             )
 
-        def quantize(pool, name, src, words, tag=None):
-            codes = pool.tile([P, words], U32, name=name + "_codes", tag=tag or name + "_codes", align_bytes=64)
-            scales = pool.tile([P, words], U8, name=name + "_scales", align_bytes=64)
+        def quantize(codes, scales, src):
             nc.vector.quantize_mx(out=codes[:].bitcast(FP8X4), scales=scales[:], in_=src)
             return codes, scales
 
+        def quantize_block(name, src):
+            codes = four.tile([P, BLOCK], U32, name=name + "_codes", align_bytes=64)
+            scales = four.tile([P, BLOCK], U8, name=name + "_scales", align_bytes=64)
+            return quantize(codes, scales, src)
+
         def load_plane(a, t):
-            tag = "plane%d" % ((PACK * a + t) % PLANE_BUFFERS)
-            plane = keep.tile([P, T], F32, name="plane%d%d" % (a, t), tag=tag)
+            plane = keep.tile([P, T], F32, name="plane%d%d" % (a, t))
             rows = xT[a * K_PASS : (a + 1) * K_PASS, :].rearrange("(p t) c -> p t c", t=PACK)
             nc.sync.dma_start(out=plane[:], in_=rows[:, t, :])
             return plane
@@ -76,16 +78,11 @@ def tile_list_pivot_irrigation_kernel(
             raw = keep.tile([P, PACK, width], F32, name=name + "_raw")
             nc.sync.dma_start(out=raw[:], in_=rows.rearrange("(p t) c -> p t c", t=PACK))
             grouped = keep.tile([P, PACK * width], BF16, name=name + "_bf", align_bytes=64)
-            interleave(nc.scalar.copy, grouped[:], raw[:])
+            interleave(grouped[:], raw[:])
             return grouped
 
         tab_sc = keep.tile([P, T], U8, align_bytes=64)
         nc.gpsimd.memset(tab_sc[:].bitcast(I32), 0)
-        for q in range(QUADRANTS):
-            nc.scalar.dma_start(
-                out=tab_sc[32 * q : 32 * q + 4 * PASSES, :].bitcast(I32),
-                in_=tab_scales[:, 4 * q : 4 * q + 4, :].bitcast(I32),
-            )
         wm_sc = keep.tile([P, PASSES * H], U8, align_bytes=64)
         wg_sc = keep.tile([P, H], U8, align_bytes=64)
         v_sc1 = keep.tile([P, S], U8, align_bytes=64)
@@ -97,12 +94,11 @@ def tile_list_pivot_irrigation_kernel(
         list1 = keep.tile([P, S // GROUP], U16)
         list2 = keep.tile([P, S // GROUP], U16)
         list3 = keep.tile([P, S // GROUP], U16)
-        nc.sync.dma_start(list1[:], offs)
         planes = {(0, 0): load_plane(0, 0)}
         nc.sync.dma_start(list2[:], offs2)
         nc.sync.dma_start(list3[:], offs3)
-        v_sc0 = keep.tile([P, S], U8, align_bytes=64)
-        nc.vector.tensor_copy(out=v_sc0[:], in_=tab_sc[:].indirect(list1[:]))
+        planes[0, 1] = load_plane(0, 1)
+        nc.sync.dma_start(list1[:], offs)
 
         x0_turned = [keep.tile([P, 2, 2, P, 2], BF16, name="x0_turned%d" % c) for c in range(CHUNKS)]
         sum_banks = {}
@@ -114,7 +110,7 @@ def tile_list_pivot_irrigation_kernel(
                 nc.vector.tensor_copy(out=pick[:], in_=planes[0, t][:].indirect(offsets[:]))
                 for c in range(CHUNKS):
                     if (e, probe) == (0, 0):
-                        sum_banks[c] = psum2.tile([P, 2, 2, P], F32, name="sum_bank", tag=("h_bank", "z_bank")[c % 2])
+                        sum_banks[c] = psum.tile([P, 2, 2, P], F32, name="sum_bank", tag=("ha_bank", "zg_bank")[c % 2])
                     for b in range(2):
                         blk = 2 * c + b
                         nc.tensor.matmul(
@@ -129,18 +125,31 @@ def tile_list_pivot_irrigation_kernel(
                         nc.scalar.copy(out=x0_turned[c][:, :, u], in_=sum_banks[c][:].rearrange("j b e p -> j b p e"))
 
         gather_pass0(0)
-        wo_bf = round_weight("wo", wo)
-        wo_q = [quantize(keep, "wo%d" % n, wo_bf[:, n * K_PASS : (n + 1) * K_PASS], P) for n in range(N // P)]
+        gather_pass0(1)
+        planes[0, 2] = load_plane(0, 2)
+        for q in range(QUADRANTS):
+            nc.sync.dma_start(
+                out=tab_sc[32 * q : 32 * q + 4 * PASSES, :].bitcast(I32),
+                in_=tab_scales[:, 4 * q : 4 * q + 4, :].bitcast(I32),
+            )
+        gather_pass0(2)
+        planes[0, 3] = load_plane(0, 3)
+        v_sc0 = keep.tile([P, S], U8, align_bytes=64)
+        nc.vector.tensor_copy(out=v_sc0[:], in_=tab_sc[:].indirect(list1[:]))
+        v_scales = [v_sc0, v_sc1]
+        nc.gpsimd.dma_start(out=v_sc1[0 : P - 4, :].bitcast(I32), in_=v_sc0[4:P, :].bitcast(I32))
+        gather_pass0(3)
+        wp_bf = [round_weight("wp%d" % a, wp[a * K_PASS : (a + 1) * K_PASS, :]) for a in range(PASSES)]
 
-        v_codes = []
+        planes[1, 0] = load_plane(1, 0)
+        planes[1, 1] = load_plane(1, 1)
+        tabs = []
         for a in range(PASSES):
             tab = keep.tile([P, T], U32, name="tab%d" % a)
             nc.sync.dma_start(out=tab[:].bitcast(I32), in_=tab_words[a].rearrange("p c t -> p (c t)").bitcast(I32))
-            picked = keep.tile([P, S], U32, name="v_codes%d" % a, align_bytes=64)
-            nc.vector.tensor_copy(out=picked[:], in_=tab[:].indirect(list1[:]))
-            v_codes.append(picked)
-        v_scales = [v_sc0, v_sc1]
-        nc.scalar.dma_start(out=v_sc1[0 : P - 4, :].bitcast(I32), in_=v_sc0[4:P, :].bitcast(I32))
+            tabs.append(tab)
+        planes[1, 2] = load_plane(1, 2)
+        planes[1, 3] = load_plane(1, 3)
 
         wm = keep.tile([P, PASSES, 2 * H], U8, align_bytes=64)
         nc.sync.dma_start(out=wm[:].bitcast(I32), in_=wm_words.bitcast(I32).rearrange("a p c -> p a c"))
@@ -149,80 +158,94 @@ def tile_list_pivot_irrigation_kernel(
                 out=wm_sc[32 * q : 32 * q + 4, :].bitcast(I32).rearrange("r (a c) -> r a c", a=PASSES),
                 in_=wm_scales[:, 4 * q : 4 * q + 4, :].bitcast(I32).rearrange("a r c -> r a c"),
             )
-
-        a_sb = []
-        for blk in range(BLOCKS):
-            cols = slice(blk * BLOCK, (blk + 1) * BLOCK)
-            bank = psum2.tile([P, H], F32, name="ab_bank")
-            for a in range(PASSES):
-                nc.tensor.matmul_mx(
-                    out=bank[:],
-                    lhsT=v_codes[a][:, cols].bitcast(FP8X4),
-                    lhsT_scale=v_scales[a][:, cols],
-                    rhs=wm[:, a, :].bitcast(FP4X4),
-                    rhs_scale=wm_sc[:, a * H : (a + 1) * H],
-                    start=(a == 0),
-                    stop=(a == PASSES - 1),
-                )
-            a_blk = keep.tile([P, PACK, P], F32, name="a_sb%d" % blk)
-            nc.scalar.copy(out=a_blk[:], in_=by_word_slot(bank))
-            a_sb.append(a_blk)
-
-        wp_bf = []
-        for a in range(PASSES):
-            planes[0, a + 1] = load_plane(0, a + 1)
-            gather_pass0(a + 1)
-            wp_bf.append(round_weight("wp%d" % a, wp[a * K_PASS : (a + 1) * K_PASS, :]))
-        planes[0, 3] = load_plane(0, 3)
-        gather_pass0(3)
-        wp_q = [quantize(keep, "wp%d" % a, wp_bf[a][:], H, "pick0_1%d" % a) for a in range(PASSES)]
-        for t in range(PACK):
-            planes[1, t] = load_plane(1, t)
-        wg = keep.tile([P, H], U32, align_bytes=64)
-        nc.sync.dma_start(out=wg[:].bitcast(I32), in_=wg_words[0].rearrange("p c t -> p (c t)").bitcast(I32))
         for q in range(QUADRANTS):
             nc.sync.dma_start(
                 out=wg_sc[32 * q : 32 * q + 4, :].bitcast(I32),
                 in_=wg_scales[0, 4 * q : 4 * q + 4, :].bitcast(I32),
             )
+        wg = keep.tile([P, H], U32, align_bytes=64)
+        nc.sync.dma_start(out=wg[:].bitcast(I32), in_=wg_words[0].rearrange("p c t -> p (c t)").bitcast(I32))
 
-        x0_bf = keep.tile([P, PACK * S], BF16, align_bytes=64)
+        x_bf = [shared([P, PASSES, PACK * CHUNK], BF16, "x_bf%d" % c, "x_bf%d" % c) for c in range(CHUNKS)]
         for c in range(CHUNKS):
-            bank = psum2.tile([P, 2, 2, BLOCK], F32, name="back_bank", tag="ab_bank")
+            bank = psum.tile([P, 2, 2, BLOCK], F32, name="back_bank", tag="b_bank")
             for b in range(2):
                 for u in range(2):
                     pairs = x0_turned[c][:, b, u].rearrange("j p e -> j (p e)").bitcast(F32)
                     nc.tensor.transpose(out=bank[:, b, u, :], in_=pairs, identity=ident[:])
-            words = x0_bf[:, PACK * c * CHUNK : PACK * (c + 1) * CHUNK].bitcast(F32)
+            words = x_bf[c][:, 0, :].bitcast(F32)
             nc.scalar.copy(
                 out=words.rearrange("p (b j u) -> p b j u", b=2, u=2), in_=bank[:].rearrange("p b u j -> p b j u")
             )
 
-        x1, picks, b_sb, diff, gate, term, z_bf = {}, {}, {}, {}, {}, {}, {}
+        x1, v_codes, picks, b_bank, a_sb, e_sb, h_bf, gate, term, z_bf, wp_q, wo_q = ({} for name in range(12))
 
-        def copier(blk):
-            return nc.vector.tensor_copy if blk == BLOCKS - 1 else nc.scalar.copy
+        def first_picks(c, ts):
+            if 0 in ts:
+                three = shared([P, 3, CHUNK], F32, "picks%d" % c, "x_slot%d" % (c % 2))
+                picks[0], picks[1], picks[3] = three[:, 0, :], three[:, 1, :], three[:, 2, :]
+            if 2 in ts:
+                picks[2] = shared([P, CHUNK], F32, "pick%d_2" % c, "wp_slot0" if c == 0 else "word_slot")[:]
+                if c == 0:
+                    picks[3] = shared([P, CHUNK], F32, "pick0_3", "wp_slot1")[:]
+            for t in ts:
+                nc.vector.tensor_copy(out=picks[t], in_=planes[1, t][:].indirect(entries(list2, c)))
 
-        def slot(kind, c):
-            return "%s_slot%d" % (kind, c % SLOT_RING)
+        def second_picks(c, ts):
+            if 0 in ts:
+                x1[c] = shared([P, PACK, CHUNK], F32, "x1_%d" % c, "x_slot%d" % ((c + 1) % 2))
+            for t in ts:
+                nc.vector.tensor_tensor(
+                    out=x1[c][:, t, :], in0=planes[1, t][:].indirect(entries(list3, c)), in1=picks[t], op=ADD
+                )
 
-        def pick_first(c, t, tag):
-            if t == 0:
-                x1[c] = two.tile([P, PACK, CHUNK], F32, name="x1")
-            picks[t] = keep.tile([P, CHUNK], F32, name="pick%d%d" % (c, t), tag=tag, align_bytes=64)
-            nc.vector.tensor_copy(out=picks[t][:], in_=planes[1, t][:].indirect(entries(list2, c * CHUNK, CHUNK)))
+        def gather_words(c):
+            v_codes[c] = shared([P, PASSES, CHUNK], U32, "v_codes%d" % c, "word_slot")
+            for a in range(PASSES):
+                nc.vector.tensor_copy(out=v_codes[c][:, a, :], in_=tabs[a][:].indirect(entries(list1, c)))
 
-        def add_second(c, t):
-            nc.vector.tensor_tensor(
-                out=x1[c][:, t, :],
-                in0=planes[1, t][:].indirect(entries(list3, c * CHUNK, CHUNK)),
-                in1=picks[t][:],
-                op=ADD,
-            )
+        def project_table(c):
+            for b in range(2):
+                blk = 2 * c + b
+                bank = psum.tile([P, H], F32, name="a_bank", tag="ha_bank")
+                for a in range(PASSES):
+                    nc.tensor.matmul_mx(
+                        out=bank[:],
+                        lhsT=v_codes[c][:, a, b * BLOCK : (b + 1) * BLOCK].bitcast(FP8X4),
+                        lhsT_scale=v_scales[a][:, blk * BLOCK : (blk + 1) * BLOCK],
+                        rhs=wm[:, a, :].bitcast(FP4X4),
+                        rhs_scale=wm_sc[:, a * H : (a + 1) * H],
+                        start=(a == 0),
+                        stop=(a == PASSES - 1),
+                    )
+                a_sb[blk] = four.tile([P, PACK, P], F32, name="a_sb")
+                nc.scalar.copy(out=a_sb[blk][:], in_=by_word_slot(bank))
 
-        def transposed_sum(name, early, late, grouped):
-            bank = psum2.tile([P, PACK, BLOCK], F32, name=name + "_bank", tag=name + "_bank")
-            for order, part in enumerate((early, late)):
+        def round_probes(c):
+            interleave(x_bf[c][:, 1, :], x1[c][:])
+
+        def project_probes(c):
+            codes = shared([P, PASSES * CHUNK], U32, "x_codes%d" % c, "x_slot%d" % (c % 2))
+            scales = shared([P, PASSES * CHUNK], U8, "x_scales%d" % c, "x_scales_slot")
+            quantize(codes, scales, x_bf[c][:].rearrange("p a c -> p (a c)"))
+            for b in range(2):
+                blk = 2 * c + b
+                b_bank[blk] = psum.tile([P, H], F32, name="b_bank", tag="b_bank")
+                for a in range(PASSES):
+                    cols = slice(a * CHUNK + b * BLOCK, a * CHUNK + (b + 1) * BLOCK)
+                    nc.tensor.matmul_mx(
+                        out=b_bank[blk][:],
+                        lhsT=codes[:, cols].bitcast(FP8X4),
+                        lhsT_scale=scales[:, cols],
+                        rhs=wp_q[a][0][:].bitcast(FP8X4),
+                        rhs_scale=wp_q[a][1][:],
+                        start=(a == 0),
+                        stop=(a == PASSES - 1),
+                    )
+
+        def transposed_sum(tag, parts):
+            bank = psum.tile([P, PACK, BLOCK], F32, name="sum_bank", tag=tag)
+            for order, part in enumerate(parts):
                 for t in range(PACK):
                     nc.tensor.matmul(
                         out=bank[:, t, :],
@@ -230,68 +253,57 @@ def tile_list_pivot_irrigation_kernel(
                         rhs=ident[:],
                         is_transpose=True,
                         start=(order == 0 and t == 0),
-                        stop=(order == 1 and t == PACK - 1),
+                        stop=(order == len(parts) - 1 and t == PACK - 1),
                     )
-            nc.scalar.copy(out=grouped, in_=bank[:].rearrange("p t j -> p j t"))
-            return grouped.rearrange("p j t -> p (j t)")
-
-        def project_probes(c, b, tag):
-            blk = 2 * c + b
-            grouped = keep.tile([P, PACK * BLOCK], BF16, name="x1_bf%d" % blk, tag=tag, align_bytes=64)
-            interleave(copier(blk), grouped[:], x1[c][:, :, b * BLOCK : (b + 1) * BLOCK])
-            x1_q = quantize(four, "x1", grouped[:], BLOCK)
-            bank = psum2.tile([P, H], F32, name="ab_bank")
-            tokens = slice(blk * BLOCK, (blk + 1) * BLOCK)
-            x_q = ((x0_q[0][:, tokens], x0_q[1][:, tokens]), (x1_q[0][:], x1_q[1][:]))
-            for a in range(PASSES):
-                nc.tensor.matmul_mx(
-                    out=bank[:],
-                    lhsT=x_q[a][0].bitcast(FP8X4),
-                    lhsT_scale=x_q[a][1],
-                    rhs=wp_q[a][0][:].bitcast(FP8X4),
-                    rhs_scale=wp_q[a][1][:],
-                    start=(a == 0),
-                    stop=(a == PASSES - 1),
-                )
-            b_sb[blk] = four.tile([P, PACK, P], F32, name="b_sb")
-            nc.scalar.copy(out=b_sb[blk][:], in_=by_word_slot(bank))
-
-        def make_gate(c, b, h_tag, gate_tag):
-            blk = 2 * c + b
-            grouped = keep.tile([P, BLOCK, PACK], BF16, name="h_bf%d" % blk, tag=h_tag, align_bytes=64)
-            h_q = quantize(four, "h", transposed_sum("h", a_sb[blk], b_sb[blk], grouped[:]), BLOCK)
-            bank = psum1.tile([P, H], F32, name="gate_bank")
-            nc.tensor.matmul_mx(
-                out=bank[:],
-                lhsT=h_q[0][:].bitcast(FP8X4),
-                lhsT_scale=h_q[1][:],
-                rhs=wg[:].bitcast(FP8X4),
-                rhs_scale=wg_sc[:],
-                start=True,
-                stop=True,
-            )
-            gate[blk] = keep.tile([P, PACK, P], F32, name="gate%d" % blk, tag=gate_tag, align_bytes=64)
-            nc.scalar.activation(out=gate[blk][:], in_=by_word_slot(bank), func=SIGMOID)
+            return bank[:].rearrange("p t j -> p j t")
 
         def difference(c):
-            kinds = ("gb", "ga") if c >= 1 else ("h", "x")
+            for blk in (2 * c, 2 * c + 1):
+                e_sb[blk] = four.tile([P, PACK, P], F32, name="e_sb")
+                nc.vector.tensor_tensor(out=e_sb[blk][:], in0=by_word_slot(b_bank[blk]), in1=a_sb[blk][:], op=SUB)
+
+        def sum_h(c):
+            for blk in (2 * c, 2 * c + 1):
+                parts = (a_sb[blk], a_sb[blk], e_sb[blk])
+                h_bf[blk] = two.tile([P, BLOCK, PACK], BF16, name="h_bf", align_bytes=64)
+                nc.scalar.copy(out=h_bf[blk][:], in_=transposed_sum("ha_bank", parts))
+
+        def make_gate(c):
             for b in range(2):
                 blk = 2 * c + b
-                diff[blk] = keep.tile([P, PACK, P], F32, name="diff%d" % blk, tag=slot(kinds[b], c), align_bytes=64)
-                nc.vector.tensor_tensor(out=diff[blk][:], in0=a_sb[blk][:], in1=b_sb[blk][:], op=SUB)
+                h_q = quantize_block("h", h_bf[blk][:].rearrange("p j t -> p (j t)"))
+                bank = psum.tile([P, H], F32, name="gate_bank", tag="zg_bank")
+                nc.tensor.matmul_mx(
+                    out=bank[:],
+                    lhsT=h_q[0][:].bitcast(FP8X4),
+                    lhsT_scale=h_q[1][:],
+                    rhs=wg[:].bitcast(FP8X4),
+                    rhs_scale=wg_sc[:],
+                    start=True,
+                    stop=True,
+                )
+                gate[blk] = shared([P, PACK, P], F32, "gate%d" % blk, "gate_slot%d" % b)
+                nc.scalar.activation(out=gate[blk][:], in_=by_word_slot(bank), func=SIGMOID, scale=-1.0)
 
-        def interpolate(c, b):
-            kinds = ("x", "z") if c >= 1 else ("x", "h")
-            blk = 2 * c + b
-            term[blk] = keep.tile([P, PACK, P], F32, name="term%d" % blk, tag=slot(kinds[b], c + 1), align_bytes=64)
-            nc.vector.tensor_tensor(out=term[blk][:], in0=gate[blk][:], in1=diff[blk][:], op=MULT)
+        def interpolate(c):
+            both = shared([P, 2, PACK, P], F32, "term%d" % c, "x_bf%d" % min(c + 1, LAST))
+            engine = nc.gpsimd if c + 2 <= LAST else nc.vector
+            for b in range(2):
+                blk = 2 * c + b
+                term[blk] = both[:, b]
+                engine.tensor_tensor(out=term[blk], in0=gate[blk][:], in1=e_sb[blk][:], op=MULT)
+
+        def sum_z(c):
+            for blk in (2 * c, 2 * c + 1):
+                parts = (a_sb[blk], term[blk]) if c == LAST else (term[blk], a_sb[blk])
+                z_bf[blk] = two.tile([P, BLOCK, PACK], BF16, name="z_bf", align_bytes=64)
+                summed = transposed_sum("b_bank" if c == LAST else "zg_bank", parts)
+                nc.scalar.copy(out=z_bf[blk][:], in_=summed)
 
         def finish(c):
-            z_bf[c] = keep.tile([P, 2, BLOCK, PACK], BF16, name="z_bf%d" % c, tag=slot("z", c + 2), align_bytes=64)
-            for b in range(2):
-                blk = 2 * c + b
-                z_q = quantize(four, "z", transposed_sum("z", b_sb[blk], term[blk], z_bf[c][:, b]), BLOCK)
-                bank = psum1.tile([P, N // P, BLOCK], F32, name="out_bank")
+            for blk in (2 * c, 2 * c + 1):
+                z_q = quantize_block("z", z_bf[blk][:].rearrange("p j t -> p (j t)"))
+                bank = psum.tile([P, N // P, BLOCK], F32, name="out_bank")
                 for n in range(N // P):
                     nc.tensor.matmul_mx(
                         out=bank[:, n, :],
@@ -303,44 +315,49 @@ def tile_list_pivot_irrigation_kernel(
                         stop=True,
                     )
                 staged = two.tile([P, N // P, BLOCK], F32, name="staged")
-                copier(blk)(out=staged[:], in_=bank[:])
+                copy = nc.vector.tensor_copy if blk == 2 * LAST + 1 else nc.scalar.copy
+                copy(out=staged[:], in_=bank[:])
                 nc.sync.dma_start(
                     out=out.rearrange("(n p) j -> p n j", p=P)[:, :, blk * BLOCK : (blk + 1) * BLOCK], in_=staged[:]
                 )
 
-        for t in range(PACK):
-            pick_first(0, t, "first%d" % (t % 2))
-            add_second(0, t)
-        x0_q = quantize(keep, "x0", x0_bf[:], S, "first1")
+        first_picks(0, (0, 1))
+        second_picks(0, (0, 1))
+        gather_words(0)
+        project_table(0)
+        first_picks(0, (2, 3))
+        second_picks(0, (2, 3))
+        round_probes(0)
+        for a in range(PASSES):
+            codes = shared([P, H], U32, "wp_codes%d" % a, "wp_slot%d" % a)
+            scales = keep.tile([P, H], U8, name="wp_scales%d" % a, align_bytes=64)
+            wp_q[a] = quantize(codes, scales, wp_bf[a][:])
+        project_probes(0)
+        wo_bf = round_weight("wo", wo)
+        for n in range(N // P):
+            codes = keep.tile([P, P], U32, name="wo_codes%d" % n, align_bytes=64)
+            scales = keep.tile([P, P], U8, name="wo_scales%d" % n, align_bytes=64)
+            wo_q[n] = quantize(codes, scales, wo_bf[:, n * K_PASS : (n + 1) * K_PASS])
 
-        for c in range(CHUNKS):
-            gathers = c + 1 < CHUNKS
-            project_probes(c, 0, slot("h", 0) if c == 0 else "x_first")
-            project_probes(c, 1, slot("x", c))
-            if c >= 1:
+        for c in range(1, CHUNKS + 2):
+            if c <= LAST:
+                first_picks(c, (0, 1, 2, 3))
+            if c - 1 <= LAST:
                 difference(c - 1)
-            make_gate(c, 0, "h_first", slot("ga", c + 1))
-            make_gate(c, 1, slot("h", c + 1), slot("gb", c + 1))
+            if c >= 2:
+                interpolate(c - 2)
+            if c - 1 <= LAST:
+                sum_h(c - 1)
+            if c >= 2:
+                sum_z(c - 2)
+            if c <= LAST:
+                second_picks(c, (0, 1, 2, 3))
+                gather_words(c)
+                round_probes(c)
+                project_table(c)
+            if c - 1 <= LAST:
+                make_gate(c - 1)
             if c >= 2:
                 finish(c - 2)
-            if gathers:
-                pick_first(c + 1, 0, slot("h", c))
-                pick_first(c + 1, 1, slot("x", c))
-                add_second(c + 1, 0)
-                pick_first(c + 1, 2, slot("z" if c >= 2 else "h", c))
-                add_second(c + 1, 1)
-                if c == 0:
-                    pick_first(c + 1, 3, slot("x", c))
-                add_second(c + 1, 2)
-            if c >= 1:
-                interpolate(c - 1, 0)
-                if gathers:
-                    pick_first(c + 1, 3, slot("ga", c))
-                interpolate(c - 1, 1)
-            if gathers:
-                add_second(c + 1, 3)
-        difference(CHUNKS - 1)
-        finish(CHUNKS - 2)
-        for b in range(2):
-            interpolate(CHUNKS - 1, b)
-        finish(CHUNKS - 1)
+            if c <= LAST:
+                project_probes(c)

@@ -15,9 +15,9 @@ U8 = mybir.dt.uint8
 FP8X4 = mybir.dt.float8_e4m3fn_x4
 FP4X4 = mybir.dt.float4_e2m1fn_x4
 ADD = mybir.AluOpType.add
-SUB = mybir.AluOpType.subtract
 MULT = mybir.AluOpType.mult
 SIGMOID = mybir.ActivationFunctionType.Sigmoid
+COPY = mybir.ActivationFunctionType.Copy
 
 P = 128
 PACK = 4
@@ -62,10 +62,19 @@ def tile_list_pivot_irrigation_kernel(
             nc.vector.quantize_mx(out=codes[:].bitcast(FP8X4), scales=scales[:], in_=src)
             return codes, scales
 
-        def quantize_block(name, src):
-            codes = four.tile([P, BLOCK], U32, name=name + "_codes", align_bytes=64)
-            scales = four.tile([P, BLOCK], U8, name=name + "_scales", align_bytes=64)
-            return quantize(codes, scales, src)
+        def quantize_chunk(c, codes, scales, src):
+            if c < LAST:
+                return quantize(codes, scales, src.rearrange("p b c -> p (b c)"))
+            words = src.shape[2] // PACK
+            for b in range(2):
+                cols = slice(b * words, (b + 1) * words)
+                nc.vector.quantize_mx(out=codes[:, cols].bitcast(FP8X4), scales=scales[:, cols], in_=src[:, b, :])
+            return codes, scales
+
+        def quantize_sum(name, c, src):
+            codes = two.tile([P, CHUNK], U32, name=name + "_codes", align_bytes=64)
+            scales = two.tile([P, CHUNK], U8, name=name + "_scales", align_bytes=64)
+            return quantize_chunk(c, codes, scales, src.rearrange("p b j t -> p b (j t)"))
 
         def load_plane(a, t):
             plane = keep.tile([P, T], F32, name="plane%d%d" % (a, t))
@@ -75,13 +84,13 @@ def tile_list_pivot_irrigation_kernel(
 
         def round_weight(name, rows):
             width = rows.shape[1]
-            raw = keep.tile([P, PACK, width], F32, name=name + "_raw")
+            raw = shared([P, PACK, width], F32, name + "_raw", name + "_raw")
             nc.sync.dma_start(out=raw[:], in_=rows.rearrange("(p t) c -> p t c", t=PACK))
             grouped = keep.tile([P, PACK * width], BF16, name=name + "_bf", align_bytes=64)
             interleave(grouped[:], raw[:])
             return grouped
 
-        tab_sc = keep.tile([P, T], U8, align_bytes=64)
+        tab_sc = shared([P, T], U8, "tab_sc", "x_slot1")
         nc.gpsimd.memset(tab_sc[:].bitcast(I32), 0)
         wm_sc = keep.tile([P, PASSES * H], U8, align_bytes=64)
         wg_sc = keep.tile([P, H], U8, align_bytes=64)
@@ -126,20 +135,11 @@ def tile_list_pivot_irrigation_kernel(
 
         gather_pass0(0)
         gather_pass0(1)
+        wp_bf = [round_weight("wp0", wp[:K_PASS, :])]
         planes[0, 2] = load_plane(0, 2)
-        for q in range(QUADRANTS):
-            nc.sync.dma_start(
-                out=tab_sc[32 * q : 32 * q + 4 * PASSES, :].bitcast(I32),
-                in_=tab_scales[:, 4 * q : 4 * q + 4, :].bitcast(I32),
-            )
         gather_pass0(2)
         planes[0, 3] = load_plane(0, 3)
-        v_sc0 = keep.tile([P, S], U8, align_bytes=64)
-        nc.vector.tensor_copy(out=v_sc0[:], in_=tab_sc[:].indirect(list1[:]))
-        v_scales = [v_sc0, v_sc1]
-        nc.gpsimd.dma_start(out=v_sc1[0 : P - 4, :].bitcast(I32), in_=v_sc0[4:P, :].bitcast(I32))
         gather_pass0(3)
-        wp_bf = [round_weight("wp%d" % a, wp[a * K_PASS : (a + 1) * K_PASS, :]) for a in range(PASSES)]
 
         planes[1, 0] = load_plane(1, 0)
         planes[1, 1] = load_plane(1, 1)
@@ -149,8 +149,13 @@ def tile_list_pivot_irrigation_kernel(
             nc.sync.dma_start(out=tab[:].bitcast(I32), in_=tab_words[a].rearrange("p c t -> p (c t)").bitcast(I32))
             tabs.append(tab)
         planes[1, 2] = load_plane(1, 2)
+        for q in range(QUADRANTS):
+            nc.sync.dma_start(
+                out=tab_sc[32 * q : 32 * q + 4 * PASSES, :].bitcast(I32),
+                in_=tab_scales[:, 4 * q : 4 * q + 4, :].bitcast(I32),
+            )
         planes[1, 3] = load_plane(1, 3)
-
+        wp_bf.append(round_weight("wp1", wp[K_PASS:, :]))
         wm = keep.tile([P, PASSES, 2 * H], U8, align_bytes=64)
         nc.sync.dma_start(out=wm[:].bitcast(I32), in_=wm_words.bitcast(I32).rearrange("a p c -> p a c"))
         for q in range(QUADRANTS):
@@ -166,34 +171,35 @@ def tile_list_pivot_irrigation_kernel(
         wg = keep.tile([P, H], U32, align_bytes=64)
         nc.sync.dma_start(out=wg[:].bitcast(I32), in_=wg_words[0].rearrange("p c t -> p (c t)").bitcast(I32))
 
-        x_bf = [shared([P, PASSES, PACK * CHUNK], BF16, "x_bf%d" % c, "x_bf%d" % c) for c in range(CHUNKS)]
+        x_bf = [shared([P, PASSES * PACK * CHUNK], BF16, "x_bf%d" % c, "x_bf%d" % c) for c in range(CHUNKS)]
         for c in range(CHUNKS):
             bank = psum.tile([P, 2, 2, BLOCK], F32, name="back_bank", tag="b_bank")
             for b in range(2):
                 for u in range(2):
                     pairs = x0_turned[c][:, b, u].rearrange("j p e -> j (p e)").bitcast(F32)
                     nc.tensor.transpose(out=bank[:, b, u, :], in_=pairs, identity=ident[:])
-            words = x_bf[c][:, 0, :].bitcast(F32)
+            words = x_bf[c][:, : PACK * CHUNK].bitcast(F32)
             nc.scalar.copy(
                 out=words.rearrange("p (b j u) -> p b j u", b=2, u=2), in_=bank[:].rearrange("p b u j -> p b j u")
             )
 
-        x1, v_codes, picks, b_bank, a_sb, e_sb, h_bf, gate, term, z_bf, wp_q, wo_q = ({} for name in range(12))
+        x1, v_codes, picks, b_bank, twice_a, e_sb, h_bf, gate, term, z_bf, z_q, wp_q, wo_q, x1_bf = ({} for name in range(14))
+
+        def open_chunk(c):
+            x1[c] = shared([P, PACK, CHUNK], F32, "x1_%d" % c, "x_slot%d" % ((c + 1) % 2))
 
         def first_picks(c, ts):
             if 0 in ts:
-                three = shared([P, 3, CHUNK], F32, "picks%d" % c, "x_slot%d" % (c % 2))
-                picks[0], picks[1], picks[3] = three[:, 0, :], three[:, 1, :], three[:, 2, :]
-            if 2 in ts:
-                picks[2] = shared([P, CHUNK], F32, "pick%d_2" % c, "wp_slot0" if c == 0 else "word_slot")[:]
-                if c == 0:
-                    picks[3] = shared([P, CHUNK], F32, "pick0_3", "wp_slot1")[:]
+                row = shared([P, PACK, CHUNK], F32, "picks%d" % c, "x_slot%d" % (c % 2))
+                picks.update({t: row[:, t, :] for t in range(PACK)})
+            if 2 in ts and c == 0:
+                picks.update({t: shared([P, CHUNK], F32, "pick0_%d" % t, "wp_slot%d" % (t - 2))[:] for t in ts})
+            elif 2 in ts:
+                picks[2] = shared([P, CHUNK], F32, "pick%d_2" % c, "word_slot")[:]
             for t in ts:
                 nc.vector.tensor_copy(out=picks[t], in_=planes[1, t][:].indirect(entries(list2, c)))
 
         def second_picks(c, ts):
-            if 0 in ts:
-                x1[c] = shared([P, PACK, CHUNK], F32, "x1_%d" % c, "x_slot%d" % ((c + 1) % 2))
             for t in ts:
                 nc.vector.tensor_tensor(
                     out=x1[c][:, t, :], in0=planes[1, t][:].indirect(entries(list3, c)), in1=picks[t], op=ADD
@@ -218,16 +224,22 @@ def tile_list_pivot_irrigation_kernel(
                         start=(a == 0),
                         stop=(a == PASSES - 1),
                     )
-                a_sb[blk] = four.tile([P, PACK, P], F32, name="a_sb")
-                nc.scalar.copy(out=a_sb[blk][:], in_=by_word_slot(bank))
+                twice_a[blk] = four.tile([P, PACK, P], F32, name="twice_a")
+                nc.scalar.activation(out=twice_a[blk][:], in_=by_word_slot(bank), func=COPY, scale=2.0)
 
         def round_probes(c):
-            interleave(x_bf[c][:, 1, :], x1[c][:])
+            x1_bf[c] = x_bf[c][:, PACK * CHUNK :] if c else shared([P, PACK * CHUNK], BF16, "x1_bf0", "wp1_raw")[:]
+            width = BLOCK if c == LAST else CHUNK
+            for first in range(0, CHUNK, width):
+                interleave(x1_bf[c][:, PACK * first : PACK * (first + width)], x1[c][:, :, first : first + width])
 
         def project_probes(c):
             codes = shared([P, PASSES * CHUNK], U32, "x_codes%d" % c, "x_slot%d" % (c % 2))
             scales = shared([P, PASSES * CHUNK], U8, "x_scales%d" % c, "x_scales_slot")
-            quantize(codes, scales, x_bf[c][:].rearrange("p a c -> p (a c)"))
+            cuts = {0: (0, CHUNK, 2 * CHUNK), LAST: (0, CHUNK, CHUNK + BLOCK, 2 * CHUNK)}.get(c, (0, 2 * CHUNK))
+            for lo, hi in zip(cuts, cuts[1:]):
+                src = x_bf[c][:, PACK * lo : PACK * hi] if c or lo < CHUNK else x1_bf[c]
+                nc.vector.quantize_mx(out=codes[:, lo:hi].bitcast(FP8X4), scales=scales[:, lo:hi], in_=src)
             for b in range(2):
                 blk = 2 * c + b
                 b_bank[blk] = psum.tile([P, H], F32, name="b_bank", tag="b_bank")
@@ -259,75 +271,94 @@ def tile_list_pivot_irrigation_kernel(
 
         def difference(c):
             for blk in (2 * c, 2 * c + 1):
-                e_sb[blk] = four.tile([P, PACK, P], F32, name="e_sb")
-                nc.vector.tensor_tensor(out=e_sb[blk][:], in0=by_word_slot(b_bank[blk]), in1=a_sb[blk][:], op=SUB)
+                e_sb[blk] = shared([P, PACK, P], F32, "e_sb%d" % blk, "e_slot%d" % (blk % 4))
+                nc.vector.scalar_tensor_tensor(
+                    out=e_sb[blk][:], in0=twice_a[blk][:], scalar=-0.5, in1=by_word_slot(b_bank[blk]), op0=MULT, op1=ADD
+                )
 
         def sum_h(c):
-            for blk in (2 * c, 2 * c + 1):
-                parts = (a_sb[blk], a_sb[blk], e_sb[blk])
-                h_bf[blk] = two.tile([P, BLOCK, PACK], BF16, name="h_bf", align_bytes=64)
-                nc.scalar.copy(out=h_bf[blk][:], in_=transposed_sum("ha_bank", parts))
+            for b in range(2):
+                blk = 2 * c + b
+                h_bf[blk] = shared([P, PACK * BLOCK], BF16, "h_bf%d" % blk, "h_slot%d" % b)[:]
+                summed = transposed_sum("ha_bank", (twice_a[blk], e_sb[blk]))
+                nc.scalar.copy(out=h_bf[blk].rearrange("p (j t) -> p j t", t=PACK), in_=summed)
 
         def make_gate(c):
             for b in range(2):
                 blk = 2 * c + b
-                h_q = quantize_block("h", h_bf[blk][:].rearrange("p j t -> p (j t)"))
-                bank = psum.tile([P, H], F32, name="gate_bank", tag="zg_bank")
+                codes = two.tile([P, BLOCK], U32, name="h_codes", align_bytes=64)
+                scales = two.tile([P, BLOCK], U8, name="h_scales", align_bytes=64)
+                quantize(codes, scales, h_bf[blk])
+                bank = psum.tile([P, H], F32, name="gate_bank", tag="ha_bank" if c == LAST else "zg_bank")
                 nc.tensor.matmul_mx(
                     out=bank[:],
-                    lhsT=h_q[0][:].bitcast(FP8X4),
-                    lhsT_scale=h_q[1][:],
+                    lhsT=codes[:].bitcast(FP8X4),
+                    lhsT_scale=scales[:],
                     rhs=wg[:].bitcast(FP8X4),
                     rhs_scale=wg_sc[:],
                     start=True,
                     stop=True,
                 )
-                gate[blk] = shared([P, PACK, P], F32, "gate%d" % blk, "gate_slot%d" % b)
+                gate[blk] = shared([P, PACK, P], F32, "gate%d" % blk, "gate_slot%d" % (blk % 4))
                 nc.scalar.activation(out=gate[blk][:], in_=by_word_slot(bank), func=SIGMOID, scale=-1.0)
 
         def interpolate(c):
-            both = shared([P, 2, PACK, P], F32, "term%d" % c, "x_bf%d" % min(c + 1, LAST))
-            engine = nc.gpsimd if c + 2 <= LAST else nc.vector
+            both = shared([P, 2, PACK, P], F32, "term%d" % c, "x_bf%d" % ((c + 1) % LAST))
             for b in range(2):
                 blk = 2 * c + b
                 term[blk] = both[:, b]
-                engine.tensor_tensor(out=term[blk], in0=gate[blk][:], in1=e_sb[blk][:], op=MULT)
+                if c + 2 <= LAST:
+                    nc.gpsimd.tensor_tensor(out=term[blk], in0=gate[blk][:], in1=e_sb[blk][:], op=MULT)
+                else:
+                    nc.vector.scalar_tensor_tensor(
+                        out=term[blk], in0=gate[blk][:], scalar=2.0, in1=e_sb[blk][:], op0=MULT, op1=MULT
+                    )
 
         def sum_z(c):
-            for blk in (2 * c, 2 * c + 1):
-                parts = (a_sb[blk], term[blk]) if c == LAST else (term[blk], a_sb[blk])
-                z_bf[blk] = two.tile([P, BLOCK, PACK], BF16, name="z_bf", align_bytes=64)
+            z_bf[c] = shared([P, 2, BLOCK, PACK], BF16, "z_bf%d" % c, "z_slot%d" % (c % 2))[:]
+            for b in range(2):
+                blk = 2 * c + b
+                parts = (twice_a[blk], term[blk]) + ((term[blk],) if c + 2 <= LAST else ())
                 summed = transposed_sum("b_bank" if c == LAST else "zg_bank", parts)
-                nc.scalar.copy(out=z_bf[blk][:], in_=summed)
+                nc.scalar.activation(out=z_bf[c][:, b], in_=summed, func=COPY, scale=0.5)
+
+        def quantize_z(c):
+            z_q[c] = quantize_sum("z", c, z_bf[c])
 
         def finish(c):
-            for blk in (2 * c, 2 * c + 1):
-                z_q = quantize_block("z", z_bf[blk][:].rearrange("p j t -> p (j t)"))
+            codes, scales = z_q[c]
+            for b in range(2):
+                blk = 2 * c + b
+                cols = slice(b * BLOCK, (b + 1) * BLOCK)
                 bank = psum.tile([P, N // P, BLOCK], F32, name="out_bank")
                 for n in range(N // P):
                     nc.tensor.matmul_mx(
                         out=bank[:, n, :],
                         lhsT=wo_q[n][0][:].bitcast(FP8X4),
                         lhsT_scale=wo_q[n][1][:],
-                        rhs=z_q[0][:].bitcast(FP8X4),
-                        rhs_scale=z_q[1][:],
+                        rhs=codes[:, cols].bitcast(FP8X4),
+                        rhs_scale=scales[:, cols],
                         start=True,
                         stop=True,
                     )
-                staged = two.tile([P, N // P, BLOCK], F32, name="staged")
-                copy = nc.vector.tensor_copy if blk == 2 * LAST + 1 else nc.scalar.copy
+                staged = four.tile([P, N // P, BLOCK], F32, name="staged")
+                copy = nc.vector.tensor_copy if c >= LAST - 1 and blk != 2 * LAST else nc.scalar.copy
                 copy(out=staged[:], in_=bank[:])
                 nc.sync.dma_start(
                     out=out.rearrange("(n p) j -> p n j", p=P)[:, :, blk * BLOCK : (blk + 1) * BLOCK], in_=staged[:]
                 )
 
         first_picks(0, (0, 1))
-        second_picks(0, (0, 1))
         gather_words(0)
-        project_table(0)
         first_picks(0, (2, 3))
-        second_picks(0, (2, 3))
+        v_sc0 = keep.tile([P, S], U8, align_bytes=64)
+        nc.vector.tensor_copy(out=v_sc0[:], in_=tab_sc[:].indirect(list1[:]))
+        v_scales = [v_sc0, v_sc1]
+        nc.scalar.dma_start(out=v_sc1[0 : P - 4, :].bitcast(I32), in_=v_sc0[4:P, :].bitcast(I32))
+        open_chunk(0)
+        second_picks(0, (0, 1, 2, 3))
         round_probes(0)
+        project_table(0)
         for a in range(PASSES):
             codes = shared([P, H], U32, "wp_codes%d" % a, "wp_slot%d" % a)
             scales = keep.tile([P, H], U8, name="wp_scales%d" % a, align_bytes=64)
@@ -339,25 +370,36 @@ def tile_list_pivot_irrigation_kernel(
             scales = keep.tile([P, P], U8, name="wo_scales%d" % n, align_bytes=64)
             wo_q[n] = quantize(codes, scales, wo_bf[:, n * K_PASS : (n + 1) * K_PASS])
 
-        for c in range(1, CHUNKS + 2):
-            if c <= LAST:
-                first_picks(c, (0, 1, 2, 3))
-            if c - 1 <= LAST:
-                difference(c - 1)
+        for c in range(1, CHUNKS):
+            first_picks(c, (0, 1, 2, 3))
             if c >= 2:
                 interpolate(c - 2)
-            if c - 1 <= LAST:
-                sum_h(c - 1)
+            difference(c - 1)
+            open_chunk(c)
+            sum_h(c - 1)
             if c >= 2:
                 sum_z(c - 2)
-            if c <= LAST:
-                second_picks(c, (0, 1, 2, 3))
-                gather_words(c)
-                round_probes(c)
-                project_table(c)
-            if c - 1 <= LAST:
-                make_gate(c - 1)
-            if c >= 2:
-                finish(c - 2)
-            if c <= LAST:
+            second_picks(c, (0, 1, 2, 3))
+            gather_words(c)
+            round_probes(c)
+            project_table(c)
+            if c == LAST:
                 project_probes(c)
+            make_gate(c - 1)
+            if c >= 2:
+                quantize_z(c - 2)
+                finish(c - 2)
+            if c < LAST:
+                project_probes(c)
+
+        difference(LAST)
+        sum_h(LAST)
+        make_gate(LAST)
+        interpolate(LAST - 1)
+        sum_z(LAST - 1)
+        interpolate(LAST)
+        sum_z(LAST)
+        quantize_z(LAST - 1)
+        finish(LAST - 1)
+        quantize_z(LAST)
+        finish(LAST)

@@ -15,9 +15,9 @@ U8 = mybir.dt.uint8
 FP8X4 = mybir.dt.float8_e4m3fn_x4
 FP4X4 = mybir.dt.float4_e2m1fn_x4
 ADD = mybir.AluOpType.add
+SUB = mybir.AluOpType.subtract
 MULT = mybir.AluOpType.mult
 SIGMOID = mybir.ActivationFunctionType.Sigmoid
-COPY = mybir.ActivationFunctionType.Copy
 
 P = 128
 PACK = 4
@@ -183,7 +183,7 @@ def tile_list_pivot_irrigation_kernel(
                 out=words.rearrange("p (b j u) -> p b j u", b=2, u=2), in_=bank[:].rearrange("p b u j -> p b j u")
             )
 
-        x1, v_codes, picks, b_bank, twice_a, e_sb, h_bf, gate, term, z_bf, z_q, wp_q, wo_q, x1_bf = ({} for name in range(14))
+        x1, v_codes, picks, b_bank, a_sb, e_sb, h_bf, gate, term, z_bf, z_q, wp_q, wo_q, x1_bf = ({} for name in range(14))
 
         def open_chunk(c):
             x1[c] = shared([P, PACK, CHUNK], F32, "x1_%d" % c, "x_slot%d" % ((c + 1) % 2))
@@ -224,8 +224,8 @@ def tile_list_pivot_irrigation_kernel(
                         start=(a == 0),
                         stop=(a == PASSES - 1),
                     )
-                twice_a[blk] = four.tile([P, PACK, P], F32, name="twice_a")
-                nc.scalar.activation(out=twice_a[blk][:], in_=by_word_slot(bank), func=COPY, scale=2.0)
+                a_sb[blk] = four.tile([P, PACK, P], F32, name="a_sb")
+                nc.scalar.copy(out=a_sb[blk][:], in_=by_word_slot(bank))
 
         def round_probes(c):
             x1_bf[c] = x_bf[c][:, PACK * CHUNK :] if c else shared([P, PACK * CHUNK], BF16, "x1_bf0", "wp1_raw")[:]
@@ -272,15 +272,13 @@ def tile_list_pivot_irrigation_kernel(
         def difference(c):
             for blk in (2 * c, 2 * c + 1):
                 e_sb[blk] = shared([P, PACK, P], F32, "e_sb%d" % blk, "e_slot%d" % (blk % 4))
-                nc.vector.scalar_tensor_tensor(
-                    out=e_sb[blk][:], in0=twice_a[blk][:], scalar=-0.5, in1=by_word_slot(b_bank[blk]), op0=MULT, op1=ADD
-                )
+                nc.vector.tensor_tensor(out=e_sb[blk][:], in0=by_word_slot(b_bank[blk]), in1=a_sb[blk][:], op=SUB)
 
         def sum_h(c):
             for b in range(2):
                 blk = 2 * c + b
                 h_bf[blk] = shared([P, PACK * BLOCK], BF16, "h_bf%d" % blk, "h_slot%d" % b)[:]
-                summed = transposed_sum("ha_bank", (twice_a[blk], e_sb[blk]))
+                summed = transposed_sum("ha_bank", (a_sb[blk], a_sb[blk], e_sb[blk]))
                 nc.scalar.copy(out=h_bf[blk].rearrange("p (j t) -> p j t", t=PACK), in_=summed)
 
         def make_gate(c):
@@ -307,20 +305,16 @@ def tile_list_pivot_irrigation_kernel(
             for b in range(2):
                 blk = 2 * c + b
                 term[blk] = both[:, b]
-                if c + 2 <= LAST:
-                    nc.gpsimd.tensor_tensor(out=term[blk], in0=gate[blk][:], in1=e_sb[blk][:], op=MULT)
-                else:
-                    nc.vector.scalar_tensor_tensor(
-                        out=term[blk], in0=gate[blk][:], scalar=2.0, in1=e_sb[blk][:], op0=MULT, op1=MULT
-                    )
+                engine = nc.gpsimd if c + 2 <= LAST else nc.vector
+                engine.tensor_tensor(out=term[blk], in0=gate[blk][:], in1=e_sb[blk][:], op=MULT)
 
         def sum_z(c):
             z_bf[c] = shared([P, 2, BLOCK, PACK], BF16, "z_bf%d" % c, "z_slot%d" % (c % 2))[:]
             for b in range(2):
                 blk = 2 * c + b
-                parts = (twice_a[blk], term[blk]) + ((term[blk],) if c + 2 <= LAST else ())
+                parts = (a_sb[blk], term[blk])
                 summed = transposed_sum("b_bank" if c == LAST else "zg_bank", parts)
-                nc.scalar.activation(out=z_bf[c][:, b], in_=summed, func=COPY, scale=0.5)
+                nc.scalar.copy(out=z_bf[c][:, b], in_=summed)
 
         def quantize_z(c):
             z_q[c] = quantize_sum("z", c, z_bf[c])

@@ -305,8 +305,7 @@ def tile_list_pivot_irrigation_kernel(
             for b in range(2):
                 blk = 2 * c + b
                 term[blk] = both[:, b]
-                engine = nc.gpsimd if c + 2 <= LAST else nc.vector
-                engine.tensor_tensor(out=term[blk], in0=gate[blk][:], in1=e_sb[blk][:], op=MULT)
+                nc.vector.tensor_tensor(out=term[blk], in0=gate[blk][:], in1=e_sb[blk][:], op=MULT)
 
         def sum_z(c):
             z_bf[c] = shared([P, 2, BLOCK, PACK], BF16, "z_bf%d" % c, "z_slot%d" % (c % 2))[:]

@@ -183,10 +183,12 @@ def tile_list_pivot_irrigation_kernel(
                 out=words.rearrange("p (b j u) -> p b j u", b=2, u=2), in_=bank[:].rearrange("p b u j -> p b j u")
             )
 
-        x1, v_codes, picks, b_bank, a_sb, e_sb, h_bf, gate, term, z_bf, z_q, wp_q, wo_q, x1_bf = ({} for name in range(14))
+        x1, v_codes, picks, b_sb, a_sb, e_sb, h_bf, gate, term, z_bf, z_q, wp_q, wo_q, x1_bf = ({} for name in range(14))
 
         def open_chunk(c):
-            x1[c] = shared([P, PACK, CHUNK], F32, "x1_%d" % c, "x_slot%d" % ((c + 1) % 2))
+            row = shared([P, PACK * CHUNK], F32, "x1_%d" % c, "x_slot%d" % ((c + 1) % 2))
+            x1[c] = row[:].rearrange("p (t j) -> p t j", t=PACK)
+            h_bf[c - 1] = row[:, 2 * CHUNK :].bitcast(BF16)
 
         def first_picks(c, ts):
             if 0 in ts:
@@ -194,8 +196,6 @@ def tile_list_pivot_irrigation_kernel(
                 picks.update({t: row[:, t, :] for t in range(PACK)})
             if 2 in ts and c == 0:
                 picks.update({t: shared([P, CHUNK], F32, "pick0_%d" % t, "wp_slot%d" % (t - 2))[:] for t in ts})
-            elif 2 in ts:
-                picks[2] = shared([P, CHUNK], F32, "pick%d_2" % c, "word_slot")[:]
             for t in ts:
                 nc.vector.tensor_copy(out=picks[t], in_=planes[1, t][:].indirect(entries(list2, c)))
 
@@ -224,8 +224,9 @@ def tile_list_pivot_irrigation_kernel(
                         start=(a == 0),
                         stop=(a == PASSES - 1),
                     )
-                a_sb[blk] = four.tile([P, PACK, P], F32, name="a_sb")
-                nc.scalar.copy(out=a_sb[blk][:], in_=by_word_slot(bank))
+                if b == 0:
+                    a_sb[c] = two.tile([P, 2, PACK, P], F32, name="a_sb")
+                nc.scalar.copy(out=a_sb[c][:, b], in_=by_word_slot(bank))
 
         def round_probes(c):
             x1_bf[c] = x_bf[c][:, PACK * CHUNK :] if c else shared([P, PACK * CHUNK], BF16, "x1_bf0", "wp1_raw")[:]
@@ -234,7 +235,7 @@ def tile_list_pivot_irrigation_kernel(
                 interleave(x1_bf[c][:, PACK * first : PACK * (first + width)], x1[c][:, :, first : first + width])
 
         def project_probes(c):
-            codes = shared([P, PASSES * CHUNK], U32, "x_codes%d" % c, "x_slot%d" % (c % 2))
+            codes = shared([P, PASSES * CHUNK], U32, "x_codes%d" % c, "x_last" if c == LAST else "x_slot%d" % (c % 2))
             scales = shared([P, PASSES * CHUNK], U8, "x_scales%d" % c, "x_scales_slot")
             cuts = {0: (0, CHUNK, 2 * CHUNK), LAST: (0, CHUNK, CHUNK + BLOCK, 2 * CHUNK)}.get(c, (0, 2 * CHUNK))
             for lo, hi in zip(cuts, cuts[1:]):
@@ -242,11 +243,11 @@ def tile_list_pivot_irrigation_kernel(
                 nc.vector.quantize_mx(out=codes[:, lo:hi].bitcast(FP8X4), scales=scales[:, lo:hi], in_=src)
             for b in range(2):
                 blk = 2 * c + b
-                b_bank[blk] = psum.tile([P, H], F32, name="b_bank", tag="b_bank")
+                bank = psum.tile([P, H], F32, name="b_bank", tag="b_bank")
                 for a in range(PASSES):
                     cols = slice(a * CHUNK + b * BLOCK, a * CHUNK + (b + 1) * BLOCK)
                     nc.tensor.matmul_mx(
-                        out=b_bank[blk][:],
+                        out=bank[:],
                         lhsT=codes[:, cols].bitcast(FP8X4),
                         lhsT_scale=scales[:, cols],
                         rhs=wp_q[a][0][:].bitcast(FP8X4),
@@ -254,6 +255,13 @@ def tile_list_pivot_irrigation_kernel(
                         start=(a == 0),
                         stop=(a == PASSES - 1),
                     )
+                if b == 0:
+                    b_sb[c] = two.tile([P, 2, PACK, P], F32, name="b_sb")
+                for ts in halves(c):
+                    nc.scalar.copy(out=b_sb[c][:, b, ts], in_=by_word_slot(bank)[:, ts])
+
+        def halves(c):
+            return (slice(0, 2), slice(2, PACK)) if c == LAST else (slice(0, PACK),)
 
         def transposed_sum(tag, parts):
             bank = psum.tile([P, PACK, BLOCK], F32, name="sum_bank", tag=tag)
@@ -269,50 +277,56 @@ def tile_list_pivot_irrigation_kernel(
                     )
             return bank[:].rearrange("p t j -> p j t")
 
+        def elementwise(c, out, in0, in1, op):
+            for part in ((0, 1), (1, 2)) if c == LAST else ((0, 2),):
+                blocks = slice(*part)
+                nc.vector.tensor_tensor(out=out[:, blocks], in0=in0[:, blocks], in1=in1[:, blocks], op=op)
+
         def difference(c):
-            for blk in (2 * c, 2 * c + 1):
-                e_sb[blk] = shared([P, PACK, P], F32, "e_sb%d" % blk, "e_slot%d" % (blk % 4))
-                nc.vector.tensor_tensor(out=e_sb[blk][:], in0=by_word_slot(b_bank[blk]), in1=a_sb[blk][:], op=SUB)
+            e_sb[c] = keep.tile([P, 2, PACK, P], F32, name="diff")
+            elementwise(c, e_sb[c], a_sb[c], b_sb[c], SUB)
 
         def sum_h(c):
+            if c == LAST:
+                h_bf[c] = keep.tile([P, PACK * CHUNK], BF16, name="h_last", align_bytes=64)[:]
             for b in range(2):
-                blk = 2 * c + b
-                h_bf[blk] = shared([P, PACK * BLOCK], BF16, "h_bf%d" % blk, "h_slot%d" % b)[:]
-                summed = transposed_sum("ha_bank", (a_sb[blk], a_sb[blk], e_sb[blk]))
-                nc.scalar.copy(out=h_bf[blk].rearrange("p (j t) -> p j t", t=PACK), in_=summed)
+                summed = transposed_sum("ha_bank", (a_sb[c][:, b], b_sb[c][:, b]))
+                rounded = h_bf[c][:, b * PACK * BLOCK : (b + 1) * PACK * BLOCK]
+                nc.scalar.copy(out=rounded.rearrange("p (j t) -> p j t", t=PACK), in_=summed)
 
         def make_gate(c):
+            codes = shared([P, CHUNK], U32, "h_codes%d" % c, "word_slot")
+            scales = two.tile([P, CHUNK], U8, name="h_scales", align_bytes=64)
+            quantize_chunk(c, codes, scales, h_bf[c].rearrange("p (b c) -> p b c", b=2))
+            gate[c] = two.tile([P, 2, PACK, P], F32, name="gate")
             for b in range(2):
-                blk = 2 * c + b
-                codes = two.tile([P, BLOCK], U32, name="h_codes", align_bytes=64)
-                scales = two.tile([P, BLOCK], U8, name="h_scales", align_bytes=64)
-                quantize(codes, scales, h_bf[blk])
+                cols = slice(b * BLOCK, (b + 1) * BLOCK)
                 bank = psum.tile([P, H], F32, name="gate_bank", tag="ha_bank" if c == LAST else "zg_bank")
                 nc.tensor.matmul_mx(
                     out=bank[:],
-                    lhsT=codes[:].bitcast(FP8X4),
-                    lhsT_scale=scales[:],
+                    lhsT=codes[:, cols].bitcast(FP8X4),
+                    lhsT_scale=scales[:, cols],
                     rhs=wg[:].bitcast(FP8X4),
                     rhs_scale=wg_sc[:],
                     start=True,
                     stop=True,
                 )
-                gate[blk] = shared([P, PACK, P], F32, "gate%d" % blk, "gate_slot%d" % (blk % 4))
-                nc.scalar.activation(out=gate[blk][:], in_=by_word_slot(bank), func=SIGMOID, scale=-1.0)
+                for ts in halves(c):
+                    nc.scalar.activation(out=gate[c][:, b, ts], in_=by_word_slot(bank)[:, ts], func=SIGMOID)
 
         def interpolate(c):
-            both = shared([P, 2, PACK, P], F32, "term%d" % c, "x_bf%d" % ((c + 1) % LAST))
+            term[c] = two.tile([P, 2, PACK, P], F32, name="term")
+            if c < LAST:
+                nc.vector.tensor_tensor(out=term[c][:], in0=gate[c][:], in1=e_sb[c][:], op=MULT)
+                return
             for b in range(2):
-                blk = 2 * c + b
-                term[blk] = both[:, b]
-                nc.vector.tensor_tensor(out=term[blk], in0=gate[blk][:], in1=e_sb[blk][:], op=MULT)
+                for ts in halves(c):
+                    nc.vector.tensor_tensor(out=term[c][:, b, ts], in0=gate[c][:, b, ts], in1=e_sb[c][:, b, ts], op=MULT)
 
         def sum_z(c):
             z_bf[c] = shared([P, 2, BLOCK, PACK], BF16, "z_bf%d" % c, "z_slot%d" % (c % 2))[:]
             for b in range(2):
-                blk = 2 * c + b
-                parts = (a_sb[blk], term[blk])
-                summed = transposed_sum("b_bank" if c == LAST else "zg_bank", parts)
+                summed = transposed_sum("b_bank" if c == LAST else "zg_bank", (b_sb[c][:, b], term[c][:, b]))
                 nc.scalar.copy(out=z_bf[c][:, b], in_=summed)
 
         def quantize_z(c):
@@ -365,31 +379,28 @@ def tile_list_pivot_irrigation_kernel(
 
         for c in range(1, CHUNKS):
             first_picks(c, (0, 1, 2, 3))
-            if c >= 2:
-                interpolate(c - 2)
-            difference(c - 1)
             open_chunk(c)
+            second_picks(c, (0, 1))
             sum_h(c - 1)
-            if c >= 2:
-                sum_z(c - 2)
-            second_picks(c, (0, 1, 2, 3))
-            gather_words(c)
-            round_probes(c)
-            project_table(c)
-            if c == LAST:
-                project_probes(c)
+            difference(c - 1)
             make_gate(c - 1)
             if c >= 2:
                 quantize_z(c - 2)
+            second_picks(c, (2, 3))
+            gather_words(c)
+            round_probes(c)
+            interpolate(c - 1)
+            project_table(c)
+            project_probes(c)
+            if c >= 2:
                 finish(c - 2)
             if c < LAST:
-                project_probes(c)
+                sum_z(c - 1)
 
-        difference(LAST)
         sum_h(LAST)
         make_gate(LAST)
-        interpolate(LAST - 1)
         sum_z(LAST - 1)
+        difference(LAST)
         interpolate(LAST)
         sum_z(LAST)
         quantize_z(LAST - 1)

@@ -39,6 +39,14 @@ def by_word_slot(bank):
     return bank[:].rearrange("j (p t) -> j t p", t=PACK)
 
 
+def by_token(row):
+    return row.rearrange("p (j t) -> p j t", t=PACK)
+
+
+def by_slot(row):
+    return row.rearrange("j (t p) -> j t p", t=PACK)
+
+
 def tile_list_pivot_irrigation_kernel(
     tc, tab_words, tab_scales, offs, xT, offs2, offs3, wm_words, wm_scales, wp, wg_words, wg_scales, wo, out
 ):
@@ -72,7 +80,7 @@ def tile_list_pivot_irrigation_kernel(
             return codes, scales
 
         def quantize_sum(name, c, src):
-            codes = two.tile([P, CHUNK], U32, name=name + "_codes", align_bytes=64)
+            codes = shared([P, CHUNK], U32, "z_codes%d" % c, "x_slot0" if c == LAST - 2 else "z_codes%d" % (c % 2))
             scales = two.tile([P, CHUNK], U8, name=name + "_scales", align_bytes=64)
             return quantize_chunk(c, codes, scales, src.rearrange("p b j t -> p b (j t)"))
 
@@ -82,12 +90,18 @@ def tile_list_pivot_irrigation_kernel(
             nc.sync.dma_start(out=plane[:], in_=rows[:, t, :])
             return plane
 
-        def round_weight(name, rows):
+        def round_weight(name, rows, dealt=False):
             width = rows.shape[1]
             raw = shared([P, PACK, width], F32, name + "_raw", name + "_raw")
             nc.sync.dma_start(out=raw[:], in_=rows.rearrange("(p t) c -> p t c", t=PACK))
             grouped = keep.tile([P, PACK * width], BF16, name=name + "_bf", align_bytes=64)
-            interleave(grouped[:], raw[:])
+            if dealt:
+                nc.scalar.copy(
+                    out=grouped[:].rearrange("p (t m j) -> p m t j", t=PACK, j=PACK),
+                    in_=raw[:].rearrange("p j (m t) -> p m t j", t=PACK),
+                )
+            else:
+                interleave(grouped[:], raw[:])
             return grouped
 
         tab_sc = shared([P, T], U8, "tab_sc", "x_slot1")
@@ -135,7 +149,7 @@ def tile_list_pivot_irrigation_kernel(
 
         gather_pass0(0)
         gather_pass0(1)
-        wp_bf = [round_weight("wp0", wp[:K_PASS, :])]
+        wp_bf = [round_weight("wp0", wp[:K_PASS, :], dealt=True)]
         planes[0, 2] = load_plane(0, 2)
         gather_pass0(2)
         planes[0, 3] = load_plane(0, 3)
@@ -155,7 +169,7 @@ def tile_list_pivot_irrigation_kernel(
                 in_=tab_scales[:, 4 * q : 4 * q + 4, :].bitcast(I32),
             )
         planes[1, 3] = load_plane(1, 3)
-        wp_bf.append(round_weight("wp1", wp[K_PASS:, :]))
+        wp_bf.append(round_weight("wp1", wp[K_PASS:, :], dealt=True))
         wm = keep.tile([P, PASSES, 2 * H], U8, align_bytes=64)
         nc.sync.dma_start(out=wm[:].bitcast(I32), in_=wm_words.bitcast(I32).rearrange("a p c -> p a c"))
         for q in range(QUADRANTS):
@@ -183,7 +197,7 @@ def tile_list_pivot_irrigation_kernel(
                 out=words.rearrange("p (b j u) -> p b j u", b=2, u=2), in_=bank[:].rearrange("p b u j -> p b j u")
             )
 
-        x1, v_codes, picks, b_sb, a_sb, e_sb, h_bf, gate, term, z_bf, z_q, wp_q, wo_q, x1_bf = ({} for name in range(14))
+        x1, v_codes, picks, b_sb, a_sb, diff, h_bf, gate, term, z_bf, z_q, wp_q, wo_q, x1_bf = ({} for name in range(14))
 
         def open_chunk(c):
             row = shared([P, PACK * CHUNK], F32, "x1_%d" % c, "x_slot%d" % ((c + 1) % 2))
@@ -206,14 +220,14 @@ def tile_list_pivot_irrigation_kernel(
                 )
 
         def gather_words(c):
-            v_codes[c] = shared([P, PASSES, CHUNK], U32, "v_codes%d" % c, "word_slot")
+            v_codes[c] = shared([P, PASSES, CHUNK], U32, "v_codes%d" % c, "x_last" if c == LAST else "word_slot")
             for a in range(PASSES):
                 nc.vector.tensor_copy(out=v_codes[c][:, a, :], in_=tabs[a][:].indirect(entries(list1, c)))
 
         def project_table(c):
             for b in range(2):
                 blk = 2 * c + b
-                bank = psum.tile([P, H], F32, name="a_bank", tag="ha_bank")
+                bank = psum.tile([P, H], F32, name="a_bank", tag="out_bank" if c == LAST else "ha_bank")
                 for a in range(PASSES):
                     nc.tensor.matmul_mx(
                         out=bank[:],
@@ -225,8 +239,8 @@ def tile_list_pivot_irrigation_kernel(
                         stop=(a == PASSES - 1),
                     )
                 if b == 0:
-                    a_sb[c] = two.tile([P, 2, PACK, P], F32, name="a_sb")
-                nc.scalar.copy(out=a_sb[c][:, b], in_=by_word_slot(bank))
+                    a_sb[c] = two.tile([P, 2, H], F32, name="a_sb", tag="term" if c == LAST else "a_sb")
+                nc.scalar.copy(out=by_slot(a_sb[c][:, b]), in_=by_word_slot(bank))
 
         def round_probes(c):
             x1_bf[c] = x_bf[c][:, PACK * CHUNK :] if c else shared([P, PACK * CHUNK], BF16, "x1_bf0", "wp1_raw")[:]
@@ -241,27 +255,40 @@ def tile_list_pivot_irrigation_kernel(
             for lo, hi in zip(cuts, cuts[1:]):
                 src = x_bf[c][:, PACK * lo : PACK * hi] if c or lo < CHUNK else x1_bf[c]
                 nc.vector.quantize_mx(out=codes[:, lo:hi].bitcast(FP8X4), scales=scales[:, lo:hi], in_=src)
+            b_sb[c] = {} if c == LAST else two.tile([P, 2, H], F32, name="b_sb")
             for b in range(2):
-                blk = 2 * c + b
+                cols = [slice(a * CHUNK + b * BLOCK, a * CHUNK + (b + 1) * BLOCK) for a in range(PASSES)]
+                if c == LAST:
+                    passes = [(*wp_q[a], codes[:, cols[a]], scales[:, cols[a]]) for a in range(PASSES)]
+                    b_sb[c][b] = channel_product("b_bank", passes)
+                    continue
                 bank = psum.tile([P, H], F32, name="b_bank", tag="b_bank")
                 for a in range(PASSES):
-                    cols = slice(a * CHUNK + b * BLOCK, a * CHUNK + (b + 1) * BLOCK)
                     nc.tensor.matmul_mx(
                         out=bank[:],
-                        lhsT=codes[:, cols].bitcast(FP8X4),
-                        lhsT_scale=scales[:, cols],
+                        lhsT=codes[:, cols[a]].bitcast(FP8X4),
+                        lhsT_scale=scales[:, cols[a]],
                         rhs=wp_q[a][0][:].bitcast(FP8X4),
                         rhs_scale=wp_q[a][1][:],
                         start=(a == 0),
                         stop=(a == PASSES - 1),
                     )
-                if b == 0:
-                    b_sb[c] = two.tile([P, 2, PACK, P], F32, name="b_sb")
-                for ts in halves(c):
-                    nc.scalar.copy(out=b_sb[c][:, b, ts], in_=by_word_slot(bank)[:, ts])
+                nc.scalar.copy(out=b_sb[c][:, b], in_=bank[:])
 
-        def halves(c):
-            return (slice(0, 2), slice(2, PACK)) if c == LAST else (slice(0, PACK),)
+        def channel_product(tag, passes):
+            bank = psum.tile([P, PACK, BLOCK], F32, name="channel_bank", tag=tag)
+            for t in range(PACK):
+                for i, (weight, weight_scales, tokens, token_scales) in enumerate(passes):
+                    nc.tensor.matmul_mx(
+                        out=bank[:, t, :],
+                        lhsT=weight[:, t * P : (t + 1) * P].bitcast(FP8X4),
+                        lhsT_scale=weight_scales[:, t * P : (t + 1) * P],
+                        rhs=tokens.bitcast(FP8X4),
+                        rhs_scale=token_scales,
+                        start=(i == 0),
+                        stop=(i == len(passes) - 1),
+                    )
+            return bank[:].rearrange("p t j -> p j t")
 
         def transposed_sum(tag, parts):
             bank = psum.tile([P, PACK, BLOCK], F32, name="sum_bank", tag=tag)
@@ -269,7 +296,7 @@ def tile_list_pivot_irrigation_kernel(
                 for t in range(PACK):
                     nc.tensor.matmul(
                         out=bank[:, t, :],
-                        lhsT=part[:, t, :],
+                        lhsT=part[:, t * P : (t + 1) * P],
                         rhs=ident[:],
                         is_transpose=True,
                         start=(order == 0 and t == 0),
@@ -277,31 +304,27 @@ def tile_list_pivot_irrigation_kernel(
                     )
             return bank[:].rearrange("p t j -> p j t")
 
-        def elementwise(c, out, in0, in1, op):
-            for part in ((0, 1), (1, 2)) if c == LAST else ((0, 2),):
-                blocks = slice(*part)
-                nc.vector.tensor_tensor(out=out[:, blocks], in0=in0[:, blocks], in1=in1[:, blocks], op=op)
-
         def difference(c):
-            e_sb[c] = keep.tile([P, 2, PACK, P], F32, name="diff")
-            elementwise(c, e_sb[c], a_sb[c], b_sb[c], SUB)
+            diff[c] = keep.tile([P, 2, H], F32, name="diff")
+            nc.vector.tensor_tensor(out=diff[c][:], in0=a_sb[c][:], in1=b_sb[c][:], op=SUB)
 
         def sum_h(c):
-            if c == LAST:
-                h_bf[c] = keep.tile([P, PACK * CHUNK], BF16, name="h_last", align_bytes=64)[:]
             for b in range(2):
                 summed = transposed_sum("ha_bank", (a_sb[c][:, b], b_sb[c][:, b]))
-                rounded = h_bf[c][:, b * PACK * BLOCK : (b + 1) * PACK * BLOCK]
-                nc.scalar.copy(out=rounded.rearrange("p (j t) -> p j t", t=PACK), in_=summed)
+                nc.scalar.copy(out=by_token(h_bf[c][:, b * H : (b + 1) * H]), in_=summed)
 
         def make_gate(c):
             codes = shared([P, CHUNK], U32, "h_codes%d" % c, "word_slot")
             scales = two.tile([P, CHUNK], U8, name="h_scales", align_bytes=64)
             quantize_chunk(c, codes, scales, h_bf[c].rearrange("p (b c) -> p b c", b=2))
-            gate[c] = two.tile([P, 2, PACK, P], F32, name="gate")
+            gate[c] = two.tile([P, 2, H], F32, name="gate")
             for b in range(2):
                 cols = slice(b * BLOCK, (b + 1) * BLOCK)
-                bank = psum.tile([P, H], F32, name="gate_bank", tag="ha_bank" if c == LAST else "zg_bank")
+                if c == LAST:
+                    bank = channel_product("ha_bank", [(wg_dealt, wg_sc_dealt, codes[:, cols], scales[:, cols])])
+                    nc.scalar.activation(out=by_token(gate[c][:, b]), in_=bank, func=SIGMOID, scale=-1.0)
+                    continue
+                bank = psum.tile([P, H], F32, name="gate_bank", tag="zg_bank")
                 nc.tensor.matmul_mx(
                     out=bank[:],
                     lhsT=codes[:, cols].bitcast(FP8X4),
@@ -311,23 +334,17 @@ def tile_list_pivot_irrigation_kernel(
                     start=True,
                     stop=True,
                 )
-                for ts in halves(c):
-                    nc.scalar.activation(out=gate[c][:, b, ts], in_=by_word_slot(bank)[:, ts], func=SIGMOID)
+                nc.scalar.activation(out=by_slot(gate[c][:, b]), in_=by_word_slot(bank), func=SIGMOID)
 
         def interpolate(c):
-            term[c] = two.tile([P, 2, PACK, P], F32, name="term")
-            if c < LAST:
-                nc.vector.tensor_tensor(out=term[c][:], in0=gate[c][:], in1=e_sb[c][:], op=MULT)
-                return
-            for b in range(2):
-                for ts in halves(c):
-                    nc.vector.tensor_tensor(out=term[c][:, b, ts], in0=gate[c][:, b, ts], in1=e_sb[c][:, b, ts], op=MULT)
+            term[c] = two.tile([P, 2, H], F32, name="term")
+            for blocks in (slice(0, 1), slice(1, 2)) if c == LAST - 1 else (slice(0, 2),):
+                nc.vector.tensor_tensor(out=term[c][:, blocks], in0=gate[c][:, blocks], in1=diff[c][:, blocks], op=MULT)
 
         def sum_z(c):
             z_bf[c] = shared([P, 2, BLOCK, PACK], BF16, "z_bf%d" % c, "z_slot%d" % (c % 2))[:]
             for b in range(2):
-                summed = transposed_sum("b_bank" if c == LAST else "zg_bank", (b_sb[c][:, b], term[c][:, b]))
-                nc.scalar.copy(out=z_bf[c][:, b], in_=summed)
+                nc.scalar.copy(out=z_bf[c][:, b], in_=transposed_sum("zg_bank", (b_sb[c][:, b], term[c][:, b])))
 
         def quantize_z(c):
             z_q[c] = quantize_sum("z", c, z_bf[c])
@@ -337,7 +354,8 @@ def tile_list_pivot_irrigation_kernel(
             for b in range(2):
                 blk = 2 * c + b
                 cols = slice(b * BLOCK, (b + 1) * BLOCK)
-                bank = psum.tile([P, N // P, BLOCK], F32, name="out_bank")
+                tag = "b_bank" if c == LAST else "out_bank"
+                bank = psum.tile([P, N // P, BLOCK], F32, name="out_bank", tag=tag)
                 for n in range(N // P):
                     nc.tensor.matmul_mx(
                         out=bank[:, n, :],
@@ -349,7 +367,7 @@ def tile_list_pivot_irrigation_kernel(
                         stop=True,
                     )
                 staged = four.tile([P, N // P, BLOCK], F32, name="staged")
-                copy = nc.vector.tensor_copy if c >= LAST - 1 and blk != 2 * LAST else nc.scalar.copy
+                copy = nc.vector.tensor_copy if blk == 2 * LAST + 1 else nc.scalar.copy
                 copy(out=staged[:], in_=bank[:])
                 nc.sync.dma_start(
                     out=out.rearrange("(n p) j -> p n j", p=P)[:, :, blk * BLOCK : (blk + 1) * BLOCK], in_=staged[:]
@@ -357,6 +375,7 @@ def tile_list_pivot_irrigation_kernel(
 
         first_picks(0, (0, 1))
         gather_words(0)
+        gather_words(LAST)
         first_picks(0, (2, 3))
         v_sc0 = keep.tile([P, S], U8, align_bytes=64)
         nc.vector.tensor_copy(out=v_sc0[:], in_=tab_sc[:].indirect(list1[:]))
@@ -371,12 +390,6 @@ def tile_list_pivot_irrigation_kernel(
             scales = keep.tile([P, H], U8, name="wp_scales%d" % a, align_bytes=64)
             wp_q[a] = quantize(codes, scales, wp_bf[a][:])
         project_probes(0)
-        wo_bf = round_weight("wo", wo)
-        for n in range(N // P):
-            codes = keep.tile([P, P], U32, name="wo_codes%d" % n, align_bytes=64)
-            scales = keep.tile([P, P], U8, name="wo_scales%d" % n, align_bytes=64)
-            wo_q[n] = quantize(codes, scales, wo_bf[:, n * K_PASS : (n + 1) * K_PASS])
-
         for c in range(1, CHUNKS):
             first_picks(c, (0, 1, 2, 3))
             open_chunk(c)
@@ -384,26 +397,55 @@ def tile_list_pivot_irrigation_kernel(
             sum_h(c - 1)
             difference(c - 1)
             make_gate(c - 1)
-            if c >= 2:
+            if 2 <= c < LAST:
                 quantize_z(c - 2)
             second_picks(c, (2, 3))
-            gather_words(c)
+            if c < LAST:
+                gather_words(c)
             round_probes(c)
             interpolate(c - 1)
-            project_table(c)
+            if c < LAST:
+                project_table(c)
             project_probes(c)
+            if c == LAST:
+                quantize_z(c - 2)
             if c >= 2:
                 finish(c - 2)
+            if c == 1:
+                project_table(LAST)
+                a_last = keep.tile([P, 2, BLOCK, PACK], F32)
+                for b in range(2):
+                    nc.scalar.copy(out=a_last[:, b], in_=transposed_sum("out_bank", (a_sb[LAST][:, b],)))
+                wo_bf = round_weight("wo", wo)
+                for n in range(N // P):
+                    codes = keep.tile([P, P], U32, name="wo_codes%d" % n, align_bytes=64)
+                    scales = keep.tile([P, P], U8, name="wo_scales%d" % n, align_bytes=64)
+                    wo_q[n] = quantize(codes, scales, wo_bf[:, n * K_PASS : (n + 1) * K_PASS])
             if c < LAST:
                 sum_z(c - 1)
 
-        sum_h(LAST)
+        wg_dealt = shared([P, H], U32, "wg_dealt", "x_bf%d" % LAST)
+        wg_sc_dealt = shared([P, H], U8, "wg_sc_dealt", "x_slot1")
+        for dealt, natural in ((wg_dealt, wg), (wg_sc_dealt, wg_sc)):
+            nc.vector.tensor_copy(
+                out=dealt[:].rearrange("p (t m) -> p t m", t=PACK), in_=natural[:].rearrange("p (m t) -> p t m", t=PACK)
+            )
+        h_bf[LAST] = keep.tile([P, 2 * H], BF16, name="h_last", align_bytes=64)[:]
+        for b in range(2):
+            rounded = by_token(h_bf[LAST][:, b * H : (b + 1) * H])
+            nc.vector.tensor_tensor(out=rounded, in0=b_sb[LAST][b], in1=a_last[:, b], op=ADD)
         make_gate(LAST)
+        diff[LAST] = keep.tile([P, 2, H], F32, name="diff")
+        for b in range(2):
+            nc.vector.tensor_tensor(out=by_token(diff[LAST][:, b]), in0=b_sb[LAST][b], in1=a_last[:, b], op=SUB)
         sum_z(LAST - 1)
-        difference(LAST)
-        interpolate(LAST)
-        sum_z(LAST)
+        term[LAST] = two.tile([P, 2, H], F32, name="term")
+        for b in range(2):
+            nc.vector.tensor_tensor(out=term[LAST][:, b], in0=gate[LAST][:, b], in1=diff[LAST][:, b], op=MULT)
         quantize_z(LAST - 1)
         finish(LAST - 1)
+        z_bf[LAST] = shared([P, 2, BLOCK, PACK], BF16, "z_last", "z_slot1")[:]
+        for b in range(2):
+            nc.vector.tensor_tensor(out=z_bf[LAST][:, b], in0=by_token(term[LAST][:, b]), in1=a_last[:, b], op=ADD)
         quantize_z(LAST)
         finish(LAST)

@@ -344,7 +344,7 @@ def tile_list_pivot_irrigation_kernel(
         def sum_z(c):
             z_bf[c] = shared([P, 2, BLOCK, PACK], BF16, "z_bf%d" % c, "z_slot%d" % (c % 2))[:]
             for b in range(2):
-                nc.scalar.copy(out=z_bf[c][:, b], in_=transposed_sum("zg_bank", (b_sb[c][:, b], term[c][:, b])))
+                nc.scalar.copy(out=z_bf[c][:, b], in_=transposed_sum("zg_bank" if c == LAST - 1 else "b_bank", (b_sb[c][:, b], term[c][:, b])))
 
         def quantize_z(c):
             z_q[c] = quantize_sum("z", c, z_bf[c])
@@ -397,19 +397,18 @@ def tile_list_pivot_irrigation_kernel(
             sum_h(c - 1)
             difference(c - 1)
             make_gate(c - 1)
-            if 2 <= c < LAST:
-                quantize_z(c - 2)
             second_picks(c, (2, 3))
             if c < LAST:
                 gather_words(c)
             round_probes(c)
+            if c >= 2:
+                sum_z(c - 2)
             interpolate(c - 1)
             if c < LAST:
                 project_table(c)
             project_probes(c)
-            if c == LAST:
-                quantize_z(c - 2)
             if c >= 2:
+                quantize_z(c - 2)
                 finish(c - 2)
             if c == 1:
                 project_table(LAST)
@@ -421,8 +420,6 @@ def tile_list_pivot_irrigation_kernel(
                     codes = keep.tile([P, P], U32, name="wo_codes%d" % n, align_bytes=64)
                     scales = keep.tile([P, P], U8, name="wo_scales%d" % n, align_bytes=64)
                     wo_q[n] = quantize(codes, scales, wo_bf[:, n * K_PASS : (n + 1) * K_PASS])
-            if c < LAST:
-                sum_z(c - 1)
 
         wg_dealt = shared([P, H], U32, "wg_dealt", "x_bf%d" % LAST)
         wg_sc_dealt = shared([P, H], U8, "wg_sc_dealt", "x_slot1")

@@ -24,27 +24,33 @@ PACK = 4
 K_PASS = P * PACK
 PASSES = K // K_PASS
 QUADRANTS = 4
+SCALE_ROWS = 16
 GROUP = 16
 BLOCK = 128
 CHUNK = 2 * BLOCK
 CHUNKS = S // CHUNK
 LAST = CHUNKS - 1
+ROW = 2 * H
 
 
-def entries(offsets, c):
-    return offsets[:, c * CHUNK // GROUP : (c + 1) * CHUNK // GROUP]
-
-
-def by_word_slot(bank):
-    return bank[:].rearrange("j (p t) -> j t p", t=PACK)
+def entries(offsets, first, count):
+    return offsets[:, first // GROUP : (first + count) // GROUP]
 
 
 def by_token(row):
     return row.rearrange("p (j t) -> p j t", t=PACK)
 
 
-def by_slot(row):
-    return row.rearrange("j (t p) -> j t p", t=PACK)
+def block_of(row, b):
+    return row.rearrange("j (g b u p) -> j g b u p", g=2, b=2, u=2)[:, :, b]
+
+
+def natural(bank):
+    return bank[:].rearrange("j (p g u) -> j g u p", g=2, u=2)
+
+
+def dealt(bank):
+    return bank[:].rearrange("j (g u p) -> j g u p", g=2, u=2)
 
 
 def tile_list_pivot_irrigation_kernel(
@@ -54,11 +60,11 @@ def tile_list_pivot_irrigation_kernel(
     with ExitStack() as ctx:
         keep = ctx.enter_context(tc.tile_pool(name="keep", bufs=1))
         two = ctx.enter_context(tc.tile_pool(name="two", bufs=2))
-        four = ctx.enter_context(tc.tile_pool(name="four", bufs=4))
-        psum = ctx.enter_context(tc.psum_pool(name="psum", bufs=2))
+        four = ctx.enter_context(tc.tile_pool(name="four", bufs=6))
+        psum = ctx.enter_context(tc.psum_pool(name="psum", bufs=1))
 
-        def shared(shape, dtype, name, tag):
-            return keep.tile(shape, dtype, name=name, tag=tag, align_bytes=64)
+        def shared(shape, dtype, name, tag=None):
+            return keep.tile(shape, dtype, name=name, tag=tag or name, align_bytes=64)
 
         def interleave(dst, src):
             nc.scalar.copy(
@@ -67,49 +73,39 @@ def tile_list_pivot_irrigation_kernel(
             )
 
         def quantize(codes, scales, src):
-            nc.vector.quantize_mx(out=codes[:].bitcast(FP8X4), scales=scales[:], in_=src)
-            return codes, scales
-
-        def quantize_chunk(c, codes, scales, src):
-            if c < LAST:
-                return quantize(codes, scales, src.rearrange("p b c -> p (b c)"))
-            words = src.shape[2] // PACK
-            for b in range(2):
-                cols = slice(b * words, (b + 1) * words)
-                nc.vector.quantize_mx(out=codes[:, cols].bitcast(FP8X4), scales=scales[:, cols], in_=src[:, b, :])
-            return codes, scales
-
-        def quantize_sum(name, c, src):
-            codes = shared([P, CHUNK], U32, "z_codes%d" % c, "x_slot0" if c == LAST - 2 else "z_codes%d" % (c % 2))
-            scales = two.tile([P, CHUNK], U8, name=name + "_scales", align_bytes=64)
-            return quantize_chunk(c, codes, scales, src.rearrange("p b j t -> p b (j t)"))
+            nc.vector.quantize_mx(out=codes.bitcast(FP8X4), scales=scales, in_=src)
 
         def load_plane(a, t):
-            plane = keep.tile([P, T], F32, name="plane%d%d" % (a, t))
+            plane = shared([P, T], F32, "plane%d%d" % (a, t))
             rows = xT[a * K_PASS : (a + 1) * K_PASS, :].rearrange("(p t) c -> p t c", t=PACK)
             nc.sync.dma_start(out=plane[:], in_=rows[:, t, :])
             return plane
 
-        def round_weight(name, rows, dealt=False):
-            width = rows.shape[1]
-            raw = shared([P, PACK, width], F32, name + "_raw", name + "_raw")
+        def load_weight(name, rows):
+            raw = shared([P, PACK, rows.shape[1]], F32, name)
             nc.sync.dma_start(out=raw[:], in_=rows.rearrange("(p t) c -> p t c", t=PACK))
-            grouped = keep.tile([P, PACK * width], BF16, name=name + "_bf", align_bytes=64)
-            if dealt:
-                nc.scalar.copy(
-                    out=grouped[:].rearrange("p (t m j) -> p m t j", t=PACK, j=PACK),
-                    in_=raw[:].rearrange("p j (m t) -> p m t j", t=PACK),
-                )
-            else:
-                interleave(grouped[:], raw[:])
-            return grouped
+            return raw
 
-        tab_sc = shared([P, T], U8, "tab_sc", "x_slot1")
-        nc.gpsimd.memset(tab_sc[:].bitcast(I32), 0)
-        wm_sc = keep.tile([P, PASSES * H], U8, align_bytes=64)
-        wg_sc = keep.tile([P, H], U8, align_bytes=64)
-        v_sc1 = keep.tile([P, S], U8, align_bytes=64)
-        for scale_tile in (wm_sc, wg_sc, v_sc1):
+        def load_words(a):
+            tab = shared([P, T], U32, "tab%d" % a)
+            nc.sync.dma_start(out=tab[:].bitcast(I32), in_=tab_words[a].rearrange("p c t -> p (c t)").bitcast(I32))
+            return tab
+
+        def round_wp(a):
+            raw = load_weight("wp%d_raw" % a, wp[a * K_PASS : (a + 1) * K_PASS, :])
+            nc.scalar.copy(
+                out=wp_bf[:, a * PACK * H : (a + 1) * PACK * H].rearrange("p (t m j) -> p m t j", t=PACK, j=PACK),
+                in_=raw[:].rearrange("p j (m t) -> p m t j", t=PACK),
+            )
+
+        first_row = P - PASSES * SCALE_ROWS
+        tab_sc = shared([P, T], U8, "tab_sc")
+        nc.vector.memset(tab_sc[:first_row, :].bitcast(I32), 0)
+        nc.sync.dma_start(out=tab_sc[first_row:, :].bitcast(I32), in_=tab_scales.rearrange("a r c -> (a r) c").bitcast(I32))
+        v_sc = shared([P, PASSES * S], U8, "v_sc")
+        wm_sc = shared([P, PASSES * H], U8, "wm_sc")
+        wg_sc = shared([P, H], U8, "wg_sc")
+        for scale_tile in (v_sc, wm_sc, wg_sc):
             nc.vector.memset(scale_tile[:].bitcast(I32), 0)
         ident = keep.tile([P, P], F32)
         make_identity(nc, ident[:])
@@ -117,23 +113,37 @@ def tile_list_pivot_irrigation_kernel(
         list1 = keep.tile([P, S // GROUP], U16)
         list2 = keep.tile([P, S // GROUP], U16)
         list3 = keep.tile([P, S // GROUP], U16)
+        nc.sync.dma_start(list1[:], offs)
         planes = {(0, 0): load_plane(0, 0)}
         nc.sync.dma_start(list2[:], offs2)
         nc.sync.dma_start(list3[:], offs3)
-        planes[0, 1] = load_plane(0, 1)
-        nc.sync.dma_start(list1[:], offs)
+        picked_sc = shared([P, S], U8, "picked_sc")
+        nc.vector.tensor_copy(out=picked_sc[:], in_=tab_sc[:].indirect(list1[:]))
 
-        x0_turned = [keep.tile([P, 2, 2, P, 2], BF16, name="x0_turned%d" % c) for c in range(CHUNKS)]
+        def place_scales(q):
+            for a in range(PASSES):
+                row = first_row + SCALE_ROWS * a + 4 * q
+                nc.sync.dma_start(
+                    out=v_sc[32 * q : 32 * q + 4, a * S : (a + 1) * S].bitcast(I32), in_=picked_sc[row : row + 4, :].bitcast(I32)
+                )
+            nc.sync.dma_start(
+                out=wm_sc[32 * q : 32 * q + 4, :].bitcast(I32).rearrange("r (a c) -> r a c", a=PASSES),
+                in_=wm_scales[:, 4 * q : 4 * q + 4, :].bitcast(I32).rearrange("a r c -> r a c"),
+            )
+
+        x_bf = [shared([P, PASSES * PACK * CHUNK], BF16, "x_bf%d" % c) for c in range(CHUNKS)]
+        turned = [shared([P, PACK * CHUNK], BF16, "x0_turned%d" % c)[:] for c in range(LAST)] + [x_bf[0][:, PACK * CHUNK :]]
+        x0_turned = [row.rearrange("j (b u p e) -> j b u p e", b=2, u=2, e=2) for row in turned]
         sum_banks = {}
 
         def gather_pass0(t):
             u, e = divmod(t, 2)
             for probe, offsets in enumerate((list2, list3)):
-                pick = keep.tile([P, S], F32, name="pick0_%d%d" % (t, probe), tag="pick0_%d%d" % (e, probe), align_bytes=64)
+                pick = shared([P, S], F32, "pick0_%d%d" % (t, probe), "pick%d%d" % (e, probe))
                 nc.vector.tensor_copy(out=pick[:], in_=planes[0, t][:].indirect(offsets[:]))
                 for c in range(CHUNKS):
                     if (e, probe) == (0, 0):
-                        sum_banks[c] = psum.tile([P, 2, 2, P], F32, name="sum_bank", tag=("ha_bank", "zg_bank")[c % 2])
+                        sum_banks[c] = psum.tile([P, 2, 2, P], F32, name="sum_bank", tag=("h0", "g0", "h1", "g1")[c])
                     for b in range(2):
                         blk = 2 * c + b
                         nc.tensor.matmul(
@@ -147,133 +157,77 @@ def tile_list_pivot_irrigation_kernel(
                     if (e, probe) == (1, 1):
                         nc.scalar.copy(out=x0_turned[c][:, :, u], in_=sum_banks[c][:].rearrange("j b e p -> j b p e"))
 
-        gather_pass0(0)
-        gather_pass0(1)
-        wp_bf = [round_weight("wp0", wp[:K_PASS, :], dealt=True)]
-        planes[0, 2] = load_plane(0, 2)
-        gather_pass0(2)
-        planes[0, 3] = load_plane(0, 3)
-        gather_pass0(3)
-
-        planes[1, 0] = load_plane(1, 0)
-        planes[1, 1] = load_plane(1, 1)
-        tabs = []
-        for a in range(PASSES):
-            tab = keep.tile([P, T], U32, name="tab%d" % a)
-            nc.sync.dma_start(out=tab[:].bitcast(I32), in_=tab_words[a].rearrange("p c t -> p (c t)").bitcast(I32))
-            tabs.append(tab)
-        planes[1, 2] = load_plane(1, 2)
-        for q in range(QUADRANTS):
-            nc.sync.dma_start(
-                out=tab_sc[32 * q : 32 * q + 4 * PASSES, :].bitcast(I32),
-                in_=tab_scales[:, 4 * q : 4 * q + 4, :].bitcast(I32),
-            )
-        planes[1, 3] = load_plane(1, 3)
-        wp_bf.append(round_weight("wp1", wp[K_PASS:, :], dealt=True))
-        wm = keep.tile([P, PASSES, 2 * H], U8, align_bytes=64)
-        nc.sync.dma_start(out=wm[:].bitcast(I32), in_=wm_words.bitcast(I32).rearrange("a p c -> p a c"))
-        for q in range(QUADRANTS):
-            nc.sync.dma_start(
-                out=wm_sc[32 * q : 32 * q + 4, :].bitcast(I32).rearrange("r (a c) -> r a c", a=PASSES),
-                in_=wm_scales[:, 4 * q : 4 * q + 4, :].bitcast(I32).rearrange("a r c -> r a c"),
-            )
-        for q in range(QUADRANTS):
-            nc.sync.dma_start(
-                out=wg_sc[32 * q : 32 * q + 4, :].bitcast(I32),
-                in_=wg_scales[0, 4 * q : 4 * q + 4, :].bitcast(I32),
-            )
-        wg = keep.tile([P, H], U32, align_bytes=64)
-        nc.sync.dma_start(out=wg[:].bitcast(I32), in_=wg_words[0].rearrange("p c t -> p (c t)").bitcast(I32))
-
-        x_bf = [shared([P, PASSES * PACK * CHUNK], BF16, "x_bf%d" % c, "x_bf%d" % c) for c in range(CHUNKS)]
-        for c in range(CHUNKS):
-            bank = psum.tile([P, 2, 2, BLOCK], F32, name="back_bank", tag="b_bank")
-            for b in range(2):
-                for u in range(2):
-                    pairs = x0_turned[c][:, b, u].rearrange("j p e -> j (p e)").bitcast(F32)
-                    nc.tensor.transpose(out=bank[:, b, u, :], in_=pairs, identity=ident[:])
-            words = x_bf[c][:, : PACK * CHUNK].bitcast(F32)
-            nc.scalar.copy(
-                out=words.rearrange("p (b j u) -> p b j u", b=2, u=2), in_=bank[:].rearrange("p b u j -> p b j u")
-            )
-
-        x1, v_codes, picks, b_sb, a_sb, diff, h_bf, gate, term, z_bf, z_q, wp_q, wo_q, x1_bf = ({} for name in range(14))
-
-        def open_chunk(c):
-            row = shared([P, PACK * CHUNK], F32, "x1_%d" % c, "x_slot%d" % ((c + 1) % 2))
-            x1[c] = row[:].rearrange("p (t j) -> p t j", t=PACK)
-            h_bf[c - 1] = row[:, 2 * CHUNK :].bitcast(BF16)
+        first, x1, a_row, b_row, diff, h_bf, gate, term, z_bf, z_q, wo_q, x_q = ({} for name in range(12))
 
         def first_picks(c, ts):
-            if 0 in ts:
-                row = shared([P, PACK, CHUNK], F32, "picks%d" % c, "x_slot%d" % (c % 2))
-                picks.update({t: row[:, t, :] for t in range(PACK)})
-            if 2 in ts and c == 0:
-                picks.update({t: shared([P, CHUNK], F32, "pick0_%d" % t, "wp_slot%d" % (t - 2))[:] for t in ts})
             for t in ts:
-                nc.vector.tensor_copy(out=picks[t], in_=planes[1, t][:].indirect(entries(list2, c)))
+                nc.vector.tensor_copy(out=first[c, t], in_=planes[1, t][:].indirect(entries(list2, c * CHUNK, CHUNK)))
 
         def second_picks(c, ts):
             for t in ts:
                 nc.vector.tensor_tensor(
-                    out=x1[c][:, t, :], in0=planes[1, t][:].indirect(entries(list3, c)), in1=picks[t], op=ADD
+                    out=x1[c][:, t, :],
+                    in0=planes[1, t][:].indirect(entries(list3, c * CHUNK, CHUNK)),
+                    in1=first[c, t],
+                    op=ADD,
                 )
 
-        def gather_words(c):
-            v_codes[c] = shared([P, PASSES, CHUNK], U32, "v_codes%d" % c, "x_last" if c == LAST else "word_slot")
-            for a in range(PASSES):
-                nc.vector.tensor_copy(out=v_codes[c][:, a, :], in_=tabs[a][:].indirect(entries(list1, c)))
+        def gather_words(a):
+            nc.vector.tensor_copy(out=v_codes[:, a, :], in_=load_words(a)[:].indirect(list1[:]))
 
         def project_table(c):
             for b in range(2):
                 blk = 2 * c + b
-                bank = psum.tile([P, H], F32, name="a_bank", tag="out_bank" if c == LAST else "ha_bank")
+                bank = psum.tile([P, H], F32, name="a_bank", tag="og"[c % 2] + str(b))
                 for a in range(PASSES):
                     nc.tensor.matmul_mx(
                         out=bank[:],
-                        lhsT=v_codes[c][:, a, b * BLOCK : (b + 1) * BLOCK].bitcast(FP8X4),
-                        lhsT_scale=v_scales[a][:, blk * BLOCK : (blk + 1) * BLOCK],
+                        lhsT=v_codes[:, a, blk * BLOCK : (blk + 1) * BLOCK].bitcast(FP8X4),
+                        lhsT_scale=v_sc[:, a * S + blk * BLOCK : a * S + (blk + 1) * BLOCK],
                         rhs=wm[:, a, :].bitcast(FP4X4),
                         rhs_scale=wm_sc[:, a * H : (a + 1) * H],
                         start=(a == 0),
                         stop=(a == PASSES - 1),
                     )
-                if b == 0:
-                    a_sb[c] = two.tile([P, 2, H], F32, name="a_sb", tag="term" if c == LAST else "a_sb")
-                nc.scalar.copy(out=by_slot(a_sb[c][:, b]), in_=by_word_slot(bank))
+                nc.scalar.copy(out=block_of(a_row[c], b), in_=natural(bank))
 
         def round_probes(c):
-            x1_bf[c] = x_bf[c][:, PACK * CHUNK :] if c else shared([P, PACK * CHUNK], BF16, "x1_bf0", "wp1_raw")[:]
-            width = BLOCK if c == LAST else CHUNK
-            for first in range(0, CHUNK, width):
-                interleave(x1_bf[c][:, PACK * first : PACK * (first + width)], x1[c][:, :, first : first + width])
+            for lo, hi in ((0, 1), (1, 2)) if c == LAST else ((0, 2),):
+                interleave(probe_rows(c)[:, 1, lo:hi].rearrange("p b w -> p (b w)"), x1[c][:, :, lo * BLOCK : hi * BLOCK])
+
+        def quantize_probes(c):
+            codes = two.tile([P, PASSES * CHUNK], U32, name="x_codes", align_bytes=64)
+            scales = two.tile([P, PASSES * CHUNK], U8, name="x_scales", align_bytes=64)
+            width = PASSES * (BLOCK if c == LAST else CHUNK)
+            for lo in range(0, PASSES * CHUNK, width):
+                quantize(codes[:, lo : lo + width], scales[:, lo : lo + width], x_bf[c][:, PACK * lo : PACK * (lo + width)])
+            x_q[c] = codes, scales
 
         def project_probes(c):
-            codes = shared([P, PASSES * CHUNK], U32, "x_codes%d" % c, "x_last" if c == LAST else "x_slot%d" % (c % 2))
-            scales = shared([P, PASSES * CHUNK], U8, "x_scales%d" % c, "x_scales_slot")
-            cuts = {0: (0, CHUNK, 2 * CHUNK), LAST: (0, CHUNK, CHUNK + BLOCK, 2 * CHUNK)}.get(c, (0, 2 * CHUNK))
-            for lo, hi in zip(cuts, cuts[1:]):
-                src = x_bf[c][:, PACK * lo : PACK * hi] if c or lo < CHUNK else x1_bf[c]
-                nc.vector.quantize_mx(out=codes[:, lo:hi].bitcast(FP8X4), scales=scales[:, lo:hi], in_=src)
-            b_sb[c] = {} if c == LAST else two.tile([P, 2, H], F32, name="b_sb")
+            codes, scales = x_q[c]
+            b_row[c] = {} if c == LAST else two.tile([P, ROW], F32, name="b_row")[:]
             for b in range(2):
-                cols = [slice(a * CHUNK + b * BLOCK, a * CHUNK + (b + 1) * BLOCK) for a in range(PASSES)]
+                places = [PASSES * b + a if c == LAST else 2 * a + b for a in range(PASSES)]
+                cols = [slice(place * BLOCK, (place + 1) * BLOCK) for place in places]
                 if c == LAST:
-                    passes = [(*wp_q[a], codes[:, cols[a]], scales[:, cols[a]]) for a in range(PASSES)]
-                    b_sb[c][b] = channel_product("b_bank", passes)
+                    passes = [
+                        (wp_codes[:, a * H : (a + 1) * H], wp_scales[:, a * H : (a + 1) * H], codes[:, cols[a]], scales[:, cols[a]])
+                        for a in range(PASSES)
+                    ]
+                    b_row[c][b] = channel_product("b%d" % b, passes)
                     continue
-                bank = psum.tile([P, H], F32, name="b_bank", tag="b_bank")
+                bank = psum.tile([P, H], F32, name="b_bank", tag="b%d" % b)
                 for a in range(PASSES):
                     nc.tensor.matmul_mx(
                         out=bank[:],
                         lhsT=codes[:, cols[a]].bitcast(FP8X4),
                         lhsT_scale=scales[:, cols[a]],
-                        rhs=wp_q[a][0][:].bitcast(FP8X4),
-                        rhs_scale=wp_q[a][1][:],
+                        rhs=wp_codes[:, a * H : (a + 1) * H].bitcast(FP8X4),
+                        rhs_scale=wp_scales[:, a * H : (a + 1) * H],
                         start=(a == 0),
                         stop=(a == PASSES - 1),
                     )
-                nc.scalar.copy(out=b_sb[c][:, b], in_=bank[:])
+                nc.scalar.copy(out=block_of(b_row[c], b), in_=dealt(bank))
 
         def channel_product(tag, passes):
             bank = psum.tile([P, PACK, BLOCK], F32, name="channel_bank", tag=tag)
@@ -290,41 +244,54 @@ def tile_list_pivot_irrigation_kernel(
                     )
             return bank[:].rearrange("p t j -> p j t")
 
-        def transposed_sum(tag, parts):
+        def transposed_sum(tag, rows, b):
             bank = psum.tile([P, PACK, BLOCK], F32, name="sum_bank", tag=tag)
-            for order, part in enumerate(parts):
+            for order, row in enumerate(rows):
                 for t in range(PACK):
                     nc.tensor.matmul(
                         out=bank[:, t, :],
-                        lhsT=part[:, t * P : (t + 1) * P],
+                        lhsT=block_of(row, b)[:, t // 2, t % 2, :],
                         rhs=ident[:],
                         is_transpose=True,
                         start=(order == 0 and t == 0),
-                        stop=(order == len(parts) - 1 and t == PACK - 1),
+                        stop=(order == len(rows) - 1 and t == PACK - 1),
                     )
             return bank[:].rearrange("p t j -> p j t")
 
+        def elementwise(dst, left, right, op, pieces):
+            width = ROW // pieces
+            for lo in range(0, ROW, width):
+                nc.vector.tensor_tensor(out=dst[:, lo : lo + width], in0=left[:, lo : lo + width], in1=right[:, lo : lo + width], op=op)
+
         def difference(c):
-            diff[c] = keep.tile([P, 2, H], F32, name="diff")
-            nc.vector.tensor_tensor(out=diff[c][:], in0=a_sb[c][:], in1=b_sb[c][:], op=SUB)
+            diff[c] = rows[c + 1][:, ROW:]
+            for half in (slice(H, ROW), slice(0, H)) if c < LAST - 1 else (slice(0, ROW),):
+                nc.vector.tensor_tensor(out=diff[c][:, half], in0=a_row[c][:, half], in1=b_row[c][:, half], op=SUB)
 
         def sum_h(c):
             for b in range(2):
-                summed = transposed_sum("ha_bank", (a_sb[c][:, b], b_sb[c][:, b]))
-                nc.scalar.copy(out=by_token(h_bf[c][:, b * H : (b + 1) * H]), in_=summed)
+                nc.scalar.copy(out=by_token(h_bf[c][:, b * H : (b + 1) * H]), in_=transposed_sum("h%d" % b, (b_row[c], a_row[c]) if b and c < LAST - 1 else (a_row[c], b_row[c]), b))
 
-        def make_gate(c):
-            codes = shared([P, CHUNK], U32, "h_codes%d" % c, "word_slot")
-            scales = two.tile([P, CHUNK], U8, name="h_scales", align_bytes=64)
-            quantize_chunk(c, codes, scales, h_bf[c].rearrange("p (b c) -> p b c", b=2))
-            gate[c] = two.tile([P, 2, H], F32, name="gate")
+        def quantize_pair(name, c, src):
+            codes = shared([P, CHUNK], U32, "%s_codes%d" % (name, c), "%s_codes%d" % (name, c % 2))
+            scales = two.tile([P, CHUNK], U8, name=name + "_scales", align_bytes=64)
+            width = BLOCK if c == LAST else CHUNK
+            for lo in range(0, CHUNK, width):
+                quantize(codes[:, lo : lo + width], scales[:, lo : lo + width], src[:, PACK * lo : PACK * (lo + width)])
+            return codes, scales
+
+        def quantize_h(c):
+            return quantize_pair("h", c, h_bf[c])
+
+        def make_gate(c, codes, scales):
+            gate[c] = two.tile([P, ROW], F32, name="gate")[:]
             for b in range(2):
                 cols = slice(b * BLOCK, (b + 1) * BLOCK)
                 if c == LAST:
-                    bank = channel_product("ha_bank", [(wg_dealt, wg_sc_dealt, codes[:, cols], scales[:, cols])])
-                    nc.scalar.activation(out=by_token(gate[c][:, b]), in_=bank, func=SIGMOID, scale=-1.0)
+                    bank = channel_product("g%d" % b, [(wg_dealt, wg_sc_dealt, codes[:, cols], scales[:, cols])])
+                    nc.scalar.activation(out=by_token(gate[c][:, b * H : (b + 1) * H]), in_=bank, func=SIGMOID, scale=-1.0)
                     continue
-                bank = psum.tile([P, H], F32, name="gate_bank", tag="zg_bank")
+                bank = psum.tile([P, H], F32, name="gate_bank", tag="g%d" % b)
                 nc.tensor.matmul_mx(
                     out=bank[:],
                     lhsT=codes[:, cols].bitcast(FP8X4),
@@ -334,28 +301,33 @@ def tile_list_pivot_irrigation_kernel(
                     start=True,
                     stop=True,
                 )
-                nc.scalar.activation(out=by_slot(gate[c][:, b]), in_=by_word_slot(bank), func=SIGMOID)
+                nc.scalar.activation(out=block_of(gate[c], b), in_=natural(bank), func=SIGMOID)
 
-        def interpolate(c):
-            term[c] = two.tile([P, 2, H], F32, name="term")
-            for blocks in (slice(0, 1), slice(1, 2)) if c == LAST - 1 else (slice(0, 2),):
-                nc.vector.tensor_tensor(out=term[c][:, blocks], in0=gate[c][:, blocks], in1=diff[c][:, blocks], op=MULT)
+        def interpolate(c, pieces):
+            term[c] = two.tile([P, ROW], F32, name="term")[:]
+            elementwise(term[c], gate[c], diff[c], MULT, pieces)
 
         def sum_z(c):
-            z_bf[c] = shared([P, 2, BLOCK, PACK], BF16, "z_bf%d" % c, "z_slot%d" % (c % 2))[:]
+            z_bf[c] = two.tile([P, 2 * H], BF16, name="z_bf", align_bytes=64)
             for b in range(2):
-                nc.scalar.copy(out=z_bf[c][:, b], in_=transposed_sum("zg_bank" if c == LAST - 1 else "b_bank", (b_sb[c][:, b], term[c][:, b])))
+                nc.scalar.copy(out=by_token(z_bf[c][:, b * H : (b + 1) * H]), in_=transposed_sum(("h%d" if c == LAST - 1 else "o%d") % b, (b_row[c], term[c]), b))
+
+        def quantize_wo(n, wo_bf):
+            interleave(wo_bf, wo_raw[:, :, n * P : (n + 1) * P])
+            codes = shared([P, P], U32, "wo_codes%d" % n)
+            scales = shared([P, P], U8, "wo_scales%d" % n)
+            quantize(codes[:], scales[:], wo_bf)
+            wo_q[n] = codes, scales
 
         def quantize_z(c):
-            z_q[c] = quantize_sum("z", c, z_bf[c])
+            z_q[c] = quantize_pair("z", c, z_bf[c])
 
         def finish(c):
             codes, scales = z_q[c]
             for b in range(2):
                 blk = 2 * c + b
                 cols = slice(b * BLOCK, (b + 1) * BLOCK)
-                tag = "b_bank" if c == LAST else "out_bank"
-                bank = psum.tile([P, N // P, BLOCK], F32, name="out_bank", tag=tag)
+                bank = psum.tile([P, N // P, BLOCK], F32, name="out_bank", tag="goho"[c] + str(b))
                 for n in range(N // P):
                     nc.tensor.matmul_mx(
                         out=bank[:, n, :],
@@ -373,76 +345,134 @@ def tile_list_pivot_irrigation_kernel(
                     out=out.rearrange("(n p) j -> p n j", p=P)[:, :, blk * BLOCK : (blk + 1) * BLOCK], in_=staged[:]
                 )
 
-        first_picks(0, (0, 1))
+        wp_bf = shared([P, PASSES * PACK * H], BF16, "wp_bf")
+        gather_pass0(0)
+        round_wp(0)
+        planes[0, 1] = load_plane(0, 1)
+        gather_pass0(1)
+        round_wp(1)
+        for t in (2, 3):
+            planes[0, t] = load_plane(0, t)
+            gather_pass0(t)
+
+        def probe_rows(c):
+            return x_bf[c][:].rearrange("p (b a w) -> p a b w" if c == LAST else "p (a b w) -> p a b w", b=2, a=PASSES)
+
+        for c in range(CHUNKS):
+            bank = psum.tile([P, 2, 2, BLOCK], F32, name="back_bank", tag="b%d" % (c % 2))
+            for b in range(2):
+                for u in range(2):
+                    pairs = x0_turned[c][:, b, u].rearrange("j p e -> j (p e)").bitcast(F32)
+                    nc.tensor.transpose(out=bank[:, b, u, :], in_=pairs, identity=ident[:])
+            words = probe_rows(c)[:, 0].bitcast(F32)
+            nc.scalar.copy(out=words.rearrange("p b (j u) -> p b j u", u=2), in_=bank[:].rearrange("p b u j -> p b j u"))
+
+        v_codes = shared([P, PASSES, S], U32, "v_codes", "wp0_raw")
         gather_words(0)
-        gather_words(LAST)
-        first_picks(0, (2, 3))
-        v_sc0 = keep.tile([P, S], U8, align_bytes=64)
-        nc.vector.tensor_copy(out=v_sc0[:], in_=tab_sc[:].indirect(list1[:]))
-        v_scales = [v_sc0, v_sc1]
-        nc.scalar.dma_start(out=v_sc1[0 : P - 4, :].bitcast(I32), in_=v_sc0[4:P, :].bitcast(I32))
-        open_chunk(0)
-        second_picks(0, (0, 1, 2, 3))
+        wm = keep.tile([P, PASSES, 2 * H], U8, align_bytes=64)
+        nc.sync.dma_start(out=wm[:].bitcast(I32), in_=wm_words.bitcast(I32).rearrange("a p c -> p a c"))
+        for q in range(QUADRANTS):
+            place_scales(q)
+        gather_words(1)
+        rows = [shared([P, 2 * ROW], F32, "rows%d" % c, "plane0%d" % c) for c in range(CHUNKS)]
+        for c in range(CHUNKS):
+            a_row[c] = rows[c][:, :ROW]
+            project_table(c)
+        for t in range(PACK):
+            planes[1, t] = load_plane(1, t)
+        for q in range(QUADRANTS):
+            nc.sync.dma_start(
+                out=wg_sc[32 * q : 32 * q + 4, :].bitcast(I32),
+                in_=wg_scales[0, 4 * q : 4 * q + 4, :].bitcast(I32),
+            )
+        wg = keep.tile([P, H], U32, align_bytes=64)
+        nc.sync.dma_start(out=wg[:].bitcast(I32), in_=wg_words[0].rearrange("p c t -> p (c t)").bitcast(I32))
+        wo_raw = load_weight("wo_raw", wo)
+
+        work = shared([P, ROW], F32, "work", "x0_turned2")
+        for c in range(CHUNKS):
+            first.update({(c, t): work[:, (t - 1) * CHUNK : t * CHUNK] for t in (1, 2, 3)})
+            h_bf[c] = work[:, BLOCK : BLOCK + H].bitcast(BF16)
+            sums = rows[min(c, LAST - 1) - 1][:, ROW - CHUNK : 2 * ROW - CHUNK] if c else rows[0][:, ROW:]
+            x1[c] = sums.rearrange("p (t j) -> p t j", t=PACK)
+        first[0, 0] = work[:, 3 * CHUNK :]
+        first[0, 3] = shared([P, CHUNK], F32, "first03", "x0_turned1")[:]
+        first_picks(0, range(PACK))
+        second_picks(0, range(PACK))
         round_probes(0)
-        project_table(0)
-        for a in range(PASSES):
-            codes = shared([P, H], U32, "wp_codes%d" % a, "wp_slot%d" % a)
-            scales = keep.tile([P, H], U8, name="wp_scales%d" % a, align_bytes=64)
-            wp_q[a] = quantize(codes, scales, wp_bf[a][:])
+        first_picks(1, (1,))
+        wp_codes = shared([P, PASSES * H], U32, "wp_codes", "x0_turned1")
+        wp_scales = shared([P, PASSES * H], U8, "wp_scales")
+        quantize(wp_codes[:], wp_scales[:], wp_bf[:])
+        wg_dealt = shared([P, H], U32, "wg_dealt")
+        wg_sc_dealt = shared([P, H], U8, "wg_sc_dealt")
+        for dealt_tile, natural_tile in ((wg_dealt, wg), (wg_sc_dealt, wg_sc)):
+            nc.vector.tensor_copy(
+                out=dealt_tile[:].rearrange("p (t m) -> p t m", t=PACK), in_=natural_tile[:].rearrange("p (m t) -> p t m", t=PACK)
+            )
+        quantize_probes(0)
         project_probes(0)
-        for c in range(1, CHUNKS):
-            first_picks(c, (0, 1, 2, 3))
-            open_chunk(c)
-            second_picks(c, (0, 1))
+        late = shared([P, 3, CHUNK], F32, "late", "x_bf0")
+        first.update({(1, 2): late[:, 0], (1, 3): late[:, 1], (1, 0): late[:, 2]})
+        second_picks(1, (1,))
+        first_picks(1, (2, 3, 0))
+        second_picks(1, (2, 3))
+        a_last = shared([P, 2, BLOCK, PACK], F32, "a_last", "tab0")
+        for b in range(2):
+            nc.scalar.copy(out=a_last[:, b], in_=transposed_sum("o%d" % b, (a_row[LAST],), b))
+        quantize_wo(0, x1[0][:, 3, :].bitcast(BF16))
+        for c in range(1, LAST):
             sum_h(c - 1)
             difference(c - 1)
-            make_gate(c - 1)
-            second_picks(c, (2, 3))
-            if c < LAST:
-                gather_words(c)
+            second_picks(c, (0,))
+            codes = quantize_h(c - 1)
             round_probes(c)
+            make_gate(c - 1, *codes)
             if c >= 2:
                 sum_z(c - 2)
-            interpolate(c - 1)
-            if c < LAST:
-                project_table(c)
-            project_probes(c)
-            if c >= 2:
                 quantize_z(c - 2)
-                finish(c - 2)
-            if c == 1:
-                project_table(LAST)
-                a_last = keep.tile([P, 2, BLOCK, PACK], F32)
-                for b in range(2):
-                    nc.scalar.copy(out=a_last[:, b], in_=transposed_sum("out_bank", (a_sb[LAST][:, b],)))
-                wo_bf = round_weight("wo", wo)
-                for n in range(N // P):
-                    codes = keep.tile([P, P], U32, name="wo_codes%d" % n, align_bytes=64)
-                    scales = keep.tile([P, P], U8, name="wo_scales%d" % n, align_bytes=64)
-                    wo_q[n] = quantize(codes, scales, wo_bf[:, n * K_PASS : (n + 1) * K_PASS])
+            first_picks(c + 1, (1, 2, 3))
+            quantize_probes(c)
+            project_probes(c)
+            if c + 1 < LAST:
+                first[c + 1, 0] = x1[c][:, 1, :]
+                first_picks(c + 1, (0,))
+                interpolate(c - 1, 2)
+                second_picks(c + 1, (1, 2, 3))
+                quantize_wo(1, x1[1][:, 2, :].bitcast(BF16))
+                quantize_wo(2, x1[1][:, 3, :].bitcast(BF16))
+        first[LAST, 0] = shared([P, CHUNK], F32, "first_last", "x_bf2")[:]
+        second_picks(LAST, (1,))
+        first_picks(LAST, (0,))
+        second_picks(LAST, (2, 3, 0))
+        finish(0)
+        sum_h(2)
+        round_probes(LAST)
+        interpolate(1, 1)
+        sum_z(1)
+        quantize_probes(LAST)
+        make_gate(2, *quantize_h(2))
+        project_probes(LAST)
+        difference(2)
+        quantize_z(1)
 
-        wg_dealt = shared([P, H], U32, "wg_dealt", "x_bf%d" % LAST)
-        wg_sc_dealt = shared([P, H], U8, "wg_sc_dealt", "x_slot1")
-        for dealt, natural in ((wg_dealt, wg), (wg_sc_dealt, wg_sc)):
-            nc.vector.tensor_copy(
-                out=dealt[:].rearrange("p (t m) -> p t m", t=PACK), in_=natural[:].rearrange("p (m t) -> p t m", t=PACK)
-            )
-        h_bf[LAST] = keep.tile([P, 2 * H], BF16, name="h_last", align_bytes=64)[:]
+        h_bf[LAST] = shared([P, 2 * H], BF16, "h_last")
         for b in range(2):
-            rounded = by_token(h_bf[LAST][:, b * H : (b + 1) * H])
-            nc.vector.tensor_tensor(out=rounded, in0=b_sb[LAST][b], in1=a_last[:, b], op=ADD)
-        make_gate(LAST)
-        diff[LAST] = keep.tile([P, 2, H], F32, name="diff")
-        for b in range(2):
-            nc.vector.tensor_tensor(out=by_token(diff[LAST][:, b]), in0=b_sb[LAST][b], in1=a_last[:, b], op=SUB)
+            nc.vector.tensor_tensor(out=by_token(h_bf[LAST][:, b * H : (b + 1) * H]), in0=b_row[LAST][b], in1=a_last[:, b], op=ADD)
+        make_gate(LAST, *quantize_h(LAST))
+        interpolate(LAST - 1, 1)
         sum_z(LAST - 1)
-        term[LAST] = two.tile([P, 2, H], F32, name="term")
-        for b in range(2):
-            nc.vector.tensor_tensor(out=term[LAST][:, b], in0=gate[LAST][:, b], in1=diff[LAST][:, b], op=MULT)
+        finish(1)
         quantize_z(LAST - 1)
-        finish(LAST - 1)
-        z_bf[LAST] = shared([P, 2, BLOCK, PACK], BF16, "z_last", "z_slot1")[:]
+        diff[LAST] = shared([P, ROW], F32, "diff3", "tab1")[:]
         for b in range(2):
-            nc.vector.tensor_tensor(out=z_bf[LAST][:, b], in0=by_token(term[LAST][:, b]), in1=a_last[:, b], op=ADD)
+            nc.vector.tensor_tensor(out=by_token(diff[LAST][:, b * H : (b + 1) * H]), in0=b_row[LAST][b], in1=a_last[:, b], op=SUB)
+        finish(LAST - 1)
+        interpolate(LAST, 2)
+        z_bf[LAST] = two.tile([P, 2 * H], BF16, name="z_bf", align_bytes=64)
+        for b in range(2):
+            nc.vector.tensor_tensor(
+                out=by_token(z_bf[LAST][:, b * H : (b + 1) * H]), in0=by_token(term[LAST][:, b * H : (b + 1) * H]), in1=a_last[:, b], op=ADD
+            )
         quantize_z(LAST)
         finish(LAST)

@@ -61,6 +61,7 @@ def tile_list_pivot_irrigation_kernel(
         keep = ctx.enter_context(tc.tile_pool(name="keep", bufs=1))
         two = ctx.enter_context(tc.tile_pool(name="two", bufs=2))
         four = ctx.enter_context(tc.tile_pool(name="four", bufs=6))
+        placed = ctx.enter_context(tc.tile_pool(name="placed", bufs=1))
         psum = ctx.enter_context(tc.psum_pool(name="psum", bufs=1))
 
         def shared(shape, dtype, name, tag=None):
@@ -132,8 +133,7 @@ def tile_list_pivot_irrigation_kernel(
             )
 
         x_bf = [shared([P, PASSES * PACK * CHUNK], BF16, "x_bf%d" % c) for c in range(CHUNKS)]
-        turned = [shared([P, PACK * CHUNK], BF16, "x0_turned%d" % c)[:] for c in range(LAST)] + [x_bf[0][:, PACK * CHUNK :]]
-        x0_turned = [row.rearrange("j (b u p e) -> j b u p e", b=2, u=2, e=2) for row in turned]
+        x0_turned = [shared([P, 2, 2, P, 2], BF16, "x0_turned%d" % c) for c in range(CHUNKS)]
         sum_banks = {}
 
         def gather_pass0(t):
@@ -157,7 +157,7 @@ def tile_list_pivot_irrigation_kernel(
                     if (e, probe) == (1, 1):
                         nc.scalar.copy(out=x0_turned[c][:, :, u], in_=sum_banks[c][:].rearrange("j b e p -> j b p e"))
 
-        first, x1, a_row, b_row, diff, h_bf, gate, term, z_bf, z_q, wo_q, x_q = ({} for name in range(12))
+        first, x1, a_row, b_row, diff, h_bf, gate, term, z_bf, z_q, x_q, z_banks, x1_bf = ({} for name in range(13))
 
         def first_picks(c, ts):
             for t in ts:
@@ -178,7 +178,7 @@ def tile_list_pivot_irrigation_kernel(
         def project_table(c):
             for b in range(2):
                 blk = 2 * c + b
-                bank = psum.tile([P, H], F32, name="a_bank", tag="og"[c % 2] + str(b))
+                bank = psum.tile([P, H], F32, name="a_bank", tag="ob"[c % 2] + str(b))
                 for a in range(PASSES):
                     nc.tensor.matmul_mx(
                         out=bank[:],
@@ -192,29 +192,42 @@ def tile_list_pivot_irrigation_kernel(
                 nc.scalar.copy(out=block_of(a_row[c], b), in_=natural(bank))
 
         def round_probes(c):
-            for lo, hi in ((0, 1), (1, 2)) if c == LAST else ((0, 2),):
-                interleave(probe_rows(c)[:, 1, lo:hi].rearrange("p b w -> p (b w)"), x1[c][:, :, lo * BLOCK : hi * BLOCK])
+            if c == LAST:
+                x1_bf[c] = [b_row[1][:, b * H : b * H + CHUNK].bitcast(BF16) for b in range(2)]
+            elif c == 0:
+                x1_bf[c] = [shared([P, PACK * CHUNK], BF16, "x1_bf0", "x0_turned3")[:]]
+            else:
+                x1_bf[c] = [x_bf[c][:, PACK * CHUNK :]]
+            width = CHUNK // len(x1_bf[c])
+            for i, piece in enumerate(x1_bf[c]):
+                interleave(piece, x1[c][:, :, i * width : (i + 1) * width])
 
         def quantize_probes(c):
-            codes = two.tile([P, PASSES * CHUNK], U32, name="x_codes", align_bytes=64)
             scales = two.tile([P, PASSES * CHUNK], U8, name="x_scales", align_bytes=64)
-            width = PASSES * (BLOCK if c == LAST else CHUNK)
-            for lo in range(0, PASSES * CHUNK, width):
-                quantize(codes[:, lo : lo + width], scales[:, lo : lo + width], x_bf[c][:, PACK * lo : PACK * (lo + width)])
+            if c:
+                codes = shared([P, PASSES * CHUNK], U32, "x_codes%d" % c, "plane10" if c == LAST else None)
+            else:
+                codes = placed.tile([P, PASSES * CHUNK], U32, name="x_codes0", align_bytes=64, offset=4 * PASSES * H)
             x_q[c] = codes, scales
+            if 0 < c < LAST:
+                return quantize(codes[:], scales[:], x_bf[c][:])
+            quantize(codes[:, :CHUNK], scales[:, :CHUNK], x_bf[c][:, : PACK * CHUNK])
+            width = CHUNK // len(x1_bf[c])
+            for i, piece in enumerate(x1_bf[c]):
+                cols = slice(CHUNK + i * width, CHUNK + (i + 1) * width)
+                quantize(codes[:, cols], scales[:, cols], piece)
 
         def project_probes(c):
             codes, scales = x_q[c]
-            b_row[c] = {} if c == LAST else two.tile([P, ROW], F32, name="b_row")[:]
+            b_row[c] = {} if c == LAST else two.tile([P, ROW], F32, name="b_row", align_bytes=64)[:]
             for b in range(2):
-                places = [PASSES * b + a if c == LAST else 2 * a + b for a in range(PASSES)]
-                cols = [slice(place * BLOCK, (place + 1) * BLOCK) for place in places]
+                cols = [slice(a * CHUNK + b * BLOCK, a * CHUNK + (b + 1) * BLOCK) for a in range(PASSES)]
                 if c == LAST:
                     passes = [
                         (wp_codes[:, a * H : (a + 1) * H], wp_scales[:, a * H : (a + 1) * H], codes[:, cols[a]], scales[:, cols[a]])
                         for a in range(PASSES)
                     ]
-                    b_row[c][b] = channel_product("b%d" % b, passes)
+                    b_row[c][b] = channel_product("o%d" % b, passes)
                     continue
                 bank = psum.tile([P, H], F32, name="b_bank", tag="b%d" % b)
                 for a in range(PASSES):
@@ -244,18 +257,21 @@ def tile_list_pivot_irrigation_kernel(
                     )
             return bank[:].rearrange("p t j -> p j t")
 
+        def turn(bank, row, b, opens, closes, ts=range(PACK)):
+            for t in ts:
+                nc.tensor.matmul(
+                    out=bank[:, t, :],
+                    lhsT=block_of(row, b)[:, t // 2, t % 2, :],
+                    rhs=ident[:],
+                    is_transpose=True,
+                    start=(opens and t == 0),
+                    stop=(closes and t == PACK - 1),
+                )
+
         def transposed_sum(tag, rows, b):
             bank = psum.tile([P, PACK, BLOCK], F32, name="sum_bank", tag=tag)
             for order, row in enumerate(rows):
-                for t in range(PACK):
-                    nc.tensor.matmul(
-                        out=bank[:, t, :],
-                        lhsT=block_of(row, b)[:, t // 2, t % 2, :],
-                        rhs=ident[:],
-                        is_transpose=True,
-                        start=(order == 0 and t == 0),
-                        stop=(order == len(rows) - 1 and t == PACK - 1),
-                    )
+                turn(bank, row, b, order == 0, order == len(rows) - 1)
             return bank[:].rearrange("p t j -> p j t")
 
         def elementwise(dst, left, right, op, pieces):
@@ -264,13 +280,17 @@ def tile_list_pivot_irrigation_kernel(
                 nc.vector.tensor_tensor(out=dst[:, lo : lo + width], in0=left[:, lo : lo + width], in1=right[:, lo : lo + width], op=op)
 
         def difference(c):
-            diff[c] = rows[c + 1][:, ROW:]
-            for half in (slice(H, ROW), slice(0, H)) if c < LAST - 1 else (slice(0, ROW),):
+            diff[c] = rows[c + 1][:, ROW:] if c < LAST - 1 else b_row[1]
+            for half in (slice(H, ROW), slice(0, H)) if c < LAST - 1 else (slice(0, H), slice(H, ROW)):
                 nc.vector.tensor_tensor(out=diff[c][:, half], in0=a_row[c][:, half], in1=b_row[c][:, half], op=SUB)
 
         def sum_h(c):
             for b in range(2):
-                nc.scalar.copy(out=by_token(h_bf[c][:, b * H : (b + 1) * H]), in_=transposed_sum("h%d" % b, (b_row[c], a_row[c]) if b and c < LAST - 1 else (a_row[c], b_row[c]), b))
+                bank = psum.tile([P, PACK, BLOCK], F32, name="h_bank", tag="h%d" % b)
+                turn(bank, a_row[c], b, True, False, range(PACK - 1))
+                turn(bank, b_row[c], b, False, False)
+                turn(bank, a_row[c], b, False, True, (PACK - 1,))
+                nc.scalar.copy(out=by_token(h_bf[c][:, b * H : (b + 1) * H]), in_=bank[:].rearrange("p t j -> p j t"))
 
         def quantize_pair(name, c, src):
             codes = shared([P, CHUNK], U32, "%s_codes%d" % (name, c), "%s_codes%d" % (name, c % 2))
@@ -307,17 +327,16 @@ def tile_list_pivot_irrigation_kernel(
             term[c] = two.tile([P, ROW], F32, name="term")[:]
             elementwise(term[c], gate[c], diff[c], MULT, pieces)
 
+        def open_z(c):
+            z_banks[c] = [psum.tile([P, PACK, BLOCK], F32, name="z_bank", tag="obh"[c] + str(b)) for b in range(2)]
+            for b in range(2):
+                turn(z_banks[c][b], b_row[c], b, True, False)
+
         def sum_z(c):
             z_bf[c] = two.tile([P, 2 * H], BF16, name="z_bf", align_bytes=64)
             for b in range(2):
-                nc.scalar.copy(out=by_token(z_bf[c][:, b * H : (b + 1) * H]), in_=transposed_sum(("h%d" if c == LAST - 1 else "o%d") % b, (b_row[c], term[c]), b))
-
-        def quantize_wo(n, wo_bf):
-            interleave(wo_bf, wo_raw[:, :, n * P : (n + 1) * P])
-            codes = shared([P, P], U32, "wo_codes%d" % n)
-            scales = shared([P, P], U8, "wo_scales%d" % n)
-            quantize(codes[:], scales[:], wo_bf)
-            wo_q[n] = codes, scales
+                turn(z_banks[c][b], term[c], b, False, True)
+                nc.scalar.copy(out=by_token(z_bf[c][:, b * H : (b + 1) * H]), in_=z_banks[c][b][:].rearrange("p t j -> p j t"))
 
         def quantize_z(c):
             z_q[c] = quantize_pair("z", c, z_bf[c])
@@ -327,19 +346,19 @@ def tile_list_pivot_irrigation_kernel(
             for b in range(2):
                 blk = 2 * c + b
                 cols = slice(b * BLOCK, (b + 1) * BLOCK)
-                bank = psum.tile([P, N // P, BLOCK], F32, name="out_bank", tag="goho"[c] + str(b))
+                bank = psum.tile([P, N // P, BLOCK], F32, name="out_bank", tag="gbho"[c] + str(b))
                 for n in range(N // P):
                     nc.tensor.matmul_mx(
                         out=bank[:, n, :],
-                        lhsT=wo_q[n][0][:].bitcast(FP8X4),
-                        lhsT_scale=wo_q[n][1][:],
+                        lhsT=wo_codes[:, n * P : (n + 1) * P].bitcast(FP8X4),
+                        lhsT_scale=wo_scales[:, n * P : (n + 1) * P],
                         rhs=codes[:, cols].bitcast(FP8X4),
                         rhs_scale=scales[:, cols],
                         start=True,
                         stop=True,
                     )
                 staged = four.tile([P, N // P, BLOCK], F32, name="staged")
-                copy = nc.vector.tensor_copy if blk == 2 * LAST + 1 else nc.scalar.copy
+                copy = nc.vector.tensor_copy if c >= LAST - 1 and b else nc.scalar.copy
                 copy(out=staged[:], in_=bank[:])
                 nc.sync.dma_start(
                     out=out.rearrange("(n p) j -> p n j", p=P)[:, :, blk * BLOCK : (blk + 1) * BLOCK], in_=staged[:]
@@ -350,13 +369,28 @@ def tile_list_pivot_irrigation_kernel(
         round_wp(0)
         planes[0, 1] = load_plane(0, 1)
         gather_pass0(1)
-        round_wp(1)
+        v_codes = shared([P, PASSES, S], U32, "v_codes", "wp0_raw")
+        wm = keep.tile([P, PASSES, 2 * H], U8, align_bytes=64)
+        nc.sync.dma_start(out=wm[:].bitcast(I32), in_=wm_words.bitcast(I32).rearrange("a p c -> p a c"))
+        for a in range(PASSES):
+            gather_words(a)
+            place_scales(2 * a)
+            place_scales(2 * a + 1)
+        rows = [shared([P, 2 * ROW + (0 if c else H)], F32, "rows%d" % c, ("plane00", "plane01", "tab0", "tab1")[c]) for c in range(CHUNKS)]
+        a_row.update({c: rows[c][:, :ROW] for c in range(CHUNKS)})
+        project_table(LAST)
+        a_last = shared([P, 2, BLOCK, PACK], F32, "a_last")
+        for b in range(2):
+            nc.scalar.copy(out=a_last[:, b], in_=transposed_sum("b%d" % b, (a_row[LAST],), b))
+        for c in range(LAST):
+            project_table(c)
         for t in (2, 3):
             planes[0, t] = load_plane(0, t)
             gather_pass0(t)
+        round_wp(1)
 
         def probe_rows(c):
-            return x_bf[c][:].rearrange("p (b a w) -> p a b w" if c == LAST else "p (a b w) -> p a b w", b=2, a=PASSES)
+            return x_bf[c][:].rearrange("p (a b w) -> p a b w", b=2, a=PASSES)
 
         for c in range(CHUNKS):
             bank = psum.tile([P, 2, 2, BLOCK], F32, name="back_bank", tag="b%d" % (c % 2))
@@ -367,17 +401,6 @@ def tile_list_pivot_irrigation_kernel(
             words = probe_rows(c)[:, 0].bitcast(F32)
             nc.scalar.copy(out=words.rearrange("p b (j u) -> p b j u", u=2), in_=bank[:].rearrange("p b u j -> p b j u"))
 
-        v_codes = shared([P, PASSES, S], U32, "v_codes", "wp0_raw")
-        gather_words(0)
-        wm = keep.tile([P, PASSES, 2 * H], U8, align_bytes=64)
-        nc.sync.dma_start(out=wm[:].bitcast(I32), in_=wm_words.bitcast(I32).rearrange("a p c -> p a c"))
-        for q in range(QUADRANTS):
-            place_scales(q)
-        gather_words(1)
-        rows = [shared([P, 2 * ROW], F32, "rows%d" % c, "plane0%d" % c) for c in range(CHUNKS)]
-        for c in range(CHUNKS):
-            a_row[c] = rows[c][:, :ROW]
-            project_table(c)
         for t in range(PACK):
             planes[1, t] = load_plane(1, t)
         for q in range(QUADRANTS):
@@ -389,38 +412,38 @@ def tile_list_pivot_irrigation_kernel(
         nc.sync.dma_start(out=wg[:].bitcast(I32), in_=wg_words[0].rearrange("p c t -> p (c t)").bitcast(I32))
         wo_raw = load_weight("wo_raw", wo)
 
-        work = shared([P, ROW], F32, "work", "x0_turned2")
+        work = shared([P, ROW], F32, "work")
         for c in range(CHUNKS):
             first.update({(c, t): work[:, (t - 1) * CHUNK : t * CHUNK] for t in (1, 2, 3)})
             h_bf[c] = work[:, BLOCK : BLOCK + H].bitcast(BF16)
-            sums = rows[min(c, LAST - 1) - 1][:, ROW - CHUNK : 2 * ROW - CHUNK] if c else rows[0][:, ROW:]
+            sums = rows[c - 1][:, ROW - CHUNK : 2 * ROW - CHUNK] if 0 < c < LAST else rows[c // 2][:, ROW : 2 * ROW]
             x1[c] = sums.rearrange("p (t j) -> p t j", t=PACK)
         first[0, 0] = work[:, 3 * CHUNK :]
-        first[0, 3] = shared([P, CHUNK], F32, "first03", "x0_turned1")[:]
-        first_picks(0, range(PACK))
-        second_picks(0, range(PACK))
+        first[0, 3] = placed.tile([P, CHUNK], F32, name="first03", align_bytes=64, offset=4 * (PASSES * H - BLOCK))[:]
+        spacers = shared([P, PACK, CHUNK], F32, "first1", "pick00")
+        for t in range(PACK):
+            first[1, t] = spacers[:, t, :]
+            first_picks(0, (t,))
+            first_picks(1, (t,))
+            second_picks(0, (t,))
         round_probes(0)
-        first_picks(1, (1,))
-        wp_codes = shared([P, PASSES * H], U32, "wp_codes", "x0_turned1")
+        wp_codes = placed.tile([P, PASSES * H], U32, name="wp_codes", align_bytes=64, offset=0)
         wp_scales = shared([P, PASSES * H], U8, "wp_scales")
         quantize(wp_codes[:], wp_scales[:], wp_bf[:])
-        wg_dealt = shared([P, H], U32, "wg_dealt")
-        wg_sc_dealt = shared([P, H], U8, "wg_sc_dealt")
-        for dealt_tile, natural_tile in ((wg_dealt, wg), (wg_sc_dealt, wg_sc)):
-            nc.vector.tensor_copy(
-                out=dealt_tile[:].rearrange("p (t m) -> p t m", t=PACK), in_=natural_tile[:].rearrange("p (m t) -> p t m", t=PACK)
-            )
         quantize_probes(0)
         project_probes(0)
-        late = shared([P, 3, CHUNK], F32, "late", "x_bf0")
-        first.update({(1, 2): late[:, 0], (1, 3): late[:, 1], (1, 0): late[:, 2]})
-        second_picks(1, (1,))
-        first_picks(1, (2, 3, 0))
-        second_picks(1, (2, 3))
-        a_last = shared([P, 2, BLOCK, PACK], F32, "a_last", "tab0")
-        for b in range(2):
-            nc.scalar.copy(out=a_last[:, b], in_=transposed_sum("o%d" % b, (a_row[LAST],), b))
-        quantize_wo(0, x1[0][:, 3, :].bitcast(BF16))
+        second_picks(1, (1, 2, 3))
+        ahead = shared([P, 2, CHUNK], F32, "ahead", "x0_turned3")
+        first.update({(2, 1): ahead[:, 0], (LAST, 3): ahead[:, 1]})
+        first.update({(LAST, t): work[:, t * CHUNK : (t + 1) * CHUNK] for t in range(3)})
+        first_picks(2, (1,))
+        first_picks(LAST, (3,))
+        wo_bf = rows[0][:, 2 * ROW - CHUNK :].bitcast(BF16)
+        interleave(wo_bf, wo_raw[:])
+        wo_codes = shared([P, N], U32, "wo_codes")
+        wo_scales = shared([P, N], U8, "wo_scales")
+        for cols in (slice(0, 2 * P), slice(2 * P, N)):
+            quantize(wo_codes[:, cols], wo_scales[:, cols], wo_bf[:, PACK * cols.start : PACK * cols.stop])
         for c in range(1, LAST):
             sum_h(c - 1)
             difference(c - 1)
@@ -428,43 +451,49 @@ def tile_list_pivot_irrigation_kernel(
             codes = quantize_h(c - 1)
             round_probes(c)
             make_gate(c - 1, *codes)
-            if c >= 2:
-                sum_z(c - 2)
-                quantize_z(c - 2)
-            first_picks(c + 1, (1, 2, 3))
+            first_picks(c + 1, (2, 3) if c == 1 else (0, 1, 2))
             quantize_probes(c)
+            if c + 1 == LAST:
+                finish(0)
             project_probes(c)
             if c + 1 < LAST:
+                open_z(0)
                 first[c + 1, 0] = x1[c][:, 1, :]
                 first_picks(c + 1, (0,))
                 interpolate(c - 1, 2)
                 second_picks(c + 1, (1, 2, 3))
-                quantize_wo(1, x1[1][:, 2, :].bitcast(BF16))
-                quantize_wo(2, x1[1][:, 3, :].bitcast(BF16))
-        first[LAST, 0] = shared([P, CHUNK], F32, "first_last", "x_bf2")[:]
-        second_picks(LAST, (1,))
-        first_picks(LAST, (0,))
-        second_picks(LAST, (2, 3, 0))
-        finish(0)
+                second_picks(LAST, (3,))
+                sum_z(0)
+                quantize_z(0)
+        second_picks(LAST, (0, 1, 2))
         sum_h(2)
+        open_z(1)
         round_probes(LAST)
         interpolate(1, 1)
-        sum_z(1)
+        wg_dealt = shared([P, H], U32, "wg_dealt", "plane12")
+        wg_sc_dealt = shared([P, H], U8, "wg_sc_dealt", "plane11")
+        for dealt_tile, natural_tile in ((wg_dealt, wg), (wg_sc_dealt, wg_sc)):
+            nc.vector.tensor_copy(
+                out=dealt_tile[:].rearrange("p (t m) -> p t m", t=PACK), in_=natural_tile[:].rearrange("p (m t) -> p t m", t=PACK)
+            )
         quantize_probes(LAST)
         make_gate(2, *quantize_h(2))
         project_probes(LAST)
+        sum_z(1)
+        open_z(2)
         difference(2)
-        quantize_z(1)
+        tail = shared([P, ROW + H], F32, "tail", "work")
+        h_bf[LAST] = tail[:, ROW:].bitcast(BF16)
 
-        h_bf[LAST] = shared([P, 2 * H], BF16, "h_last")
         for b in range(2):
             nc.vector.tensor_tensor(out=by_token(h_bf[LAST][:, b * H : (b + 1) * H]), in0=b_row[LAST][b], in1=a_last[:, b], op=ADD)
         make_gate(LAST, *quantize_h(LAST))
         interpolate(LAST - 1, 1)
         sum_z(LAST - 1)
+        quantize_z(1)
         finish(1)
         quantize_z(LAST - 1)
-        diff[LAST] = shared([P, ROW], F32, "diff3", "tab1")[:]
+        diff[LAST] = tail[:, :ROW]
         for b in range(2):
             nc.vector.tensor_tensor(out=by_token(diff[LAST][:, b * H : (b + 1) * H]), in0=b_row[LAST][b], in1=a_last[:, b], op=SUB)
         finish(LAST - 1)

@@ -132,7 +132,7 @@ def tile_list_pivot_irrigation_kernel(
                 in_=wm_scales[:, 4 * q : 4 * q + 4, :].bitcast(I32).rearrange("a r c -> r a c"),
             )
 
-        x_bf = [shared([P, PASSES * PACK * CHUNK], BF16, "x_bf%d" % c) for c in range(CHUNKS)]
+        x0_bf = [shared([P, PACK * CHUNK], BF16, "x0_bf%d" % c) for c in range(CHUNKS)]
         x0_turned = [shared([P, 2, 2, P, 2], BF16, "x0_turned%d" % c) for c in range(CHUNKS)]
         sum_banks = {}
 
@@ -191,27 +191,29 @@ def tile_list_pivot_irrigation_kernel(
                     )
                 nc.scalar.copy(out=block_of(a_row[c], b), in_=natural(bank))
 
+        def slot(c, dtype, name):
+            shape = [P, PACK * CHUNK if dtype == BF16 else PASSES * CHUNK]
+            if c % 2:
+                return shared(shape, dtype, name, "x0_turned3")
+            return placed.tile(shape, dtype, name=name, align_bytes=64, offset=4 * PASSES * H)
+
         def round_probes(c):
             if c == LAST:
                 x1_bf[c] = [b_row[1][:, b * H : b * H + CHUNK].bitcast(BF16) for b in range(2)]
-            elif c == 0:
-                x1_bf[c] = [shared([P, PACK * CHUNK], BF16, "x1_bf0", "x0_turned3")[:]]
             else:
-                x1_bf[c] = [x_bf[c][:, PACK * CHUNK :]]
+                x1_bf[c] = [slot(c + 1, BF16, "x1_bf%d" % c)[:]]
             width = CHUNK // len(x1_bf[c])
             for i, piece in enumerate(x1_bf[c]):
                 interleave(piece, x1[c][:, :, i * width : (i + 1) * width])
 
-        def quantize_probes(c):
+        def quantize_pass0(c):
             scales = two.tile([P, PASSES * CHUNK], U8, name="x_scales", align_bytes=64)
-            if c:
-                codes = shared([P, PASSES * CHUNK], U32, "x_codes%d" % c, "plane10" if c == LAST else None)
-            else:
-                codes = placed.tile([P, PASSES * CHUNK], U32, name="x_codes0", align_bytes=64, offset=4 * PASSES * H)
+            codes = slot(c, U32, "x_codes%d" % c)
             x_q[c] = codes, scales
-            if 0 < c < LAST:
-                return quantize(codes[:], scales[:], x_bf[c][:])
-            quantize(codes[:, :CHUNK], scales[:, :CHUNK], x_bf[c][:, : PACK * CHUNK])
+            quantize(codes[:, :CHUNK], scales[:, :CHUNK], x0_bf[c][:])
+
+        def quantize_pass1(c):
+            codes, scales = x_q[c]
             width = CHUNK // len(x1_bf[c])
             for i, piece in enumerate(x1_bf[c]):
                 cols = slice(CHUNK + i * width, CHUNK + (i + 1) * width)
@@ -257,8 +259,8 @@ def tile_list_pivot_irrigation_kernel(
                     )
             return bank[:].rearrange("p t j -> p j t")
 
-        def turn(bank, row, b, opens, closes, ts=range(PACK)):
-            for t in ts:
+        def turn(bank, row, b, opens, closes):
+            for t in range(PACK):
                 nc.tensor.matmul(
                     out=bank[:, t, :],
                     lhsT=block_of(row, b)[:, t // 2, t % 2, :],
@@ -280,17 +282,12 @@ def tile_list_pivot_irrigation_kernel(
                 nc.vector.tensor_tensor(out=dst[:, lo : lo + width], in0=left[:, lo : lo + width], in1=right[:, lo : lo + width], op=op)
 
         def difference(c):
-            diff[c] = rows[c + 1][:, ROW:] if c < LAST - 1 else b_row[1]
-            for half in (slice(H, ROW), slice(0, H)) if c < LAST - 1 else (slice(0, H), slice(H, ROW)):
-                nc.vector.tensor_tensor(out=diff[c][:, half], in0=a_row[c][:, half], in1=b_row[c][:, half], op=SUB)
+            diff[c] = rows[c + 1][:, ROW : 2 * ROW] if c < LAST - 1 else b_row[1]
+            elementwise(diff[c], a_row[c], b_row[c], SUB, 1 if c < LAST - 1 else 2)
 
         def sum_h(c):
             for b in range(2):
-                bank = psum.tile([P, PACK, BLOCK], F32, name="h_bank", tag="h%d" % b)
-                turn(bank, a_row[c], b, True, False, range(PACK - 1))
-                turn(bank, b_row[c], b, False, False)
-                turn(bank, a_row[c], b, False, True, (PACK - 1,))
-                nc.scalar.copy(out=by_token(h_bf[c][:, b * H : (b + 1) * H]), in_=bank[:].rearrange("p t j -> p j t"))
+                nc.scalar.copy(out=by_token(h_bf[c][:, b * H : (b + 1) * H]), in_=transposed_sum("h%d" % b, (a_row[c], b_row[c]), b))
 
         def quantize_pair(name, c, src):
             codes = shared([P, CHUNK], U32, "%s_codes%d" % (name, c), "%s_codes%d" % (name, c % 2))
@@ -299,6 +296,10 @@ def tile_list_pivot_irrigation_kernel(
             for lo in range(0, CHUNK, width):
                 quantize(codes[:, lo : lo + width], scales[:, lo : lo + width], src[:, PACK * lo : PACK * (lo + width)])
             return codes, scales
+
+        def deal(dst, src):
+            nc.vector.tensor_copy(out=dst[:].rearrange("p (t m) -> p t m", t=PACK), in_=src[:].rearrange("p (m t) -> p t m", t=PACK))
+            return dst
 
         def quantize_h(c):
             return quantize_pair("h", c, h_bf[c])
@@ -333,7 +334,7 @@ def tile_list_pivot_irrigation_kernel(
                 turn(z_banks[c][b], b_row[c], b, True, False)
 
         def sum_z(c):
-            z_bf[c] = two.tile([P, 2 * H], BF16, name="z_bf", align_bytes=64)
+            z_bf[c] = shared([P, 2 * H], BF16, "z_bf%d" % c)
             for b in range(2):
                 turn(z_banks[c][b], term[c], b, False, True)
                 nc.scalar.copy(out=by_token(z_bf[c][:, b * H : (b + 1) * H]), in_=z_banks[c][b][:].rearrange("p t j -> p j t"))
@@ -346,7 +347,7 @@ def tile_list_pivot_irrigation_kernel(
             for b in range(2):
                 blk = 2 * c + b
                 cols = slice(b * BLOCK, (b + 1) * BLOCK)
-                bank = psum.tile([P, N // P, BLOCK], F32, name="out_bank", tag="gbho"[c] + str(b))
+                bank = psum.tile([P, N // P, BLOCK], F32, name="out_bank", tag="ggho"[c] + str(b))
                 for n in range(N // P):
                     nc.tensor.matmul_mx(
                         out=bank[:, n, :],
@@ -358,7 +359,7 @@ def tile_list_pivot_irrigation_kernel(
                         stop=True,
                     )
                 staged = four.tile([P, N // P, BLOCK], F32, name="staged")
-                copy = nc.vector.tensor_copy if c >= LAST - 1 and b else nc.scalar.copy
+                copy = nc.vector.tensor_copy if blk == 2 * LAST + 1 else nc.scalar.copy
                 copy(out=staged[:], in_=bank[:])
                 nc.sync.dma_start(
                     out=out.rearrange("(n p) j -> p n j", p=P)[:, :, blk * BLOCK : (blk + 1) * BLOCK], in_=staged[:]
@@ -366,9 +367,9 @@ def tile_list_pivot_irrigation_kernel(
 
         wp_bf = shared([P, PASSES * PACK * H], BF16, "wp_bf")
         gather_pass0(0)
-        round_wp(0)
         planes[0, 1] = load_plane(0, 1)
         gather_pass0(1)
+        round_wp(0)
         v_codes = shared([P, PASSES, S], U32, "v_codes", "wp0_raw")
         wm = keep.tile([P, PASSES, 2 * H], U8, align_bytes=64)
         nc.sync.dma_start(out=wm[:].bitcast(I32), in_=wm_words.bitcast(I32).rearrange("a p c -> p a c"))
@@ -376,7 +377,7 @@ def tile_list_pivot_irrigation_kernel(
             gather_words(a)
             place_scales(2 * a)
             place_scales(2 * a + 1)
-        rows = [shared([P, 2 * ROW + (0 if c else H)], F32, "rows%d" % c, ("plane00", "plane01", "tab0", "tab1")[c]) for c in range(CHUNKS)]
+        rows = [shared([P, 2 * ROW], F32, "rows%d" % c, ("plane00", "plane01", "tab0", "tab1")[c]) for c in range(CHUNKS)]
         a_row.update({c: rows[c][:, :ROW] for c in range(CHUNKS)})
         project_table(LAST)
         a_last = shared([P, 2, BLOCK, PACK], F32, "a_last")
@@ -389,17 +390,14 @@ def tile_list_pivot_irrigation_kernel(
             gather_pass0(t)
         round_wp(1)
 
-        def probe_rows(c):
-            return x_bf[c][:].rearrange("p (a b w) -> p a b w", b=2, a=PASSES)
-
         for c in range(CHUNKS):
             bank = psum.tile([P, 2, 2, BLOCK], F32, name="back_bank", tag="b%d" % (c % 2))
             for b in range(2):
                 for u in range(2):
                     pairs = x0_turned[c][:, b, u].rearrange("j p e -> j (p e)").bitcast(F32)
                     nc.tensor.transpose(out=bank[:, b, u, :], in_=pairs, identity=ident[:])
-            words = probe_rows(c)[:, 0].bitcast(F32)
-            nc.scalar.copy(out=words.rearrange("p b (j u) -> p b j u", u=2), in_=bank[:].rearrange("p b u j -> p b j u"))
+            words = x0_bf[c][:].bitcast(F32)
+            nc.scalar.copy(out=words.rearrange("p (b j u) -> p b j u", b=2, u=2), in_=bank[:].rearrange("p b u j -> p b j u"))
 
         for t in range(PACK):
             planes[1, t] = load_plane(1, t)
@@ -413,16 +411,17 @@ def tile_list_pivot_irrigation_kernel(
         wo_raw = load_weight("wo_raw", wo)
 
         work = shared([P, ROW], F32, "work")
-        for c in range(CHUNKS):
-            first.update({(c, t): work[:, (t - 1) * CHUNK : t * CHUNK] for t in (1, 2, 3)})
-            h_bf[c] = work[:, BLOCK : BLOCK + H].bitcast(BF16)
-            sums = rows[c - 1][:, ROW - CHUNK : 2 * ROW - CHUNK] if 0 < c < LAST else rows[c // 2][:, ROW : 2 * ROW]
-            x1[c] = sums.rearrange("p (t j) -> p t j", t=PACK)
-        first[0, 0] = work[:, 3 * CHUNK :]
-        first[0, 3] = placed.tile([P, CHUNK], F32, name="first03", align_bytes=64, offset=4 * (PASSES * H - BLOCK))[:]
         spacers = shared([P, PACK, CHUNK], F32, "first1", "pick00")
+        sums = shared([P, ROW + 3 * CHUNK], F32, "sums", "pick01")
+        for c, row in enumerate((sums[:, BLOCK : BLOCK + ROW], sums[:, :ROW], sums[:, :ROW], rows[1][:, ROW : 2 * ROW])):
+            x1[c] = row.rearrange("p (t j) -> p t j", t=PACK)
         for t in range(PACK):
-            first[1, t] = spacers[:, t, :]
+            first.update({(0, t): work[:, t * CHUNK : (t + 1) * CHUNK], (1, t): spacers[:, t], (2, t): spacers[:, t], (3, t): x1[2][:, t]})
+        first[LAST, 0] = spacers[:, 0]
+        h_bf[2] = work[:, :H].bitcast(BF16)
+        first[0, 3] = placed.tile([P, CHUNK], F32, name="first03", align_bytes=64, offset=4 * (PASSES * H - BLOCK))[:]
+        h_bf.update({c: sums[:, 3 * BLOCK : 3 * BLOCK + H].bitcast(BF16) for c in range(2)})
+        for t in range(PACK):
             first_picks(0, (t,))
             first_picks(1, (t,))
             second_picks(0, (t,))
@@ -430,75 +429,73 @@ def tile_list_pivot_irrigation_kernel(
         wp_codes = placed.tile([P, PASSES * H], U32, name="wp_codes", align_bytes=64, offset=0)
         wp_scales = shared([P, PASSES * H], U8, "wp_scales")
         quantize(wp_codes[:], wp_scales[:], wp_bf[:])
-        quantize_probes(0)
+        quantize_pass0(0)
+        wg_sc_dealt = deal(shared([P, H], U8, "wg_sc_dealt", "wp_bf"), wg_sc)
+        quantize_pass1(0)
         project_probes(0)
-        second_picks(1, (1, 2, 3))
-        ahead = shared([P, 2, CHUNK], F32, "ahead", "x0_turned3")
-        first.update({(2, 1): ahead[:, 0], (LAST, 3): ahead[:, 1]})
-        first.update({(LAST, t): work[:, t * CHUNK : (t + 1) * CHUNK] for t in range(3)})
-        first_picks(2, (1,))
-        first_picks(LAST, (3,))
-        wo_bf = rows[0][:, 2 * ROW - CHUNK :].bitcast(BF16)
+        second_picks(1, range(PACK))
+        wo_bf = sums[:, ROW:].bitcast(BF16)
         interleave(wo_bf, wo_raw[:])
         wo_codes = shared([P, N], U32, "wo_codes")
         wo_scales = shared([P, N], U8, "wo_scales")
         for cols in (slice(0, 2 * P), slice(2 * P, N)):
             quantize(wo_codes[:, cols], wo_scales[:, cols], wo_bf[:, PACK * cols.start : PACK * cols.stop])
-        for c in range(1, LAST):
-            sum_h(c - 1)
-            difference(c - 1)
-            second_picks(c, (0,))
-            codes = quantize_h(c - 1)
-            round_probes(c)
-            make_gate(c - 1, *codes)
-            first_picks(c + 1, (2, 3) if c == 1 else (0, 1, 2))
-            quantize_probes(c)
-            if c + 1 == LAST:
-                finish(0)
-            project_probes(c)
-            if c + 1 < LAST:
-                open_z(0)
-                first[c + 1, 0] = x1[c][:, 1, :]
-                first_picks(c + 1, (0,))
-                interpolate(c - 1, 2)
-                second_picks(c + 1, (1, 2, 3))
-                second_picks(LAST, (3,))
-                sum_z(0)
-                quantize_z(0)
-        second_picks(LAST, (0, 1, 2))
+        quantize_pass0(1)
+        first_picks(2, range(PACK))
+        round_probes(1)
+        sum_h(0)
+        difference(0)
+        quantize_pass1(1)
+        project_probes(1)
+        second_picks(2, (0,))
+        quantize_pass0(2)
+        first_picks(LAST, (0,))
+        codes = quantize_h(0)
+        second_picks(2, (1, 2, 3))
+        make_gate(0, *codes)
+        open_z(0)
+        round_probes(2)
+        sum_h(1)
+        difference(1)
+        interpolate(0, 1)
+        quantize_pass1(2)
+        sum_z(0)
+        project_probes(2)
+        second_picks(LAST, (0,))
+        quantize_pass0(LAST)
+        make_gate(1, *quantize_h(1))
+        first_picks(LAST, (1, 2, 3))
+        second_picks(LAST, (1, 2, 3))
+        quantize_z(0)
         sum_h(2)
         open_z(1)
         round_probes(LAST)
         interpolate(1, 1)
-        wg_dealt = shared([P, H], U32, "wg_dealt", "plane12")
-        wg_sc_dealt = shared([P, H], U8, "wg_sc_dealt", "plane11")
-        for dealt_tile, natural_tile in ((wg_dealt, wg), (wg_sc_dealt, wg_sc)):
-            nc.vector.tensor_copy(
-                out=dealt_tile[:].rearrange("p (t m) -> p t m", t=PACK), in_=natural_tile[:].rearrange("p (m t) -> p t m", t=PACK)
-            )
-        quantize_probes(LAST)
-        make_gate(2, *quantize_h(2))
+        wg_dealt = deal(shared([P, H], U32, "wg_dealt", "plane13"), wg)
+        codes = quantize_h(2)
+        quantize_pass1(LAST)
+        make_gate(2, *codes)
         project_probes(LAST)
-        sum_z(1)
-        open_z(2)
         difference(2)
+        sum_z(1)
+        finish(0)
+        interpolate(2, 1)
+        open_z(2)
+        sum_z(2)
         tail = shared([P, ROW + H], F32, "tail", "work")
         h_bf[LAST] = tail[:, ROW:].bitcast(BF16)
-
         for b in range(2):
             nc.vector.tensor_tensor(out=by_token(h_bf[LAST][:, b * H : (b + 1) * H]), in0=b_row[LAST][b], in1=a_last[:, b], op=ADD)
         make_gate(LAST, *quantize_h(LAST))
-        interpolate(LAST - 1, 1)
-        sum_z(LAST - 1)
         quantize_z(1)
-        finish(1)
-        quantize_z(LAST - 1)
         diff[LAST] = tail[:, :ROW]
         for b in range(2):
             nc.vector.tensor_tensor(out=by_token(diff[LAST][:, b * H : (b + 1) * H]), in0=b_row[LAST][b], in1=a_last[:, b], op=SUB)
-        finish(LAST - 1)
+        quantize_z(2)
         interpolate(LAST, 2)
-        z_bf[LAST] = two.tile([P, 2 * H], BF16, name="z_bf", align_bytes=64)
+        finish(1)
+        finish(2)
+        z_bf[LAST] = shared([P, 2 * H], BF16, "z_bf3", "pick10")
         for b in range(2):
             nc.vector.tensor_tensor(
                 out=by_token(z_bf[LAST][:, b * H : (b + 1) * H]), in0=by_token(term[LAST][:, b * H : (b + 1) * H]), in1=a_last[:, b], op=ADD

@@ -92,10 +92,12 @@ def tile_list_pivot_irrigation_kernel(
             nc.sync.dma_start(out=tab[:].bitcast(I32), in_=tab_words[a].rearrange("p c t -> p (c t)").bitcast(I32))
             return tab
 
-        def round_wp(a):
-            raw = load_weight("wp%d_raw" % a, wp[a * K_PASS : (a + 1) * K_PASS, :])
+        def round_wp(a, lo, hi, tag):
+            raw = shared([P, PACK, PACK * (hi - lo)], F32, "wp%d_raw%d" % (a, lo), tag)
+            rows = wp[a * K_PASS : (a + 1) * K_PASS, PACK * lo : PACK * hi]
+            nc.sync.dma_start(out=raw[:], in_=rows.rearrange("(p t) c -> p t c", t=PACK))
             nc.scalar.copy(
-                out=wp_bf[:, a * PACK * H : (a + 1) * PACK * H].rearrange("p (t m j) -> p m t j", t=PACK, j=PACK),
+                out=wp_bf[:, a * PACK * H : (a + 1) * PACK * H].rearrange("p (t m j) -> p m t j", t=PACK, j=PACK)[:, lo:hi],
                 in_=raw[:].rearrange("p j (m t) -> p m t j", t=PACK),
             )
 
@@ -298,7 +300,7 @@ def tile_list_pivot_irrigation_kernel(
             return codes, scales
 
         def deal(dst, src):
-            nc.vector.tensor_copy(out=dst[:].rearrange("p (t m) -> p t m", t=PACK), in_=src[:].rearrange("p (m t) -> p t m", t=PACK))
+            nc.vector.tensor_copy(out=dst[:].rearrange("p (t m) -> p m t", t=PACK), in_=src[:].rearrange("p (m t) -> p m t", t=PACK))
             return dst
 
         def quantize_h(c):
@@ -369,7 +371,7 @@ def tile_list_pivot_irrigation_kernel(
         gather_pass0(0)
         planes[0, 1] = load_plane(0, 1)
         gather_pass0(1)
-        round_wp(0)
+        round_wp(0, 0, P // 2, "wp0_raw")
         v_codes = shared([P, PASSES, S], U32, "v_codes", "wp0_raw")
         wm = keep.tile([P, PASSES, 2 * H], U8, align_bytes=64)
         nc.sync.dma_start(out=wm[:].bitcast(I32), in_=wm_words.bitcast(I32).rearrange("a p c -> p a c"))
@@ -377,6 +379,8 @@ def tile_list_pivot_irrigation_kernel(
             gather_words(a)
             place_scales(2 * a)
             place_scales(2 * a + 1)
+        planes[0, 2] = load_plane(0, 2)
+        round_wp(0, P // 2, P, None)
         rows = [shared([P, 2 * ROW], F32, "rows%d" % c, ("plane00", "plane01", "tab0", "tab1")[c]) for c in range(CHUNKS)]
         a_row.update({c: rows[c][:, :ROW] for c in range(CHUNKS)})
         project_table(LAST)
@@ -385,10 +389,10 @@ def tile_list_pivot_irrigation_kernel(
             nc.scalar.copy(out=a_last[:, b], in_=transposed_sum("b%d" % b, (a_row[LAST],), b))
         for c in range(LAST):
             project_table(c)
-        for t in (2, 3):
-            planes[0, t] = load_plane(0, t)
-            gather_pass0(t)
-        round_wp(1)
+        gather_pass0(2)
+        planes[0, 3] = load_plane(0, 3)
+        gather_pass0(3)
+        round_wp(1, 0, P, "wp1_raw")
 
         for c in range(CHUNKS):
             bank = psum.tile([P, 2, 2, BLOCK], F32, name="back_bank", tag="b%d" % (c % 2))
@@ -417,7 +421,7 @@ def tile_list_pivot_irrigation_kernel(
             x1[c] = row.rearrange("p (t j) -> p t j", t=PACK)
         for t in range(PACK):
             first.update({(0, t): work[:, t * CHUNK : (t + 1) * CHUNK], (1, t): spacers[:, t], (2, t): spacers[:, t], (3, t): x1[2][:, t]})
-        first[LAST, 0] = spacers[:, 0]
+        first[LAST, 0] = spacers[:, 1]
         h_bf[2] = work[:, :H].bitcast(BF16)
         first[0, 3] = placed.tile([P, CHUNK], F32, name="first03", align_bytes=64, offset=4 * (PASSES * H - BLOCK))[:]
         h_bf.update({c: sums[:, 3 * BLOCK : 3 * BLOCK + H].bitcast(BF16) for c in range(2)})
@@ -449,9 +453,9 @@ def tile_list_pivot_irrigation_kernel(
         project_probes(1)
         second_picks(2, (0,))
         quantize_pass0(2)
-        first_picks(LAST, (0,))
         codes = quantize_h(0)
         second_picks(2, (1, 2, 3))
+        first_picks(LAST, (0,))
         make_gate(0, *codes)
         open_z(0)
         round_probes(2)

@@ -231,7 +231,7 @@ def tile_list_pivot_irrigation_kernel(
                         (wp_codes[:, a * H : (a + 1) * H], wp_scales[:, a * H : (a + 1) * H], codes[:, cols[a]], scales[:, cols[a]])
                         for a in range(PASSES)
                     ]
-                    b_row[c][b] = channel_product("o%d" % b, passes)
+                    b_row[c][b] = channel_product("h%d" % b, passes)
                     continue
                 bank = psum.tile([P, H], F32, name="b_bank", tag="b%d" % b)
                 for a in range(PASSES):
@@ -331,7 +331,7 @@ def tile_list_pivot_irrigation_kernel(
             elementwise(term[c], gate[c], diff[c], MULT, pieces)
 
         def open_z(c):
-            z_banks[c] = [psum.tile([P, PACK, BLOCK], F32, name="z_bank", tag="obh"[c] + str(b)) for b in range(2)]
+            z_banks[c] = [psum.tile([P, PACK, BLOCK], F32, name="z_bank", tag="obo"[c] + str(b)) for b in range(2)]
             for b in range(2):
                 turn(z_banks[c][b], b_row[c], b, True, False)
 
@@ -349,7 +349,7 @@ def tile_list_pivot_irrigation_kernel(
             for b in range(2):
                 blk = 2 * c + b
                 cols = slice(b * BLOCK, (b + 1) * BLOCK)
-                bank = psum.tile([P, N // P, BLOCK], F32, name="out_bank", tag="ggho"[c] + str(b))
+                bank = psum.tile([P, N // P, BLOCK], F32, name="out_bank", tag="ggoh"[c] + str(b))
                 for n in range(N // P):
                     nc.tensor.matmul_mx(
                         out=bank[:, n, :],
@@ -430,11 +430,12 @@ def tile_list_pivot_irrigation_kernel(
             first_picks(1, (t,))
             second_picks(0, (t,))
         round_probes(0)
+        wg_sc_dealt = deal(shared([P, H], U8, "wg_sc_dealt"), wg_sc)
         wp_codes = placed.tile([P, PASSES * H], U32, name="wp_codes", align_bytes=64, offset=0)
         wp_scales = shared([P, PASSES * H], U8, "wp_scales")
         quantize(wp_codes[:], wp_scales[:], wp_bf[:])
         quantize_pass0(0)
-        wg_sc_dealt = deal(shared([P, H], U8, "wg_sc_dealt", "wp_bf"), wg_sc)
+        wg_dealt = deal(shared([P, H], U32, "wg_dealt"), wg)
         quantize_pass1(0)
         project_probes(0)
         second_picks(1, range(PACK))
@@ -463,24 +464,23 @@ def tile_list_pivot_irrigation_kernel(
         difference(1)
         interpolate(0, 1)
         quantize_pass1(2)
-        sum_z(0)
         project_probes(2)
         second_picks(LAST, (0,))
         quantize_pass0(LAST)
         make_gate(1, *quantize_h(1))
         first_picks(LAST, (1, 2, 3))
         second_picks(LAST, (1, 2, 3))
-        quantize_z(0)
         sum_h(2)
         open_z(1)
         round_probes(LAST)
+        sum_z(0)
         interpolate(1, 1)
-        wg_dealt = deal(shared([P, H], U32, "wg_dealt", "plane13"), wg)
         codes = quantize_h(2)
         quantize_pass1(LAST)
         make_gate(2, *codes)
         project_probes(LAST)
         difference(2)
+        quantize_z(0)
         sum_z(1)
         finish(0)
         interpolate(2, 1)

@@ -159,7 +159,7 @@ def tile_list_pivot_irrigation_kernel(
                     if (e, probe) == (1, 1):
                         nc.scalar.copy(out=x0_turned[c][:, :, u], in_=sum_banks[c][:].rearrange("j b e p -> j b p e"))
 
-        first, x1, a_row, b_row, diff, h_bf, gate, term, z_bf, z_q, x_q, z_banks, x1_bf = ({} for name in range(13))
+        first, x1, a_row, b_row, diff, h_bf, gate, term, z_bf, z_q, x_q, z_banks, x1_bf, b_room = ({} for name in range(14))
 
         def first_picks(c, ts):
             for t in ts:
@@ -180,7 +180,7 @@ def tile_list_pivot_irrigation_kernel(
         def project_table(c):
             for b in range(2):
                 blk = 2 * c + b
-                bank = psum.tile([P, H], F32, name="a_bank", tag="ob"[c % 2] + str(b))
+                bank = psum.tile([P, H], F32, name="a_bank", tag="gobh"[c] + str(b))
                 for a in range(PASSES):
                     nc.tensor.matmul_mx(
                         out=bank[:],
@@ -196,12 +196,12 @@ def tile_list_pivot_irrigation_kernel(
         def slot(c, dtype, name):
             shape = [P, PACK * CHUNK if dtype == BF16 else PASSES * CHUNK]
             if c % 2:
-                return shared(shape, dtype, name, "x0_turned3")
+                return shared(shape, dtype, name, "x0_turned1")
             return placed.tile(shape, dtype, name=name, align_bytes=64, offset=4 * PASSES * H)
 
         def round_probes(c):
             if c == LAST:
-                x1_bf[c] = [b_row[1][:, b * H : b * H + CHUNK].bitcast(BF16) for b in range(2)]
+                x1_bf[c] = [b_row[1][:, lo : lo + CHUNK].bitcast(BF16) for lo in (0, ROW - CHUNK)]
             else:
                 x1_bf[c] = [slot(c + 1, BF16, "x1_bf%d" % c)[:]]
             width = CHUNK // len(x1_bf[c])
@@ -223,7 +223,8 @@ def tile_list_pivot_irrigation_kernel(
 
         def project_probes(c):
             codes, scales = x_q[c]
-            b_row[c] = {} if c == LAST else two.tile([P, ROW], F32, name="b_row", align_bytes=64)[:]
+            b_room[c] = None if c == LAST else two.tile([P, CHUNK + ROW], F32, name="b_row", align_bytes=64)
+            b_row[c] = {} if c == LAST else b_room[c][:, CHUNK:]
             for b in range(2):
                 cols = [slice(a * CHUNK + b * BLOCK, a * CHUNK + (b + 1) * BLOCK) for a in range(PASSES)]
                 if c == LAST:
@@ -284,8 +285,8 @@ def tile_list_pivot_irrigation_kernel(
                 nc.vector.tensor_tensor(out=dst[:, lo : lo + width], in0=left[:, lo : lo + width], in1=right[:, lo : lo + width], op=op)
 
         def difference(c):
-            diff[c] = rows[c + 1][:, ROW : 2 * ROW] if c < LAST - 1 else b_row[1]
-            elementwise(diff[c], a_row[c], b_row[c], SUB, 1 if c < LAST - 1 else 2)
+            diff[c] = rows[c + 1][:, ROW : 2 * ROW] if c < LAST - 1 else b_room[1][:, :ROW]
+            elementwise(diff[c], a_row[c], b_row[c], SUB, 1)
 
         def sum_h(c):
             for b in range(2):
@@ -373,20 +374,20 @@ def tile_list_pivot_irrigation_kernel(
         gather_pass0(1)
         round_wp(0, 0, P // 2, "wp0_raw")
         v_codes = shared([P, PASSES, S], U32, "v_codes", "wp0_raw")
-        wm = keep.tile([P, PASSES, 2 * H], U8, align_bytes=64)
-        nc.sync.dma_start(out=wm[:].bitcast(I32), in_=wm_words.bitcast(I32).rearrange("a p c -> p a c"))
         for a in range(PASSES):
             gather_words(a)
             place_scales(2 * a)
             place_scales(2 * a + 1)
         planes[0, 2] = load_plane(0, 2)
         round_wp(0, P // 2, P, None)
+        wm = keep.tile([P, PASSES, 2 * H], U8, align_bytes=64)
+        nc.sync.dma_start(out=wm[:].bitcast(I32), in_=wm_words.bitcast(I32).rearrange("a p c -> p a c"))
         rows = [shared([P, 2 * ROW], F32, "rows%d" % c, ("plane00", "plane01", "tab0", "tab1")[c]) for c in range(CHUNKS)]
         a_row.update({c: rows[c][:, :ROW] for c in range(CHUNKS)})
         project_table(LAST)
         a_last = shared([P, 2, BLOCK, PACK], F32, "a_last")
         for b in range(2):
-            nc.scalar.copy(out=a_last[:, b], in_=transposed_sum("b%d" % b, (a_row[LAST],), b))
+            nc.scalar.copy(out=a_last[:, b], in_=transposed_sum("o%d" % b, (a_row[LAST],), b))
         for c in range(LAST):
             project_table(c)
         gather_pass0(2)
@@ -394,7 +395,7 @@ def tile_list_pivot_irrigation_kernel(
         gather_pass0(3)
         round_wp(1, 0, P, "wp1_raw")
 
-        for c in range(CHUNKS):
+        def turn_back(c):
             bank = psum.tile([P, 2, 2, BLOCK], F32, name="back_bank", tag="b%d" % (c % 2))
             for b in range(2):
                 for u in range(2):
@@ -403,6 +404,8 @@ def tile_list_pivot_irrigation_kernel(
             words = x0_bf[c][:].bitcast(F32)
             nc.scalar.copy(out=words.rearrange("p (b j u) -> p b j u", b=2, u=2), in_=bank[:].rearrange("p b u j -> p b j u"))
 
+        turn_back(0)
+        turn_back(1)
         for t in range(PACK):
             planes[1, t] = load_plane(1, t)
         for q in range(QUADRANTS):
@@ -430,6 +433,8 @@ def tile_list_pivot_irrigation_kernel(
             first_picks(1, (t,))
             second_picks(0, (t,))
         round_probes(0)
+        turn_back(2)
+        turn_back(3)
         wg_sc_dealt = deal(shared([P, H], U8, "wg_sc_dealt"), wg_sc)
         wp_codes = placed.tile([P, PASSES * H], U32, name="wp_codes", align_bytes=64, offset=0)
         wp_scales = shared([P, PASSES * H], U8, "wp_scales")

@@ -304,6 +304,18 @@ def tile_list_pivot_irrigation_kernel(
             nc.vector.tensor_copy(out=dst[:].rearrange("p (t m) -> p m t", t=PACK), in_=src[:].rearrange("p (m t) -> p m t", t=PACK))
             return dst
 
+        def warm_up(tag):
+            bank = psum.tile([P, H], F32, name="warm_bank", tag=tag)
+            nc.tensor.matmul_mx(
+                out=bank[:],
+                lhsT=wp_codes[:, :P].bitcast(FP8X4),
+                lhsT_scale=wp_scales[:, :P],
+                rhs=wp_codes[:, :H].bitcast(FP8X4),
+                rhs_scale=wp_scales[:, :H],
+                start=True,
+                stop=True,
+            )
+
         def quantize_h(c):
             return quantize_pair("h", c, h_bf[c])
 
@@ -479,6 +491,8 @@ def tile_list_pivot_irrigation_kernel(
         open_z(1)
         round_probes(LAST)
         sum_z(0)
+        warm_up("g0")
+        warm_up("g1")
         interpolate(1, 1)
         codes = quantize_h(2)
         quantize_pass1(LAST)

@@ -279,14 +279,14 @@ def tile_list_pivot_irrigation_kernel(
                 turn(bank, row, b, order == 0, order == len(rows) - 1)
             return bank[:].rearrange("p t j -> p j t")
 
-        def elementwise(dst, left, right, op, pieces):
+        def elementwise(engine, dst, left, right, op, pieces):
             width = ROW // pieces
             for lo in range(0, ROW, width):
-                nc.vector.tensor_tensor(out=dst[:, lo : lo + width], in0=left[:, lo : lo + width], in1=right[:, lo : lo + width], op=op)
+                engine.tensor_tensor(out=dst[:, lo : lo + width], in0=left[:, lo : lo + width], in1=right[:, lo : lo + width], op=op)
 
         def difference(c):
-            diff[c] = rows[c + 1][:, ROW : 2 * ROW] if c < LAST - 1 else b_room[1][:, :ROW]
-            elementwise(diff[c], a_row[c], b_row[c], SUB, 1)
+            diff[c] = shared([P, ROW], F32, "diff%d" % c, ("x0_bf1", "first_last")[c])[:] if c < 2 else b_room[1][:, :ROW]
+            elementwise(nc.gpsimd if c < 2 else nc.vector, diff[c], a_row[c], b_row[c], SUB, 1)
 
         def sum_h(c):
             for b in range(2):
@@ -340,8 +340,8 @@ def tile_list_pivot_irrigation_kernel(
                 nc.scalar.activation(out=block_of(gate[c], b), in_=natural(bank), func=SIGMOID)
 
         def interpolate(c, pieces):
-            term[c] = two.tile([P, ROW], F32, name="term")[:]
-            elementwise(term[c], gate[c], diff[c], MULT, pieces)
+            term[c] = spacers[:, CHUNK : CHUNK + ROW] if c == 0 else two.tile([P, ROW], F32, name="term")[:]
+            elementwise(nc.vector, term[c], gate[c], diff[c], MULT, pieces)
 
         def open_z(c):
             z_banks[c] = [psum.tile([P, PACK, BLOCK], F32, name="z_bank", tag="obo"[c] + str(b)) for b in range(2)]
@@ -430,16 +430,19 @@ def tile_list_pivot_irrigation_kernel(
         wo_raw = load_weight("wo_raw", wo)
 
         work = shared([P, ROW], F32, "work")
-        spacers = shared([P, PACK, CHUNK], F32, "first1", "pick00")
+        spacers = shared([P, 5 * CHUNK + BLOCK], F32, "first1", "pick00")
+        first_last = shared([P, CHUNK], F32, "first_last")
         sums = shared([P, ROW + 3 * CHUNK], F32, "sums", "pick01")
-        for c, row in enumerate((sums[:, BLOCK : BLOCK + ROW], sums[:, :ROW], sums[:, :ROW], rows[1][:, ROW : 2 * ROW])):
+        for c, row in enumerate((sums[:, BLOCK : BLOCK + ROW], sums[:, :ROW], sums[:, :ROW], rows[1][:, ROW - CHUNK : 2 * ROW - CHUNK])):
             x1[c] = row.rearrange("p (t j) -> p t j", t=PACK)
         for t in range(PACK):
-            first.update({(0, t): work[:, t * CHUNK : (t + 1) * CHUNK], (1, t): spacers[:, t], (2, t): spacers[:, t], (3, t): x1[2][:, t]})
-        first[LAST, 0] = spacers[:, 1]
+            lo = (0, CHUNK + BLOCK, 3 * CHUNK + BLOCK, 0)[t]
+            spacer = first_last[:] if t == 3 else spacers[:, lo : lo + CHUNK]
+            first.update({(0, t): work[:, t * CHUNK : (t + 1) * CHUNK], (1, t): spacer, (2, t): spacer})
+            first[LAST, t] = spacers[:, (t + 1) * CHUNK : (t + 2) * CHUNK]
         h_bf[2] = work[:, :H].bitcast(BF16)
         first[0, 3] = placed.tile([P, CHUNK], F32, name="first03", align_bytes=64, offset=4 * (PASSES * H - BLOCK))[:]
-        h_bf.update({c: sums[:, 3 * BLOCK : 3 * BLOCK + H].bitcast(BF16) for c in range(2)})
+        h_bf.update({0: sums[:, 3 * BLOCK : 3 * BLOCK + H].bitcast(BF16), 1: rows[1][:, ROW + BLOCK : ROW + BLOCK + H].bitcast(BF16)})
         for t in range(PACK):
             first_picks(0, (t,))
             first_picks(1, (t,))
@@ -473,20 +476,20 @@ def tile_list_pivot_irrigation_kernel(
         quantize_pass0(2)
         codes = quantize_h(0)
         second_picks(2, (1, 2, 3))
-        first_picks(LAST, (0,))
+        first_picks(LAST, range(PACK))
         make_gate(0, *codes)
         open_z(0)
-        round_probes(2)
         sum_h(1)
+        round_probes(2)
         difference(1)
-        interpolate(0, 1)
         quantize_pass1(2)
+        codes = quantize_h(1)
         project_probes(2)
+        make_gate(1, *codes)
         second_picks(LAST, (0,))
         quantize_pass0(LAST)
-        make_gate(1, *quantize_h(1))
-        first_picks(LAST, (1, 2, 3))
         second_picks(LAST, (1, 2, 3))
+        interpolate(0, 1)
         sum_h(2)
         open_z(1)
         round_probes(LAST)

@@ -60,7 +60,6 @@ def tile_list_pivot_irrigation_kernel(
     with ExitStack() as ctx:
         keep = ctx.enter_context(tc.tile_pool(name="keep", bufs=1))
         two = ctx.enter_context(tc.tile_pool(name="two", bufs=2))
-        four = ctx.enter_context(tc.tile_pool(name="four", bufs=6))
         placed = ctx.enter_context(tc.tile_pool(name="placed", bufs=1))
         psum = ctx.enter_context(tc.psum_pool(name="psum", bufs=1))
 
@@ -196,12 +195,14 @@ def tile_list_pivot_irrigation_kernel(
         def slot(c, dtype, name):
             shape = [P, PACK * CHUNK if dtype == BF16 else PASSES * CHUNK]
             if c % 2:
-                return shared(shape, dtype, name, "x0_turned1")
+                return shared(shape, dtype, name, "x0_bf2" if c == LAST else "x0_turned1")
             return placed.tile(shape, dtype, name=name, align_bytes=64, offset=4 * PASSES * H)
 
         def round_probes(c):
             if c == LAST:
                 x1_bf[c] = [b_row[1][:, lo : lo + CHUNK].bitcast(BF16) for lo in (0, ROW - CHUNK)]
+            elif c == 2:
+                x1_bf[c] = [late_room[:, :H].bitcast(BF16)]
             else:
                 x1_bf[c] = [slot(c + 1, BF16, "x1_bf%d" % c)[:]]
             width = CHUNK // len(x1_bf[c])
@@ -301,7 +302,7 @@ def tile_list_pivot_irrigation_kernel(
             return codes, scales
 
         def deal(dst, src):
-            nc.vector.tensor_copy(out=dst[:].rearrange("p (t m) -> p m t", t=PACK), in_=src[:].rearrange("p (m t) -> p m t", t=PACK))
+            nc.gpsimd.tensor_copy(out=dst[:].rearrange("p (t m) -> p m t", t=PACK), in_=src[:].rearrange("p (m t) -> p m t", t=PACK))
             return dst
 
         def warm_up(tag):
@@ -340,7 +341,7 @@ def tile_list_pivot_irrigation_kernel(
                 nc.scalar.activation(out=block_of(gate[c], b), in_=natural(bank), func=SIGMOID)
 
         def interpolate(c, pieces):
-            term[c] = spacers[:, CHUNK : CHUNK + ROW] if c == 0 else two.tile([P, ROW], F32, name="term")[:]
+            term[c] = spacers[:, :ROW] if c == 0 else two.tile([P, ROW], F32, name="term")[:]
             elementwise(nc.vector, term[c], gate[c], diff[c], MULT, pieces)
 
         def open_z(c):
@@ -356,6 +357,8 @@ def tile_list_pivot_irrigation_kernel(
 
         def quantize_z(c):
             z_q[c] = quantize_pair("z", c, z_bf[c])
+
+        stage_tags = ("plane02", "plane03", "plane10", "plane11", "plane12", "plane13", "wp1_raw", "wo_raw")
 
         def finish(c):
             codes, scales = z_q[c]
@@ -373,7 +376,7 @@ def tile_list_pivot_irrigation_kernel(
                         start=True,
                         stop=True,
                     )
-                staged = four.tile([P, N // P, BLOCK], F32, name="staged")
+                staged = shared([P, N // P, BLOCK], F32, "staged%d" % blk, stage_tags[blk])
                 copy = nc.vector.tensor_copy if blk == 2 * LAST + 1 else nc.scalar.copy
                 copy(out=staged[:], in_=bank[:])
                 nc.sync.dma_start(
@@ -404,6 +407,15 @@ def tile_list_pivot_irrigation_kernel(
             project_table(c)
         gather_pass0(2)
         planes[0, 3] = load_plane(0, 3)
+        for q in range(QUADRANTS):
+            nc.sync.dma_start(
+                out=wg_sc[32 * q : 32 * q + 4, :].bitcast(I32),
+                in_=wg_scales[0, 4 * q : 4 * q + 4, :].bitcast(I32),
+            )
+        wg = keep.tile([P, H], U32, align_bytes=64)
+        nc.sync.dma_start(out=wg[:].bitcast(I32), in_=wg_words[0].rearrange("p c t -> p (c t)").bitcast(I32))
+        wg_sc_dealt = deal(shared([P, H], U8, "wg_sc_dealt"), wg_sc)
+        wg_dealt = deal(shared([P, H], U32, "wg_dealt"), wg)
         gather_pass0(3)
         round_wp(1, 0, P, "wp1_raw")
 
@@ -420,29 +432,22 @@ def tile_list_pivot_irrigation_kernel(
         turn_back(1)
         for t in range(PACK):
             planes[1, t] = load_plane(1, t)
-        for q in range(QUADRANTS):
-            nc.sync.dma_start(
-                out=wg_sc[32 * q : 32 * q + 4, :].bitcast(I32),
-                in_=wg_scales[0, 4 * q : 4 * q + 4, :].bitcast(I32),
-            )
-        wg = keep.tile([P, H], U32, align_bytes=64)
-        nc.sync.dma_start(out=wg[:].bitcast(I32), in_=wg_words[0].rearrange("p c t -> p (c t)").bitcast(I32))
         wo_raw = load_weight("wo_raw", wo)
 
         work = shared([P, ROW], F32, "work")
         spacers = shared([P, 5 * CHUNK + BLOCK], F32, "first1", "pick00")
         first_last = shared([P, CHUNK], F32, "first_last")
         sums = shared([P, ROW + 3 * CHUNK], F32, "sums", "pick01")
-        for c, row in enumerate((sums[:, BLOCK : BLOCK + ROW], sums[:, :ROW], sums[:, :ROW], rows[1][:, ROW - CHUNK : 2 * ROW - CHUNK])):
+        for c, row in enumerate((sums[:, BLOCK : BLOCK + ROW], sums[:, :ROW], sums[:, :ROW])):
             x1[c] = row.rearrange("p (t j) -> p t j", t=PACK)
         for t in range(PACK):
-            lo = (0, CHUNK + BLOCK, 3 * CHUNK + BLOCK, 0)[t]
-            spacer = first_last[:] if t == 3 else spacers[:, lo : lo + CHUNK]
+            lo = (0, CHUNK + BLOCK, 0, 3 * CHUNK + BLOCK)[t]
+            spacer = first_last[:] if t == 2 else spacers[:, lo : lo + CHUNK]
             first.update({(0, t): work[:, t * CHUNK : (t + 1) * CHUNK], (1, t): spacer, (2, t): spacer})
             first[LAST, t] = spacers[:, (t + 1) * CHUNK : (t + 2) * CHUNK]
         h_bf[2] = work[:, :H].bitcast(BF16)
         first[0, 3] = placed.tile([P, CHUNK], F32, name="first03", align_bytes=64, offset=4 * (PASSES * H - BLOCK))[:]
-        h_bf.update({0: sums[:, 3 * BLOCK : 3 * BLOCK + H].bitcast(BF16), 1: rows[1][:, ROW + BLOCK : ROW + BLOCK + H].bitcast(BF16)})
+        h_bf[0] = sums[:, 3 * BLOCK : 3 * BLOCK + H].bitcast(BF16)
         for t in range(PACK):
             first_picks(0, (t,))
             first_picks(1, (t,))
@@ -450,12 +455,10 @@ def tile_list_pivot_irrigation_kernel(
         round_probes(0)
         turn_back(2)
         turn_back(3)
-        wg_sc_dealt = deal(shared([P, H], U8, "wg_sc_dealt"), wg_sc)
         wp_codes = placed.tile([P, PASSES * H], U32, name="wp_codes", align_bytes=64, offset=0)
         wp_scales = shared([P, PASSES * H], U8, "wp_scales")
         quantize(wp_codes[:], wp_scales[:], wp_bf[:])
         quantize_pass0(0)
-        wg_dealt = deal(shared([P, H], U32, "wg_dealt"), wg)
         quantize_pass1(0)
         project_probes(0)
         second_picks(1, range(PACK))
@@ -475,6 +478,10 @@ def tile_list_pivot_irrigation_kernel(
         second_picks(2, (0,))
         quantize_pass0(2)
         codes = quantize_h(0)
+        quantize_pass0(LAST)
+        late_room = shared([P, ROW + CHUNK], F32, "late_room", "x0_turned1")
+        h_bf[1] = late_room[:, 5 * BLOCK : 5 * BLOCK + H].bitcast(BF16)
+        x1[LAST] = late_room[:, CHUNK:].rearrange("p (t j) -> p t j", t=PACK)
         second_picks(2, (1, 2, 3))
         first_picks(LAST, range(PACK))
         make_gate(0, *codes)
@@ -486,9 +493,7 @@ def tile_list_pivot_irrigation_kernel(
         codes = quantize_h(1)
         project_probes(2)
         make_gate(1, *codes)
-        second_picks(LAST, (0,))
-        quantize_pass0(LAST)
-        second_picks(LAST, (1, 2, 3))
+        second_picks(LAST, range(PACK))
         interpolate(0, 1)
         sum_h(2)
         open_z(1)

@@ -305,18 +305,6 @@ def tile_list_pivot_irrigation_kernel(
             nc.gpsimd.tensor_copy(out=dst[:].rearrange("p (t m) -> p m t", t=PACK), in_=src[:].rearrange("p (m t) -> p m t", t=PACK))
             return dst
 
-        def warm_up(tag):
-            bank = psum.tile([P, H], F32, name="warm_bank", tag=tag)
-            nc.tensor.matmul_mx(
-                out=bank[:],
-                lhsT=wp_codes[:, :P].bitcast(FP8X4),
-                lhsT_scale=wp_scales[:, :P],
-                rhs=wp_codes[:, :H].bitcast(FP8X4),
-                rhs_scale=wp_scales[:, :H],
-                start=True,
-                stop=True,
-            )
-
         def quantize_h(c):
             return quantize_pair("h", c, h_bf[c])
 
@@ -499,8 +487,6 @@ def tile_list_pivot_irrigation_kernel(
         open_z(1)
         round_probes(LAST)
         sum_z(0)
-        warm_up("g0")
-        warm_up("g1")
         interpolate(1, 1)
         codes = quantize_h(2)
         quantize_pass1(LAST)

from contextlib import ExitStack

import concourse.mybir as mybir
from concourse.masks import make_identity

K, H, N, T, S = 1024, 512, 384, 2048, 1024
FLOPS = 2 * S * (2 * K * H + H * H + H * N)

F32 = mybir.dt.float32
BF16 = mybir.dt.bfloat16
I32 = mybir.dt.int32
U32 = mybir.dt.uint32
U16 = mybir.dt.uint16
U8 = mybir.dt.uint8
FP8X4 = mybir.dt.float8_e4m3fn_x4
FP4X4 = mybir.dt.float4_e2m1fn_x4
ADD = mybir.AluOpType.add
SUB = mybir.AluOpType.subtract
MULT = mybir.AluOpType.mult
SIGMOID = mybir.ActivationFunctionType.Sigmoid

P = 128
PACK = 4
K_PASS = P * PACK
PASSES = K // K_PASS
QUADRANTS = 4
SCALE_ROWS = 16
GROUP = 16
BLOCK = 128
CHUNK = 2 * BLOCK
CHUNKS = S // CHUNK
LAST = CHUNKS - 1
ROW = 2 * H


def entries(offsets, first, count):
    return offsets[:, first // GROUP : (first + count) // GROUP]


def by_token(row):
    return row.rearrange("p (j t) -> p j t", t=PACK)


def block_of(row, b):
    return row.rearrange("j (g b u p) -> j g b u p", g=2, b=2, u=2)[:, :, b]


def natural(bank):
    return bank[:].rearrange("j (p g u) -> j g u p", g=2, u=2)


def dealt(bank):
    return bank[:].rearrange("j (g u p) -> j g u p", g=2, u=2)


def tile_list_pivot_irrigation_kernel(
    tc, tab_words, tab_scales, offs, xT, offs2, offs3, wm_words, wm_scales, wp, wg_words, wg_scales, wo, out
):
    nc = tc.nc
    with ExitStack() as ctx:
        keep = ctx.enter_context(tc.tile_pool(name="keep", bufs=1))
        two = ctx.enter_context(tc.tile_pool(name="two", bufs=2))
        placed = ctx.enter_context(tc.tile_pool(name="placed", bufs=1))
        psum = ctx.enter_context(tc.psum_pool(name="psum", bufs=1))

        def shared(shape, dtype, name, tag=None):
            return keep.tile(shape, dtype, name=name, tag=tag or name, align_bytes=64)

        def interleave(dst, src):
            nc.scalar.copy(
                out=dst.rearrange("p (c i t) -> p c t i", i=2, t=PACK),
                in_=src.rearrange("p t (c i) -> p c t i", i=2),
            )

        def quantize(codes, scales, src):
            nc.vector.quantize_mx(out=codes.bitcast(FP8X4), scales=scales, in_=src)

        def load_plane(a, t):
            plane = shared([P, T], F32, "plane%d%d" % (a, t))
            rows = xT[a * K_PASS : (a + 1) * K_PASS, :].rearrange("(p t) c -> p t c", t=PACK)
            nc.sync.dma_start(out=plane[:], in_=rows[:, t, :])
            return plane

        def load_weight(name, rows):
            raw = shared([P, PACK, rows.shape[1]], F32, name)
            nc.sync.dma_start(out=raw[:], in_=rows.rearrange("(p t) c -> p t c", t=PACK))
            return raw

        def load_words(a):
            tab = shared([P, T], U32, "tab%d" % a)
            nc.sync.dma_start(out=tab[:].bitcast(I32), in_=tab_words[a].rearrange("p c t -> p (c t)").bitcast(I32))
            return tab

        def round_wp(a, lo, hi, tag):
            raw = shared([P, PACK, PACK * (hi - lo)], F32, "wp%d_raw%d" % (a, lo), tag)
            rows = wp[a * K_PASS : (a + 1) * K_PASS, PACK * lo : PACK * hi]
            nc.sync.dma_start(out=raw[:], in_=rows.rearrange("(p t) c -> p t c", t=PACK))
            nc.scalar.copy(
                out=wp_bf[:, a * PACK * H : (a + 1) * PACK * H].rearrange("p (t m j) -> p m t j", t=PACK, j=PACK)[:, lo:hi],
                in_=raw[:].rearrange("p j (m t) -> p m t j", t=PACK),
            )

        first_row = P - PASSES * SCALE_ROWS
        tab_sc = shared([P, T], U8, "tab_sc")
        nc.vector.memset(tab_sc[:first_row, :].bitcast(I32), 0)
        nc.sync.dma_start(out=tab_sc[first_row:, :].bitcast(I32), in_=tab_scales.rearrange("a r c -> (a r) c").bitcast(I32))
        v_sc = shared([P, PASSES * S], U8, "v_sc")
        wm_sc = shared([P, PASSES * H], U8, "wm_sc")
        wg_sc = shared([P, H], U8, "wg_sc")
        for scale_tile in (v_sc, wm_sc, wg_sc):
            nc.vector.memset(scale_tile[:].bitcast(I32), 0)
        ident = keep.tile([P, P], F32)
        make_identity(nc, ident[:])

        list1 = keep.tile([P, S // GROUP], U16)
        list2 = keep.tile([P, S // GROUP], U16)
        list3 = keep.tile([P, S // GROUP], U16)
        nc.sync.dma_start(list1[:], offs)
        planes = {(0, 0): load_plane(0, 0)}
        nc.sync.dma_start(list2[:], offs2)
        nc.sync.dma_start(list3[:], offs3)
        picked_sc = shared([P, S], U8, "picked_sc")
        nc.vector.tensor_copy(out=picked_sc[:], in_=tab_sc[:].indirect(list1[:]))

        def place_scales(q):
            for a in range(PASSES):
                row = first_row + SCALE_ROWS * a + 4 * q
                nc.sync.dma_start(
                    out=v_sc[32 * q : 32 * q + 4, a * S : (a + 1) * S].bitcast(I32), in_=picked_sc[row : row + 4, :].bitcast(I32)
                )
            nc.sync.dma_start(
                out=wm_sc[32 * q : 32 * q + 4, :].bitcast(I32).rearrange("r (a c) -> r a c", a=PASSES),
                in_=wm_scales[:, 4 * q : 4 * q + 4, :].bitcast(I32).rearrange("a r c -> r a c"),
            )

        x0_bf = [shared([P, PACK * CHUNK], BF16, "x0_bf%d" % c) for c in range(CHUNKS)]
        x0_turned = [shared([P, 2, 2, P, 2], BF16, "x0_turned%d" % c) for c in range(CHUNKS)]
        sum_banks = {}

        def gather_pass0(t):
            u, e = divmod(t, 2)
            for probe, offsets in enumerate((list2, list3)):
                pick = shared([P, S], F32, "pick0_%d%d" % (t, probe), "pick%d%d" % (e, probe))
                nc.vector.tensor_copy(out=pick[:], in_=planes[0, t][:].indirect(offsets[:]))
                for c in range(CHUNKS):
                    if (e, probe) == (0, 0):
                        sum_banks[c] = psum.tile([P, 2, 2, P], F32, name="sum_bank", tag=("h0", "g0", "h1", "g1")[c])
                    for b in range(2):
                        blk = 2 * c + b
                        nc.tensor.matmul(
                            out=sum_banks[c][:, b, e, :],
                            lhsT=pick[:, blk * BLOCK : (blk + 1) * BLOCK],
                            rhs=ident[:],
                            is_transpose=True,
                            start=(e, probe, b) == (0, 0, 0),
                            stop=(e, probe, b) == (1, 1, 1),
                        )
                    if (e, probe) == (1, 1):
                        nc.scalar.copy(out=x0_turned[c][:, :, u], in_=sum_banks[c][:].rearrange("j b e p -> j b p e"))

        first, x1, a_row, b_row, diff, h_bf, gate, term, z_bf, z_q, x_q, z_banks, x1_bf, b_room = ({} for name in range(14))

        def first_picks(c, ts):
            for t in ts:
                nc.vector.tensor_copy(out=first[c, t], in_=planes[1, t][:].indirect(entries(list2, c * CHUNK, CHUNK)))

        def second_picks(c, ts):
            for t in ts:
                nc.vector.tensor_tensor(
                    out=x1[c][:, t, :],
                    in0=planes[1, t][:].indirect(entries(list3, c * CHUNK, CHUNK)),
                    in1=first[c, t],
                    op=ADD,
                )

        def gather_words(a):
            nc.vector.tensor_copy(out=v_codes[:, a, :], in_=load_words(a)[:].indirect(list1[:]))

        def project_table(c):
            for b in range(2):
                blk = 2 * c + b
                bank = psum.tile([P, H], F32, name="a_bank", tag="gobh"[c] + str(b))
                for a in range(PASSES):
                    nc.tensor.matmul_mx(
                        out=bank[:],
                        lhsT=v_codes[:, a, blk * BLOCK : (blk + 1) * BLOCK].bitcast(FP8X4),
                        lhsT_scale=v_sc[:, a * S + blk * BLOCK : a * S + (blk + 1) * BLOCK],
                        rhs=wm[:, a, :].bitcast(FP4X4),
                        rhs_scale=wm_sc[:, a * H : (a + 1) * H],
                        start=(a == 0),
                        stop=(a == PASSES - 1),
                    )
                nc.scalar.copy(out=block_of(a_row[c], b), in_=natural(bank))

        def slot(c, dtype, name):
            shape = [P, PACK * CHUNK if dtype == BF16 else PASSES * CHUNK]
            if c % 2:
                return shared(shape, dtype, name, "x0_bf2" if c == LAST else "x0_turned1")
            return placed.tile(shape, dtype, name=name, align_bytes=64, offset=4 * PASSES * H)

        def round_probes(c):
            if c == LAST:
                x1_bf[c] = [b_row[1][:, lo : lo + CHUNK].bitcast(BF16) for lo in (0, ROW - CHUNK)]
            elif c == 2:
                x1_bf[c] = [late_room[:, :H].bitcast(BF16)]
            else:
                x1_bf[c] = [slot(c + 1, BF16, "x1_bf%d" % c)[:]]
            width = CHUNK // len(x1_bf[c])
            for i, piece in enumerate(x1_bf[c]):
                interleave(piece, x1[c][:, :, i * width : (i + 1) * width])

        def quantize_pass0(c):
            scales = two.tile([P, PASSES * CHUNK], U8, name="x_scales", align_bytes=64)
            codes = slot(c, U32, "x_codes%d" % c)
            x_q[c] = codes, scales
            quantize(codes[:, :CHUNK], scales[:, :CHUNK], x0_bf[c][:])

        def quantize_pass1(c):
            codes, scales = x_q[c]
            width = CHUNK // len(x1_bf[c])
            for i, piece in enumerate(x1_bf[c]):
                cols = slice(CHUNK + i * width, CHUNK + (i + 1) * width)
                quantize(codes[:, cols], scales[:, cols], piece)

        def project_probes(c):
            codes, scales = x_q[c]
            b_room[c] = None if c == LAST else two.tile([P, CHUNK + ROW], F32, name="b_row", align_bytes=64)
            b_row[c] = {} if c == LAST else b_room[c][:, CHUNK:]
            for b in range(2):
                cols = [slice(a * CHUNK + b * BLOCK, a * CHUNK + (b + 1) * BLOCK) for a in range(PASSES)]
                if c == LAST:
                    passes = [
                        (wp_codes[:, a * H : (a + 1) * H], wp_scales[:, a * H : (a + 1) * H], codes[:, cols[a]], scales[:, cols[a]])
                        for a in range(PASSES)
                    ]
                    b_row[c][b] = channel_product("h%d" % b, passes)
                    continue
                bank = psum.tile([P, H], F32, name="b_bank", tag="b%d" % b)
                for a in range(PASSES):
                    nc.tensor.matmul_mx(
                        out=bank[:],
                        lhsT=codes[:, cols[a]].bitcast(FP8X4),
                        lhsT_scale=scales[:, cols[a]],
                        rhs=wp_codes[:, a * H : (a + 1) * H].bitcast(FP8X4),
                        rhs_scale=wp_scales[:, a * H : (a + 1) * H],
                        start=(a == 0),
                        stop=(a == PASSES - 1),
                    )
                nc.scalar.copy(out=block_of(b_row[c], b), in_=dealt(bank))

        def channel_product(tag, passes):
            bank = psum.tile([P, PACK, BLOCK], F32, name="channel_bank", tag=tag)
            for t in range(PACK):
                for i, (weight, weight_scales, tokens, token_scales) in enumerate(passes):
                    nc.tensor.matmul_mx(
                        out=bank[:, t, :],
                        lhsT=weight[:, t * P : (t + 1) * P].bitcast(FP8X4),
                        lhsT_scale=weight_scales[:, t * P : (t + 1) * P],
                        rhs=tokens.bitcast(FP8X4),
                        rhs_scale=token_scales,
                        start=(i == 0),
                        stop=(i == len(passes) - 1),
                    )
            return bank[:].rearrange("p t j -> p j t")

        def turn(bank, row, b, opens, closes):
            for t in range(PACK):
                nc.tensor.matmul(
                    out=bank[:, t, :],
                    lhsT=block_of(row, b)[:, t // 2, t % 2, :],
                    rhs=ident[:],
                    is_transpose=True,
                    start=(opens and t == 0),
                    stop=(closes and t == PACK - 1),
                )

        def transposed_sum(tag, rows, b):
            bank = psum.tile([P, PACK, BLOCK], F32, name="sum_bank", tag=tag)
            for order, row in enumerate(rows):
                turn(bank, row, b, order == 0, order == len(rows) - 1)
            return bank[:].rearrange("p t j -> p j t")

        def elementwise(engine, dst, left, right, op, pieces):
            width = ROW // pieces
            for lo in range(0, ROW, width):
                engine.tensor_tensor(out=dst[:, lo : lo + width], in0=left[:, lo : lo + width], in1=right[:, lo : lo + width], op=op)

        def difference(c):
            diff[c] = shared([P, ROW], F32, "diff%d" % c, ("x0_bf1", "first_last")[c])[:] if c < 2 else b_room[1][:, :ROW]
            elementwise(nc.gpsimd if c < 2 else nc.vector, diff[c], a_row[c], b_row[c], SUB, 1)

        def sum_h(c):
            for b in range(2):
                nc.scalar.copy(out=by_token(h_bf[c][:, b * H : (b + 1) * H]), in_=transposed_sum("h%d" % b, (a_row[c], b_row[c]), b))

        def quantize_pair(name, c, src):
            codes = shared([P, CHUNK], U32, "%s_codes%d" % (name, c), "%s_codes%d" % (name, c % 2))
            scales = two.tile([P, CHUNK], U8, name=name + "_scales", align_bytes=64)
            width = BLOCK if c == LAST else CHUNK
            for lo in range(0, CHUNK, width):
                quantize(codes[:, lo : lo + width], scales[:, lo : lo + width], src[:, PACK * lo : PACK * (lo + width)])
            return codes, scales

        def deal(dst, src):
            nc.gpsimd.tensor_copy(out=dst[:].rearrange("p (t m) -> p m t", t=PACK), in_=src[:].rearrange("p (m t) -> p m t", t=PACK))
            return dst

        def quantize_h(c):
            return quantize_pair("h", c, h_bf[c])

        def make_gate(c, codes, scales):
            gate[c] = two.tile([P, ROW], F32, name="gate")[:]
            for b in range(2):
                cols = slice(b * BLOCK, (b + 1) * BLOCK)
                if c == LAST:
                    bank = channel_product("g%d" % b, [(wg_dealt, wg_sc_dealt, codes[:, cols], scales[:, cols])])
                    nc.scalar.activation(out=by_token(gate[c][:, b * H : (b + 1) * H]), in_=bank, func=SIGMOID, scale=-1.0)
                    continue
                bank = psum.tile([P, H], F32, name="gate_bank", tag="g%d" % b)
                nc.tensor.matmul_mx(
                    out=bank[:],
                    lhsT=codes[:, cols].bitcast(FP8X4),
                    lhsT_scale=scales[:, cols],
                    rhs=wg[:].bitcast(FP8X4),
                    rhs_scale=wg_sc[:],
                    start=True,
                    stop=True,
                )
                nc.scalar.activation(out=block_of(gate[c], b), in_=natural(bank), func=SIGMOID)

        def interpolate(c, pieces):
            term[c] = spacers[:, :ROW] if c == 0 else two.tile([P, ROW], F32, name="term")[:]
            elementwise(nc.vector, term[c], gate[c], diff[c], MULT, pieces)

        def open_z(c):
            z_banks[c] = [psum.tile([P, PACK, BLOCK], F32, name="z_bank", tag="obo"[c] + str(b)) for b in range(2)]
            for b in range(2):
                turn(z_banks[c][b], b_row[c], b, True, False)

        def sum_z(c):
            z_bf[c] = shared([P, 2 * H], BF16, "z_bf%d" % c)
            for b in range(2):
                turn(z_banks[c][b], term[c], b, False, True)
                nc.scalar.copy(out=by_token(z_bf[c][:, b * H : (b + 1) * H]), in_=z_banks[c][b][:].rearrange("p t j -> p j t"))

        def quantize_z(c):
            z_q[c] = quantize_pair("z", c, z_bf[c])

        stage_tags = ("plane02", "plane03", "plane10", "plane11", "plane12", "plane13", "wp1_raw", "wo_raw")

        def finish(c):
            codes, scales = z_q[c]
            for b in range(2):
                blk = 2 * c + b
                cols = slice(b * BLOCK, (b + 1) * BLOCK)
                bank = psum.tile([P, N // P, BLOCK], F32, name="out_bank", tag="ggoh"[c] + str(b))
                for n in range(N // P):
                    nc.tensor.matmul_mx(
                        out=bank[:, n, :],
                        lhsT=wo_codes[:, n * P : (n + 1) * P].bitcast(FP8X4),
                        lhsT_scale=wo_scales[:, n * P : (n + 1) * P],
                        rhs=codes[:, cols].bitcast(FP8X4),
                        rhs_scale=scales[:, cols],
                        start=True,
                        stop=True,
                    )
                staged = shared([P, N // P, BLOCK], F32, "staged%d" % blk, stage_tags[blk])
                copy = nc.vector.tensor_copy if blk == 2 * LAST + 1 else nc.scalar.copy
                copy(out=staged[:], in_=bank[:])
                nc.sync.dma_start(
                    out=out.rearrange("(n p) j -> p n j", p=P)[:, :, blk * BLOCK : (blk + 1) * BLOCK], in_=staged[:]
                )

        wp_bf = shared([P, PASSES * PACK * H], BF16, "wp_bf")
        gather_pass0(0)
        planes[0, 1] = load_plane(0, 1)
        gather_pass0(1)
        round_wp(0, 0, P // 2, "wp0_raw")
        v_codes = shared([P, PASSES, S], U32, "v_codes", "wp0_raw")
        for a in range(PASSES):
            gather_words(a)
            place_scales(2 * a)
            place_scales(2 * a + 1)
        planes[0, 2] = load_plane(0, 2)
        round_wp(0, P // 2, P, None)
        wm = keep.tile([P, PASSES, 2 * H], U8, align_bytes=64)
        nc.sync.dma_start(out=wm[:].bitcast(I32), in_=wm_words.bitcast(I32).rearrange("a p c -> p a c"))
        rows = [shared([P, 2 * ROW], F32, "rows%d" % c, ("plane00", "plane01", "tab0", "tab1")[c]) for c in range(CHUNKS)]
        a_row.update({c: rows[c][:, :ROW] for c in range(CHUNKS)})
        project_table(LAST)
        a_last = shared([P, 2, BLOCK, PACK], F32, "a_last")
        for b in range(2):
            nc.scalar.copy(out=a_last[:, b], in_=transposed_sum("o%d" % b, (a_row[LAST],), b))
        for c in range(LAST):
            project_table(c)
        gather_pass0(2)
        planes[0, 3] = load_plane(0, 3)
        for q in range(QUADRANTS):
            nc.sync.dma_start(
                out=wg_sc[32 * q : 32 * q + 4, :].bitcast(I32),
                in_=wg_scales[0, 4 * q : 4 * q + 4, :].bitcast(I32),
            )
        wg = keep.tile([P, H], U32, align_bytes=64)
        nc.sync.dma_start(out=wg[:].bitcast(I32), in_=wg_words[0].rearrange("p c t -> p (c t)").bitcast(I32))
        wg_sc_dealt = deal(shared([P, H], U8, "wg_sc_dealt"), wg_sc)
        wg_dealt = deal(shared([P, H], U32, "wg_dealt"), wg)
        gather_pass0(3)
        round_wp(1, 0, P, "wp1_raw")

        def turn_back(c):
            bank = psum.tile([P, 2, 2, BLOCK], F32, name="back_bank", tag="b%d" % (c % 2))
            for b in range(2):
                for u in range(2):
                    pairs = x0_turned[c][:, b, u].rearrange("j p e -> j (p e)").bitcast(F32)
                    nc.tensor.transpose(out=bank[:, b, u, :], in_=pairs, identity=ident[:])
            words = x0_bf[c][:].bitcast(F32)
            nc.scalar.copy(out=words.rearrange("p (b j u) -> p b j u", b=2, u=2), in_=bank[:].rearrange("p b u j -> p b j u"))

        turn_back(0)
        turn_back(1)
        for t in range(PACK):
            planes[1, t] = load_plane(1, t)
        wo_raw = load_weight("wo_raw", wo)

        work = shared([P, ROW], F32, "work")
        spacers = shared([P, 5 * CHUNK + BLOCK], F32, "first1", "pick00")
        first_last = shared([P, CHUNK], F32, "first_last")
        sums = shared([P, ROW + 3 * CHUNK], F32, "sums", "pick01")
        for c, row in enumerate((sums[:, BLOCK : BLOCK + ROW], sums[:, :ROW], sums[:, :ROW])):
            x1[c] = row.rearrange("p (t j) -> p t j", t=PACK)
        for t in range(PACK):
            lo = (0, CHUNK + BLOCK, 0, 3 * CHUNK + BLOCK)[t]
            spacer = first_last[:] if t == 2 else spacers[:, lo : lo + CHUNK]
            first.update({(0, t): work[:, t * CHUNK : (t + 1) * CHUNK], (1, t): spacer, (2, t): spacer})
            first[LAST, t] = spacers[:, (t + 1) * CHUNK : (t + 2) * CHUNK]
        h_bf[2] = work[:, :H].bitcast(BF16)
        first[0, 3] = placed.tile([P, CHUNK], F32, name="first03", align_bytes=64, offset=4 * (PASSES * H - BLOCK))[:]
        h_bf[0] = sums[:, 3 * BLOCK : 3 * BLOCK + H].bitcast(BF16)
        for t in range(PACK):
            first_picks(0, (t,))
            first_picks(1, (t,))
            second_picks(0, (t,))
        round_probes(0)
        turn_back(2)
        turn_back(3)
        wp_codes = placed.tile([P, PASSES * H], U32, name="wp_codes", align_bytes=64, offset=0)
        wp_scales = shared([P, PASSES * H], U8, "wp_scales")
        quantize(wp_codes[:], wp_scales[:], wp_bf[:])
        quantize_pass0(0)
        quantize_pass1(0)
        project_probes(0)
        second_picks(1, range(PACK))
        wo_bf = sums[:, ROW:].bitcast(BF16)
        interleave(wo_bf, wo_raw[:])
        wo_codes = shared([P, N], U32, "wo_codes")
        wo_scales = shared([P, N], U8, "wo_scales")
        for cols in (slice(0, 2 * P), slice(2 * P, N)):
            quantize(wo_codes[:, cols], wo_scales[:, cols], wo_bf[:, PACK * cols.start : PACK * cols.stop])
        quantize_pass0(1)
        first_picks(2, range(PACK))
        round_probes(1)
        sum_h(0)
        difference(0)
        quantize_pass1(1)
        project_probes(1)
        second_picks(2, (0,))
        quantize_pass0(2)
        codes = quantize_h(0)
        quantize_pass0(LAST)
        late_room = shared([P, ROW + CHUNK], F32, "late_room", "x0_turned1")
        h_bf[1] = late_room[:, 5 * BLOCK : 5 * BLOCK + H].bitcast(BF16)
        x1[LAST] = late_room[:, CHUNK:].rearrange("p (t j) -> p t j", t=PACK)
        second_picks(2, (1, 2, 3))
        first_picks(LAST, range(PACK))
        make_gate(0, *codes)
        open_z(0)
        sum_h(1)
        round_probes(2)
        difference(1)
        quantize_pass1(2)
        codes = quantize_h(1)
        project_probes(2)
        make_gate(1, *codes)
        second_picks(LAST, range(PACK))
        interpolate(0, 1)
        sum_h(2)
        open_z(1)
        round_probes(LAST)
        sum_z(0)
        interpolate(1, 1)
        codes = quantize_h(2)
        quantize_pass1(LAST)
        make_gate(2, *codes)
        project_probes(LAST)
        difference(2)
        quantize_z(0)
        sum_z(1)
        finish(0)
        interpolate(2, 1)
        open_z(2)
        sum_z(2)
        tail = shared([P, ROW + H], F32, "tail", "work")
        h_bf[LAST] = tail[:, ROW:].bitcast(BF16)
        for b in range(2):
            nc.vector.tensor_tensor(out=by_token(h_bf[LAST][:, b * H : (b + 1) * H]), in0=b_row[LAST][b], in1=a_last[:, b], op=ADD)
        make_gate(LAST, *quantize_h(LAST))
        quantize_z(1)
        diff[LAST] = tail[:, :ROW]
        for b in range(2):
            nc.vector.tensor_tensor(out=by_token(diff[LAST][:, b * H : (b + 1) * H]), in0=b_row[LAST][b], in1=a_last[:, b], op=SUB)
        quantize_z(2)
        interpolate(LAST, 2)
        finish(1)
        finish(2)
        z_bf[LAST] = shared([P, 2 * H], BF16, "z_bf3", "pick10")
        for b in range(2):
            nc.vector.tensor_tensor(
                out=by_token(z_bf[LAST][:, b * H : (b + 1) * H]), in0=by_token(term[LAST][:, b * H : (b + 1) * H]), in1=a_last[:, b], op=ADD
            )
        quantize_z(LAST)
        finish(LAST)
